import numpy as np, ml_dtypes
CORES = [5,29,101,125,133,157,229,253]
N = 8
BF = ml_dtypes.bfloat16
def gentries(a):
    return np.ascontiguousarray(a.reshape(8, 16, -1).transpose(0, 2, 1)).reshape(8, -1)
def gtable(e):
    e = np.asarray(e); return np.ascontiguousarray(e.reshape(8, -1, 16).transpose(0, 2, 1)).reshape(128, -1).astype(np.int32)
P, L, S, F, RO = 2048, 2048, 6, 256, 2
H = P - F
def depths(rng, up, top):
    s = np.where(rng.random((N, 8, P)) < up, 1, 1 - rng.geometric(0.5, (N, 8, P))); d = np.zeros((N, 8, P), np.int64); now = np.zeros((N, 8), np.int64)
    for v in range(1, P):
        now = np.minimum(np.maximum(now + s[:, :, v], 0), top); d[:, :, v] = now
    return d
def closed(d):
    e = np.zeros(d.shape, np.int64); last = np.full(d.shape[:-1] + (1,), P, np.int64)
    for k in range(int(np.max(d)) + 1):
        m = np.minimum.accumulate(np.where(d <= k, np.arange(P), P)[..., ::-1], axis=-1)[..., ::-1]
        e = np.where(d == k, np.concatenate([m[..., 1:], last], axis=-1), e)
    return e
def parts(rng):
    up = rng.choice(np.array([0.4, 0.5, 0.6]), (N, 8, 1)); top = rng.integers(3, 13, (N, 8))
    full = np.arange(P) < (P * rng.choice(np.array([8, 12, 14, 16]), (N, 8, 1))) // 16
    d = np.where(full, depths(rng, up, top), 0)
    x = np.where(rng.random((N, 8, 16, P)) < 0.25, rng.integers(0, 4, (N, 8, 16, P)), rng.integers(0, 256, (N, 8, 16, P))) * full[:, :, None, :]
    return x, d, rng.integers(0, 256, (N, 8, 16, L)), rng.integers(0, P, (N, 8, RO, L))
def pack(x, e, w, st):
    return {"x": np.ascontiguousarray(x.reshape(N, 128, P)).astype(np.float32).astype(BF), "w": np.ascontiguousarray(w.reshape(N, 128, L)).astype(np.float32).astype(BF),
            "ends": np.ascontiguousarray(e).astype(np.int32), "start": np.stack([gtable(a.reshape(8, -1)) for a in st])}
def setup_inputs(rng):
    x, d, w, st = parts(rng)
    return pack(x, closed(d), w, st)
def setup_inputs_room(rng):
    x, d, w, st = parts(rng); x = rng.integers(0, 256, x.shape); Q = P // 16; z = F // 4
    at = ((H - z, H), (H - z + 1, H + 1), (H, H + z), (H - 1, H - 1 + z), (P - z, P), (P - z + 1, P + 1), (P - 1, P - 1 + z), (H - z, -1))
    for q in range(N):
        for g in range(8):
            n = int(rng.integers(Q // 2, Q + 1)); a, b = at[(g + q) % 8]; a = a - n; b = P if b < 0 else b - n; D = d[q, g].copy()
            d[q, g] = np.concatenate([np.tile(np.arange(3), Q), D[:a - 3 * Q], np.zeros(1, np.int64), 1 + D[:b - a - 1], D[:P - b]])
            hot = 3 * rng.permutation(Q)[:n]
            st[q, g, 0] = rng.permutation(np.concatenate([hot, rng.choice(hot, L - n)]))
    return pack(x, closed(d), w, st)
def setup_inputs_ties(rng):
    x, d, w, st = parts(rng); lo = rng.choice(np.array([0, 100, 252]), (N, 8, 1, 1))
    x = lo + rng.integers(0, 4, x.shape); x[:, 1::2] = (lo + 2 * rng.integers(0, 2, (N, 8, 1, P)))[:, 1::2]
    return pack(x, closed(d), np.minimum(lo + rng.integers(0, 5, w.shape), 255), st)
def setup_inputs_alike(rng):
    x, d, w, st = parts(rng); x = rng.integers(0, 256, x.shape); e = closed(d); at = np.arange(P)
    names = rng.integers(0, P, (N, 8, RO, 6)); names[..., 0] = 0; names[..., 1] = P - 1
    st = np.take_along_axis(names, rng.integers(0, 6, st.shape), 3)
    for q in range(N):
        g = (np.arange(4) + q) % 8
        e[q, g[0]] = P; st[q, g[0], 0] = rng.choice(np.array([0, P - 1, P - 2, P - 3, P - 1 - S, P - 2 - S]), L)
        e[q, g[1]] = at + 1; e[q, g[1], :2] = P; st[q, g[1], 0] = 0
        e[q, g[2]] = at + 1
        e[q, g[3]] = np.where(at % 2 == 0, P, at + 1); st[q, g[3], 0] = rng.integers(0, P, L)
    return pack(x, e, w, st)
def setup_inputs_far(rng):
    x, d, w, st = parts(rng); x = rng.integers(0, 256, x.shape); w = rng.integers(1, 256, w.shape); g = rng.permutation(8); odd = np.arange(N) % 2 == 1; i4 = np.arange(16)[:, None] % 4
    kid = np.where(odd, rng.integers(3 * P // 4 + 2, P - 1, N), P - 1); low = np.where(odd, rng.integers(3 * P // 4, H, N), P - 1)
    left = np.where(odd, rng.integers(15 * P // 32, P // 2 - 4, N), rng.integers(7 * P // 16 + 1, 15 * P // 32, N)); T = min(P // 7, L // 4)
    st[:, g[:4]] = P - 1
    for q in range(N):
        D = d[q].copy(); b = int(kid[q]); z = int(low[q]); s = int(left[q]); m = D[g[0]]
        d[q, g[0]] = np.concatenate([np.array([0, 1, 2, 3]), 3 + m[:b - 4], np.array([2]), m[:P - b - 1]])
        x[q, g[0], :, b] = 0; st[q, g[0], 0] = 0
        d[q, g[1]] = np.concatenate([np.zeros(z + 1, np.int64), D[g[1]][:P - z - 1]])
        v = rng.choice(np.array([0, z - 2]), L); v[0] = 0; v[1] = z - 2; st[q, g[1], 0] = v
        m = D[g[2]]; d[q, g[2]] = np.concatenate([np.arange(3), 2 + m[:s - 1], m[:P - s - 2]]); st[q, g[2], 0] = 0
        m = D[g[3]]; a = H - 4 + q % 2
        d[q, g[3]] = np.concatenate([m[:H - 4], np.array([0, 0, 1, 2, 3]) if q % 2 else np.array([0, 1, 2, 3, 3]), m[:P - H - 1]])
        v = np.where(rng.random(L) < 0.5, a, rng.integers(H, P, L)); v[0] = a; st[q, g[3], 1] = v
        d[q, g[4]] = np.concatenate([np.tile(np.array([0, 1, 2, 2, 1, 2, 2]), T), D[g[4]][:P - 7 * T]])
        few = np.array([4, 0, 2, 3, 1, 2, 3])[np.arange(P) % 7]
        x[q, g[4]] = np.where(i4 == few, rng.integers(0, 61, (16, P)), rng.integers(200, 256, (16, P)))
        j = rng.permutation(np.concatenate([np.arange(4 * T), rng.integers(0, 4 * T, L - 4 * T)])); st[q, g[4], 0] = 7 * (j // 4)
        w[q, g[4]] = np.where((i4 == (j % 4) // 2) | (i4 == 2 + j % 2), rng.integers(100, 201, (16, L)), 0)
    x[:, g[0], :, 2] = 255; x[:, g[0], :, 3] = 0; x[:, g[0], :, 4] = 255; x[:, g[3], :, H - 1] = 255; x[:, g[3], :, H] = 0
    for k in (1, 2):
        x[:, g[k], :, 2] = 0; x[:, g[k], :, 3] = 255
    e = closed(d)
    for q in range(N):
        z = int(low[q]); e[q, g[1], :z + 1] = z + 1; e[q, g[1], 2] = 3
    return pack(x, e, w, st)
def setup_inputs_spread(rng):
    x, d, w, st = parts(rng)
    d = depths(rng, 0.35 + 0.35 * rng.random((N, 8, 1)), np.exp2(1 + 5 * rng.random((N, 8))).astype(np.int64) + 1)
    x = np.minimum((np.exp2(8 * rng.random((N, 8, 1, P))) * rng.random((N, 8, 16, P))).astype(np.int64), 255)
    w = np.minimum((np.exp2(8 * rng.random((N, 8, 1, L))) * rng.random((N, 8, 16, L))).astype(np.int64), 255)
    st = np.minimum((P * rng.random((N, 8, RO, L)) ** rng.choice(np.array([1, 2, 4]), (N, 8, 1, 1))).astype(np.int64), P - 1)
    return pack(x, closed(d), w, st)
def check_inputs(d):
    bad = []
    for k in ("x", "w"):
        v = d[k].astype(np.float32)
        if not np.all((v >= 0) & (v <= 255) & (v == np.floor(v))): bad.append("whole numbers from 0 to 255 in " + k)
    e = d["ends"].astype(np.int64); n = e - np.arange(P)
    if np.min(n) < 1 or np.max(e) > P: bad.append("range of ends")
    else:
        big = e; most = np.zeros(e.shape, np.int64); k = 1
        while k <= P:
            sel = (n >= k) & (n < 2 * k)
            most = np.where(sel, np.maximum(big, np.take_along_axis(big, np.where(sel, e - k, 0), 2)), most)
            big = np.concatenate([np.maximum(big[..., :P - k], big[..., k:]), big[..., P - k:]], axis=2); k = 2 * k
        if np.any(most > e): bad.append("runs that cross")
    if np.min(d["start"]) < 0 or np.max(d["start"]) > P - 1: bad.append("range of start")
    return bad
def grow(x, e, w, v):
    G = np.arange(8)[:, None]; at = np.arange(P); n = np.zeros((8, L), np.int64); par = v
    for i in range(S):
        ev = e[G, v]; a = np.minimum(v + 1, P - 1); b = e[G, a]; kids = ev > v + 1; two = kids & (b < ev); b = np.minimum(b, P - 1)
        ra = np.add.reduce(np.maximum(w - x[G, a], 0), axis=2); rb = np.add.reduce(np.maximum(w - x[G, b], 0), axis=2)
        par = np.where(kids, v, par); n = n + kids; v = np.where(kids, np.where(two & (rb > ra), b, a), v)
    hit = (n >= 2) & (e[G, v] == v + 1); gi = np.broadcast_to(G, v.shape)[hit]
    head = np.zeros((8, P), bool); head[gi, v[hit]] = True; mark = np.zeros((8, P), bool); mark[gi, par[hit]] = True
    zero = np.zeros((8, 1), np.int64); reach = np.maximum.accumulate(np.where(mark, e, 0), axis=1)
    top = mark & (np.concatenate([zero, reach[:, :-1]], axis=1) <= at); inside = reach > at; keep = ~head
    first = np.maximum.accumulate(np.where(top, at, 0), axis=1)
    K = np.concatenate([zero, np.add.accumulate(keep.astype(np.int64), axis=1)], axis=1)
    M = np.concatenate([zero, np.add.accumulate(keep * (1 + 2 * inside), axis=1)], axis=1)
    size = np.where(inside, K[G, e] - K[:, :P], M[G, e] - M[:, :P]); s = K[G, e[G, first]] - K[G, first]
    nx = np.zeros((8, P, 16), np.int64); ne = np.zeros((8, P), np.int64) + at + 1
    for c in range(3):
        q = np.where(inside, M[G, first] + c * s + K[:, :P] - K[G, first], M[:, :P])
        gk, vk = np.nonzero(keep & (inside | (c == 0)) & (q < P)); qk = q[gk, vk]
        nx[gk, qk] = np.maximum(x[gk, vk] - c, 0); ne[gk, qk] = qk + size[gk, vk]
    return nx, ne
def reference(x, w, ends, start):
    X = np.ascontiguousarray(x.astype(np.float32).astype(np.int64).reshape(N, 8, 16, P).transpose(0, 1, 3, 2)); E = ends.astype(np.int64)
    W = np.ascontiguousarray(w.astype(np.float32).astype(np.int64).reshape(N, 8, 16, L).transpose(0, 1, 3, 2))
    st = np.stack([gentries(a) for a in start]).astype(np.int64).reshape(N, 8, RO, L)
    for t in range(RO):
        both = [grow(X[r], E[r], W[r], st[r, :, t]) for r in range(N)]
        gx = np.stack([a for a, b in both]); ge = np.stack([b for a, b in both])
        X = np.concatenate([gx[:, :, :H], np.roll(gx[:, :, H:], 1, axis=0)], axis=2)
        E = np.concatenate([np.minimum(ge[:, :, :H], H), np.roll(np.minimum(ge[:, :, H:], P), 1, axis=0)], axis=2)
    return {"y": np.ascontiguousarray(X.transpose(0, 1, 3, 2)).reshape(N, 128, P).astype(np.float32).astype(BF), "ye": E.astype(np.float32)}

@@ -1,0 +1,584 @@
+from concourse.mybir import dt, AluOpType, AxisListType, ActivationFunctionType
+
+A = AluOpType
+AF = ActivationFunctionType
+P = 2048
+SC = 12
+VC = 64 - SC
+NVR = 40
+XW = 2064
+CUT = 1792
+SWW = 8192
+
+BLK = ["VF", "V1", "Q2", "ZERO", "two", "nhE", "hv", "KX", "HS", "HI", "mE", "ks", "kx", "K2", "FM", "Fs", "ex", "nex", "eq", "en",
+       "PF", "NB", "NN", "PN", "SP", "cc", "s", "L3", "tA", "tC", "tD", "EN", "HIw", "LOw", "NLO", "VAL", "nv", "hiF", "qq", "csb",
+       "ID", "TRI", "SHIFT", "SHR", "SHL", "RST", "MK0", "ONEF", "rowA", "rowB", "rowC", "rowD", "rowN", "rowT"]
+SCRATCH = {"BK": ("sbuf", [128, 128 * len(BLK)], "float32")}
+for n_ in ("E0", "E1", "E2", "hm", "RCH", "RC2", "CSs"):
+    SCRATCH[n_] = ("sbuf", [128, 132], "float32")
+for n_ in ("VI", "vint", "hii", "loi"):
+    SCRATCH[n_] = ("sbuf", [128, 128], "int32")
+for n_ in ("B16", "EL16", "off16", "q16", "L316", "LS16", "Z16", "SBE", "RLE0", "RLE1", "LE0", "LE1"):
+    SCRATCH[n_] = ("sbuf", [128, 128], "uint16")
+for n_ in ("IH", "IDB", "NIDB", "hmb", "kb", "kl", "bb", "bl", "sb", "sl", "nb", "nl"):
+    SCRATCH[n_] = ("sbuf", [128, 128], "bfloat16")
+for n_ in ("F1", "FP", "FN", "FA", "FB", "ONEB", "LOI"):
+    SCRATCH[n_] = ("sbuf", [128, 144], "bfloat16")
+for n_ in ("XPHI", "GR", "GK", "W", "KT", "ST", "HMR", "VD", "Y2", "R0", "R1"):
+    SCRATCH[n_] = ("sbuf", [128, 2048], "bfloat16")
+SCRATCH.update({
+    "X0": ("sbuf", [128, 3 * XW], "bfloat16"), "X1": ("sbuf", [128, 3 * XW], "bfloat16"),
+    "XBS": ("sbuf", [128, XW], "bfloat16"), "MB": ("sbuf", [128, XW], "bfloat16"),
+    "SW": ("sbuf", [128, SWW], "bfloat16"),
+    "LH": ("sbuf", [128, 128 * 128], "bfloat16"), "RH": ("sbuf", [128, 128 * 130], "bfloat16"),
+    "ST0": ("sbuf", [128, 256], "int32"), "EI": ("sbuf", [128, 128], "int32"),
+    "cols": ("sbuf", [128, 32], "float32"), "coli": ("sbuf", [128, 8], "int32"),
+    "SBX": ("sbuf", [128, 256], "bfloat16"), "RLX0": ("sbuf", [128, 256], "bfloat16"), "RLX1": ("sbuf", [128, 256], "bfloat16"),
+})
+for n_ in (0, 1):
+    SCRATCH["MR%d" % n_] = ("sbuf", [128, 1024], "bfloat16")
+    SCRATCH["WD%d" % n_] = ("sbuf", [128, 32 * SC], "bfloat16")
+    SCRATCH["GS%d" % n_] = ("sbuf", [128, 32 * SC], "bfloat16")
+    SCRATCH["ZF%d" % n_] = ("sbuf", [128, 128], "float32")
+for n_ in range(8):
+    SCRATCH["p%d" % n_] = ("psum", [128, 512], "float32")
+SEMAPHORES = ["q_v", "q_s", "q_t", "q_g"] + ["d%d" % k for k in range(40)] + \
+    [a + b for a in ("rx", "rn", "lx", "le", "ax", "ae") for b in "01"]
+NX, NE = 8, 4
+
+
+def pick(topo, src, dst, k, skip=0):
+    return sum(1 << e for e in topo.engines(src, dst)[skip:skip + k])
+
+
+def relays(topo, core, dst):
+    return [c for c in topo.cores_of(core) if c != core and topo.die(c) == topo.die(core) and topo.may_write(c, dst)]
+
+
+def relay_program(g, core, T, topo):
+    for r, me in enumerate(T.cores):
+        dst = T.cores[(r + 1) % len(T.cores)]
+        rl = relays(topo, me, dst)
+        if core not in rl[:2]:
+            continue
+        rid, pid = topo.addr(dst, core)
+        if core == rl[0]:
+            for t in range(2):
+                g.wait_ge(T.sem["rx%d" % t], NX)
+                out = T.X1[:, CUT:P] if t == 0 else T.Y2[:, CUT:P]
+                g.remote_dma(out, T["RLX%d" % t][:], T.sem["ax%d" % t], T.sem["lx%d" % t], pid, rid, pick(topo, core, dst, NX))
+            for t in range(2):
+                g.wait_ge(T.sem["lx%d" % t], NX)
+        else:
+            for t in range(2):
+                g.wait_ge(T.sem["rn%d" % t], NE)
+                g.remote_dma(T["LE%d" % t][:], T["RLE%d" % t][:], T.sem["ae%d" % t], T.sem["le%d" % t], pid, rid, pick(topo, core, dst, NE))
+            for t in range(2):
+                g.wait_ge(T.sem["le%d" % t], NE)
+
+
+def rank_program(g, core, T, topo):
+    if T.rank_of(core) is None:
+        return relay_program(g, core, T, topo)
+    rank = T.rank_of(core)
+    dst = T.cores[(rank + 1) % len(T.cores)]
+    rl = relays(topo, core, dst)
+    queues = {"v": g.vector, "s": g.scalar, "t": g.tensor, "g": g, "y": g.sync}
+    count = {}
+    known = {q: {} for q in queues}
+    log = {}
+    nd = [0]
+    where = {n: 128 * k for k, n in enumerate(BLK)}
+
+    def r(name, lo=0, hi=None, step=None, p=None, tag=None):
+        if name in where:
+            hi = 128 if hi is None else hi
+            lo, hi, name = lo + where[name], hi + where[name], "BK"
+        t = T[name]
+        hi = t.shape[1] if hi is None else hi
+        pp = slice(None) if p is None else p
+        return (t[pp, lo:hi] if step is None else t[pp, lo:hi:step], name, lo, hi, tag)
+
+    def rev(name, p=None):
+        o = where[name]
+        return (T.BK[slice(None) if p is None else p, o + 127:(o - 1 if o else None):-1], "BK", o, o + 128, None)
+
+    def ind(name, lo, hi, lname, a, b):
+        return (T[name][:, lo:hi].indirect(T[lname][:, a:b]), name, lo, hi, None, (None, lname, a, b, None))
+
+    def need(q, reads, writes):
+        want = {}
+        for is_w, views in ((False, reads), (True, writes)):
+            for v in views:
+                bank = v[1][0] == "p" and v[1][1:].isdigit()
+                for e in log.get(v[1], ()):
+                    same = e[4] == q
+                    if same and q == "t":
+                        continue
+                    if (same or not bank) and (e[0] >= v[3] or v[2] >= e[1] or (e[2] is not None and v[4] is not None and e[2] != v[4])):
+                        continue
+                    if not is_w and not e[3] and (same or not bank):
+                        continue
+                    old = want.get(e[5])
+                    if old is None or old[0] < e[6]:
+                        want[e[5]] = (e[6], e[7])
+        kn = known[q]
+        for sem in sorted(want, key=lambda k: -len(want[k][1])):
+            val, clock = want[sem]
+            if kn.get(sem, 0) >= val:
+                continue
+            queues[q].wait_ge(T.sem[sem], val)
+            for k2, v2 in clock.items():
+                if kn.get(k2, 0) < v2:
+                    kn[k2] = v2
+            kn[sem] = val
+
+    def note(q, reads, writes, sem, val, clock):
+        for is_w, views in ((False, reads), (True, writes)):
+            for v in views:
+                L = log.setdefault(v[1], [])
+                if is_w:
+                    L[:] = [e for e in L if not (v[2] <= e[0] and e[1] <= v[3] and (v[4] is None or v[4] == e[2]))]
+                else:
+                    L[:] = [e for e in L if not (not e[3] and e[4] == q and q != "dma" and e[0] >= v[2] and e[1] <= v[3])]
+                L.append([v[2], v[3], v[4], is_w, q, sem, val, clock])
+
+    def op(q, reads, writes, calls):
+        reads = list(reads) + [v[5] for v in list(reads) + list(writes) if len(v) > 5]
+        need(q, reads, writes)
+        sem = "q_" + q
+        for call in calls:
+            call().then_inc(T.sem[sem], 1)
+            count[sem] = count.get(sem, 0) + 1
+        clock = dict(known[q])
+        clock[sem] = count[sem]
+        note(q, reads, writes, sem, count[sem], clock)
+
+    def dma(q, out, in_, ext_in=False):
+        sem = "d%d" % nd[0]
+        nd[0] += 1
+        reads, writes = ([] if ext_in else [in_]), ([out])
+        need(q, reads, writes)
+        queues[q].dma_start(out[0], in_[0]).then_inc(T.sem[sem], 16)
+        count[sem] = 16
+        clock = dict(known[q])
+        clock[sem] = 16
+        note("dma", reads, writes, sem, 16, clock)
+
+    def ext(ap, name, lo=0, hi=2048):
+        return (ap, "#" + name, lo, hi, None)
+
+    def rows(name, k, lo, n, src):
+        dma("y", (T[name][k:128:16, lo:lo + n], name, lo, lo + n, "row%d" % k), src)
+
+    V, S, TE = g.vector, g.scalar, g.tensor
+
+    def tt(out, a, b, o):
+        op("v", [a, b], [out], [lambda: V.tensor_tensor(out[0], a[0], b[0], o)])
+
+    def ts(out, a, s1, s2, o0, o1=None):
+        rd = [a] + [s for s in (s1, s2) if isinstance(s, tuple)]
+        x1 = s1[0] if isinstance(s1, tuple) else s1
+        x2 = s2[0] if isinstance(s2, tuple) else s2
+        if o1 is None:
+            op("v", rd, [out], [lambda: V.tensor_scalar(out[0], a[0], x1, None, o0)])
+        else:
+            op("v", rd, [out], [lambda: V.tensor_scalar(out[0], a[0], x1, x2, o0, o1)])
+
+    def tc(out, a):
+        op("v", [a], [out], [lambda: V.tensor_copy(out[0], a[0])])
+
+    def fill(out, val):
+        op("v", [], [out], [lambda: V.memset(out[0], val)])
+
+    def scan(out, d0, d1, o0, o1):
+        op("v", [d0, d1], [out], [lambda: V.tensor_tensor_scan(out[0], d0[0], d1[0], 0.0, o0, o1)])
+
+    def act(out, a, f, bias=0.0):
+        rd = [a] + ([bias] if isinstance(bias, tuple) else [])
+        bb = bias[0] if isinstance(bias, tuple) else bias
+        op("s", rd, [out], [lambda: S.activation(out[0], a[0], f, bias=bb, scale=1.0)])
+
+    def mm(bank, c0, c1, lhs, rhs, p=None):
+        out = r(bank, c0, c1, p=p)
+        op("t", [lhs, rhs], [out], [lambda: TE.matmul(out[0], lhs[0], rhs[0], True, True)])
+
+    def conv(bank, c0, parts):
+        n = parts[0][4]
+        out = r(bank, c0, c0 + n)
+        for k, (F, name, base, nat, nn) in enumerate(parts):
+            calls = []
+            for i in range(16):
+                lhs = T[F][:, 15 - i:143 - i]
+                rhs = T[name][:, base + 128 * i:base + 128 * i + nn] if nat else T[name][:, base + i:base + 16 * nn:16]
+                st, sp = (k == 0 and i == 0), (k == len(parts) - 1 and i == 15)
+                calls.append(lambda lhs=lhs, rhs=rhs, st=st, sp=sp: TE.matmul(out[0], lhs, rhs, st, sp))
+            rv = r(name, base, base + (2048 if nat else 16 * nn))
+            op("t", [r(F), rv], [out], calls)
+
+    def col(k):
+        return r("cols", k, k + 1)
+
+    def slot(k):
+        return r("p7", 128 * k, 128 * k + 128)
+
+    pVF, pV1, pQN, pVB = [r("p6", 128 * k, 128 * k + 128) for k in range(4)]
+    p1 = slice(0, 1)
+
+    dma("y", r("EI"), ext(T.ends[:], "ends"), True)
+    dma("s", r("X0", 0, P), ext(T.x[:], "x"), True)
+    dma("y", r("ST0"), ext(T.start[:], "start"), True)
+    dma("y", r("W"), ext(T.w[:], "w"), True)
+    for h in range(2):
+        for k in range(2):
+            dma("y", r("WD%d" % h, 16 * SC * k, 16 * SC * (k + 1)), ext(T.w[:, 1024 * h + 16 * VC:1024 * h + 1024], "w"), True)
+
+    def iota(out, pat, base, cm, small=True):
+        op("g", [], [out], [lambda: g.iota(out[0], pat, base, cm, allow_small_or_imprecise_dtypes=True) if small else g.iota(out[0], pat, base, cm)])
+
+    def asel(out, in_, pat, cmp, fl, base, cm):
+        op("g", [in_], [out], [lambda: g.affine_select(out[0], in_[0], pat, cmp, fl, base, cm)])
+
+    fill(r("ONEF"), 1.0)
+    fill(r("ONEB"), 1.0)
+    fill(r("MB"), 0.0)
+    fill(r("XBS", 0, 16), 0.0)
+    fill(r("XBS", P, XW), 0.0)
+    fill(r("X0", P, XW), 0.0)
+    fill(r("X1", P, XW), 0.0)
+    fill(r("ZERO"), 0.0)
+    iota(r("VI"), [[1, 128]], 0, 128, False)
+    asel(r("SHIFT"), r("ONEF"), [[-1, 128]], A.is_equal, 0.0, -1, 1)
+    asel(r("SHIFT"), r("SHIFT"), [[0, 8], [1, 16]], A.not_equal, 0.0, -15, 0)
+    iota(r("coli", 0, 1), [[0, 1]], 0, 1, False)
+    asel(r("F1"), r("ONEB"), [[-16, 9], [0, 16]], A.is_ge, 0.0, 0, 1)
+    asel(r("F1"), r("F1"), [[16, 9], [0, 16]], A.is_ge, 0.0, 15, -1)
+    asel(r("F1"), r("F1"), [[0, 9], [1, 16]], A.is_equal, 0.0, -15, 0)
+    asel(r("IDB"), r("ONEB", 0, 128), [[-1, 128]], A.is_equal, 0.0, 0, 1)
+    iota(r("IH"), [[0, 8], [1, 16]], 1, 0)
+    asel(r("IH"), r("IH"), [[-16, 8], [0, 16]], A.is_ge, -1000.0, 0, 1)
+    asel(r("IH"), r("IH"), [[16, 8], [0, 16]], A.is_ge, -1000.0, 15, -1)
+    iota(r("LOI", 0, 130), [[1, 130]], -1, 0)
+    asel(r("TRI"), r("ONEF"), [[-16, 8], [0, 16]], A.is_ge, 0.0, 0, 1)
+    asel(r("TRI"), r("TRI"), [[16, 8], [0, 16]], A.is_ge, 0.0, 15, -1)
+    asel(r("TRI"), r("TRI"), [[1, 128]], A.is_ge, 0.0, -1, -1)
+    asel(r("RST"), r("ONEF"), [[0, 8], [1, 16]], A.not_equal, 0.0, 0, 0)
+    asel(r("MK0"), r("ONEF"), [[0, 8], [1, 16]], A.is_equal, 0.0, 0, 0)
+    asel(r("SHR"), r("RST"), [[-1, 128]], A.is_equal, 0.0, 1, 1)
+    asel(r("SHL"), r("RST"), [[1, 128]], A.is_equal, 0.0, -128, 1)
+    asel(r("ID"), r("ONEF"), [[-1, 128]], A.is_equal, 0.0, 0, 1)
+    iota(r("LH", 0, 2048), [[0, 128], [128, 16]], 0, 0)
+    iota(r("LH", 2048, 4096), [[1, 128], [0, 16]], 1, 0)
+    ts(r("VI"), r("VI"), 2047, None, A.bitwise_and)
+    tc(r("VF"), r("VI"))
+    tc(pVF, r("VI"))
+    ts(r("V1"), r("VF"), 1.0, None, A.add)
+    ts(pV1, r("VF"), 1.0, None, A.add)
+
+    def later():
+        for n in ("HMR", "KT", "ST", "VD"):
+            iota(r(n), [[0, 2048]], 0, 0)
+        dma("y", (T.VD[0:128:16, :], "VD", 0, 2048, "a"), r("LH", 0, 2048, p=slice(0, 128, 16)))
+        dma("y", (T.VD[1:128:16, :], "VD", 0, 2048, "b"), r("LH", 2048, 4096, p=slice(1, 128, 16)))
+        ts(pVB, r("VF"), 6145.0, None, A.add)
+        ts(pQN, r("VF"), -1.0, 8192.0, A.mult, A.add)
+        ts(r("Q2"), r("VF"), 2.0, -8192.0, A.mult, A.add)
+        ts(r("coli", 1, 2), r("coli", 0, 1), 15, None, A.bitwise_and)
+        tc(col(0), r("coli", 1, 2))
+        ts(col(1), col(0), 2.0, None, A.is_lt)
+        ts(col(2), col(0), 14.0, None, A.is_lt)
+        ts(col(3), col(0), 14.0, None, A.is_ge)
+        ts(col(4), col(3), 256.0, 1792.0, A.mult, A.add)
+        ts(r("FA"), r("F1"), col(1), None, A.mult)
+        tt(r("FB"), r("F1"), r("FA"), A.subtract)
+
+    def table_start(t):
+        E = "E%d" % t
+        mm("p0", 0, 1, r("SHIFT"), r(E, 0, 1))
+        tt(slot(0), r(E, 0, 128), pV1, A.is_gt)
+        tt(slot(1), r("VF"), slot(0), A.add)
+        tc(r(E, 128, 129), r("p0", 0, 1))
+        tt(slot(2), r(E, 1, 129), r(E, 0, 128), A.is_lt)
+        tt(r("tC"), slot(2), r(E, 1, 129), A.mult)
+        tt(slot(2), slot(1), r("tC"), A.max)
+        tc(r("B16"), slot(2))
+        tc(r("bb"), slot(2))
+        tt(r("bl"), slot(2), r("bb"), A.subtract)
+        rows("MB", 0, 1, P, r("bb"))
+        rows("MB", 1, 1, P, r("bl"))
+        tt(r("nhE"), slot(0), r(E, 0, 128), A.mult)
+        ts(slot(3), slot(0), 1.0e6, None, A.mult)
+        ts(r("EL16"), r(E, 0, 128), -1.0, None, A.add)
+        for h in range(2):
+            a = 128 * t + 64 * h
+            ts(r("Z16", 64 * h, 64 * h + 64), r("ST0", a, a + 64), 1.0, None, A.add)
+            ts(r("ZF%d" % h, 0, 64), r("ST0", a, a + 64), 1.0, None, A.add)
+
+    def permute(eng, dst_, off, src, blocks, base=0):
+        for i in blocks:
+            o = r(dst_, off + 128 * (i - base), off + 128 * (i - base) + 128)
+            a = r(src, i, 2048, 16)
+            if eng == "v":
+                tc(o, a)
+            else:
+                act(o, a, AF.Copy)
+
+    tc(r("E0", 0, 128), r("EI"))
+    table_start(0)
+    ts(r("FP"), r("F1"), 4096.0, None, A.mult)
+    ts(r("FN"), r("F1"), -4096.0, None, A.mult)
+    ts(r("NIDB"), r("IDB"), -1.0, None, A.mult)
+    later()
+
+    def j_gather(h, which, t):
+        win, base = ("X%d" % t, 0) if which == 0 else ("XBS", 1024)
+        tt(r("R%d" % h, base, base + 16 * VC), ind(win, 0, XW, "Z16", 64 * h, 64 * h + VC), r("W", 1024 * h, 1024 * h + 16 * VC), A.min)
+
+    def s_gather(h, t):
+        n = 16 * SC
+        for k, win in enumerate(("XBS", "X%d" % t)):
+            act(r("GS%d" % h, n * k, n * k + n), ind(win, 0, XW, "Z16", 64 * h + VC, 64 * h + 64), AF.Copy)
+        o = r("p%d" % (4 + h), 0, 2 * n)
+        op("t", [r("IDB"), r("NIDB"), r("WD%d" % h), r("GS%d" % h)], [o],
+           [lambda: TE.matmul(o[0], T.IDB[:], T["WD%d" % h][:], True, False),
+            lambda: TE.matmul(o[0], T.NIDB[:], T["GS%d" % h][:], False, True)])
+
+    def s_meta(h):
+        act(r("MR%d" % h), ind("MB", 0, XW, "Z16", 64 * h, 64 * h + 64), AF.Copy)
+        conv("p%d" % (2 + h), 0, [("F1", "MR%d" % h, 0, False, 64)])
+
+    def s_relu(h):
+        n = 16 * SC
+        for k in range(2):
+            act(r("R%d" % h, 1024 * k + 16 * VC, 1024 * k + 1024), r("p%d" % (4 + h), n * k, n * k + n), AF.Relu)
+        conv("p%d" % h, 0, [("FP", "R%d" % h, 0, False, 64), ("FN", "R%d" % h, 1024, False, 64)])
+
+    def decide(h, step):
+        z0 = 64 * (step % 2)
+        z1 = 64 - z0
+        zf = "ZF%d" % h
+        a, b = 64 * h, 64 * h + 64
+        nv = r("nv", a, b)
+        tt(r("tA", a, b), r("p%d" % h, 0, 64), r(zf, z0, z0 + 64), A.max)
+        tt(nv, r("p%d" % (2 + h), 0, 64), r("tA", a, b), A.min)
+        if step < 5:
+            ts(r("Z16", a, b), nv, 1.0, None, A.add)
+            ts(r(zf, z1, z1 + 64), nv, 1.0, None, A.add)
+        if step == 1:
+            tt(r("VAL", a, b), r(zf, z1, z1 + 64), r(zf, z0, z0 + 64), A.not_equal)
+        if step == 5:
+            tc(r("vint", a, b), nv)
+            ts(r("hii", a, b), r("vint", a, b), 7, None, A.arith_shift_right)
+            ts(r("loi", a, b), r("vint", a, b), 127, None, A.bitwise_and)
+            ts(r("hiF", a, b), r("hii", a, b), 1.0, None, A.add)
+            ts(r("NLO", a, b), r("loi", a, b), -1.0, 0.5, A.mult, A.add)
+            tc(r("LOw", a, b), r("loi", a, b))
+            tt(r("HIw", a, b), r("hiF", a, b), r("VAL", a, b), A.mult)
+
+    def walks(t):
+        g2(None, "X%d" % t, XW, "B16", None, "XPHI")
+        permute("s", "XBS", 1, "XPHI", range(6))
+        permute("v", "XBS", 1, "XPHI", range(6, 16))
+        for s in range(12):
+            h = s % 2
+            s_gather(h, t)
+            s_meta(h)
+            j_gather(h, 0, t)
+            j_gather(h, 1, t)
+            s_relu(h)
+            if s:
+                decide(1 - h, (s - 1) // 2)
+        decide(1, 5)
+
+    def hist():
+        order = []
+        kv = 0
+        for c in range(128):
+            want = (NVR * (c + 1)) // 128
+            order.append(("V" if want > kv else "S", c))
+            kv = max(kv, want)
+        vs = [c for e, c in order if e == "V"]
+        ss = [c for e, c in order if e == "S"]
+        for e, c in order:
+            lh = r("LH", 128 * c, 128 * c + 128)
+            ts(lh, r("IH"), r("HIw", c, c + 1), None, A.is_equal)
+            if e == "V":
+                rh = r("RH", 130 * c, 130 * c + 128)
+                ts(rh, r("LOI", 1, 129), r("LOw", c, c + 1), None, A.is_equal)
+                bank, n, st, sp = "p4", 128, c == vs[0], c == vs[-1]
+            else:
+                rh = r("RH", 130 * c, 130 * c + 129)
+                act(rh, r("LOI", 0, 129), AF.Sign, r("NLO", c, c + 1))
+                bank, n, st, sp = "p5", 129, c == ss[0], c == ss[-1]
+            o = r(bank, 0, n)
+            op("t", [lh, rh], [o], [lambda: TE.matmul(o[0], lh[0], rh[0], st, sp)])
+
+    def g2(bank, src, W, lname, F, out):
+        o, i = r(out, 0, 1024), ind(src, 0, W, lname, 0, 64)
+        op("v", [i], [o], [lambda: V.tensor_copy(o[0], i[0])])
+        act(r(out, 1024, 2048), ind(src, 0, W, lname, 64, 128), AF.Copy)
+        if F is not None:
+            for k in range(2):
+                conv(bank, 64 * k, [(F, out, 1024 * k, False, 64)])
+
+    def row(name):
+        return r(name, p=p1)
+
+    def grow(t):
+        X = "X%d" % t
+        XN, EX = ("X1" if t == 0 else "Y2"), "E%d" % (t + 1)
+        HM = r("hm", 0, 128)
+        act(r("CSs", 0, 129), r("p5", 0, 129), AF.Copy)
+        act(r(X, XW, XW + P), r(X, 0, P), AF.Relu, -1.0)
+        tt(r("tA"), r("p5", 1, 129), r("CSs", 0, 128), A.subtract)
+        tt(slot(0), r("p4", 0, 128), r("tA"), A.add)
+        tc(r("tC"), slot(3))
+        tt(HM, slot(0), r("tC"), A.is_gt)
+        tc(r("hmb"), HM)
+        rows("HMR", 0, 0, P, r("hmb"))
+        mm("p0", 0, 1, r("SHIFT"), r("hm", 0, 1))
+        scan(r("HS"), HM, r("ZERO"), A.add, A.add)
+        mm("p1", 0, 1, r("TRI"), r("HS", 127, 128))
+        tc(r("hm", 128, 129), r("p0", 0, 1))
+        tt(r("hv"), HM, pVB, A.mult)
+        ts(r("HI"), r("HS"), r("p1", 0, 1), None, A.add)
+        tt(slot(1), r("HI"), pV1, A.subtract)
+        tt(r("KX"), HM, slot(1), A.subtract)
+        ts(r("kb"), slot(1), -1.0, None, A.mult)
+        tt(r("tA"), slot(1), r("kb"), A.add)
+        ts(r("kl"), r("tA"), -1.0, None, A.mult)
+        ts(col(12), r("KX", 127, 128), r("hm", 127, 128), None, A.subtract)
+        rows("KT", 0, 0, P, r("kb"))
+        rows("KT", 1, 0, P, r("kl"))
+        fill(r("SW", 0, 2048), 0.0)
+        g2("p2", "HMR", P, "B16", "F1", "GR")
+        tt(slot(0), r("p2", 0, 128), r("hm", 1, 129), A.max)
+        tt(r("mE"), slot(0), r("nhE"), A.mult)
+        scan(r("RCH", 1, 129), r("mE"), r("ZERO"), A.max, A.add)
+        mm("p3", 0, 128, r("RCH", 128, 129), r("SHR"), p=p1)
+        scan(row("rowA"), row("RST"), r("p3", 0, 128, p=p1), A.mult, A.max)
+        mm("p3", 200, 201, row("rowA"), r("ONEF", 0, 1, p=p1))
+        ts(r("RC2", 1, 129), r("RCH", 1, 129), r("p3", 200, 201), None, A.max)
+        tc(r("RC2", 0, 1), r("p3", 200, 201))
+        tt(slot(3), r("RC2", 1, 129), pVF, A.is_gt)
+        tt(slot(1), slot(3), HM, A.subtract)
+        scan(r("ks"), slot(1), r("ZERO"), A.add, A.add)
+        mm("p4", 0, 1, r("TRI"), r("ks", 127, 128))
+        tt(r("kx"), slot(1), r("ks"), A.subtract)
+        tt(slot(2), r("RC2", 0, 128), pVF, A.is_le)
+        ts(r("K2"), r("kx"), r("p4", 0, 1), -2.0, A.subtract, A.mult)
+        tt(r("FM"), slot(2), r("K2"), A.mult)
+        scan(r("Fs"), r("FM"), r("ZERO"), A.max, A.add)
+        mm("p5", 0, 128, r("Fs", 127, 128), r("SHR"), p=p1)
+        ts(slot(0), r("ks"), r("p4", 0, 1), None, A.add)
+        scan(row("rowB"), row("RST"), r("p5", 0, 128, p=p1), A.mult, A.max)
+        mm("p5", 200, 201, row("rowB"), r("ONEF", 0, 1, p=p1))
+        tc(r("nb"), slot(0))
+        tt(r("nl"), slot(0), r("nb"), A.subtract)
+        rows("KT", 2, 0, P, r("nb"))
+        rows("KT", 3, 0, P, r("nl"))
+        ts(slot(1), r("Fs"), r("p5", 200, 201), None, A.max)
+        tt(slot(1), slot(1), r("KX"), A.add)
+        tt(slot(2), slot(1), r("hv"), A.max)
+        ts(r("off16"), slot(2), -1.0, None, A.add)
+        o = ind("SW", 0, SWW, "off16", 0, 128)
+        op("v", [r("VD")], [o], [lambda: V.tensor_copy(o[0], T.VD[:])])
+        act(r(X, 2 * XW, 2 * XW + P), r(X, XW, XW + P), AF.Relu, -1.0)
+        act(r("GK"), ind("KT", 0, P, "EL16", 0, 128), AF.Copy)
+        conv("p2", 0, [("FA", "GK", 0, False, 128)])
+        conv("p1", 0, [("FB", "GK", 0, False, 128)])
+        conv("p0", 0, [("F1", "SW", 0, True, 128)])
+        ts(r("tA"), slot(2), 2049.0, 8192.0, A.is_lt, A.mult)
+        tt(r("tA"), slot(2), r("tA"), A.max)
+        op("v", [r("tA")], [col(8)], [lambda: V.tensor_reduce(col(8)[0], r("tA")[0], AxisListType.X, A.min)])
+        ts(col(9), col(8), -1.0, 8193.0, A.mult, A.add)
+        ts(col(10), r("p7", 127, 128), -2.0, 8192.0, A.mult, A.add)
+        tt(col(11), col(10), col(12), A.subtract)
+        mm("p5", 0, 128, col(9), r("ID"), p=p1)
+        mm("p5", 128, 256, col(11), r("ID"), p=p1)
+        ts(r("ex"), r("p0", 0, 128), 0.5, None, A.is_gt)
+        tt(r("eq"), r("ex"), pVF, A.mult)
+        tt(r("en"), r("ex"), pQN, A.mult)
+        scan(r("PF"), r("eq"), r("ZERO"), A.max, A.add)
+        scan(rev("NB"), rev("en"), r("ZERO"), A.max, A.add)
+        mm("p3", 0, 128, r("PF", 127, 128), r("SHR"), p=p1)
+        mm("p4", 0, 128, r("NB", 0, 1), r("SHL"), p=p1)
+        ts(r("nex"), r("ex"), -1.0, 1.0, A.mult, A.add)
+        scan(row("rowC"), row("RST"), r("p5", 0, 128, p=p1), A.mult, A.max)
+        tt(row("rowC"), row("rowC"), r("p5", 128, 256, p=p1), A.max)
+        scan(row("rowA"), row("RST"), r("p3", 0, 128, p=p1), A.mult, A.max)
+        mm("p3", 200, 201, row("rowA"), r("ONEF", 0, 1, p=p1))
+        tt(row("rowN"), rev("rowC", p1), row("MK0"), A.mult)
+        tt(row("rowT"), r("p4", 0, 128, p=p1), row("rowN"), A.max)
+        scan(rev("rowD", p1), row("RST"), row("rowT"), A.mult, A.max)
+        mm("p4", 200, 201, row("rowD"), r("ONEF", 0, 1, p=p1))
+        tt(r("tC"), r("p2", 0, 128), r("KX"), A.subtract)
+        ts(r("tD"), slot(3), -1.0, 1.0, A.mult, A.add)
+        ts(slot(0), r("PF"), r("p3", 200, 201), None, A.max)
+        ts(slot(1), r("p1", 0, 128), 2.0, None, A.mult)
+        ts(r("NN"), r("NB"), r("p4", 200, 201), None, A.max)
+        tt(slot(2), slot(0), r("NN"), A.subtract)
+        tt(r("SP"), slot(0), r("NN"), A.add)
+        tt(slot(2), slot(2), r("Q2"), A.is_lt)
+        ts(r("s"), r("SP"), -0.5, 4095.5, A.mult, A.add)
+        tt(slot(2), slot(2), r("nex"), A.add)
+        tt(r("csb"), slot(2), r("s"), A.mult)
+        tt(r("qq"), r("csb"), pVF, A.subtract)
+        ts(r("q16"), r("qq"), -1.0, None, A.mult)
+        tt(slot(1), slot(1), r("K2"), A.subtract)
+        tt(slot(1), slot(1), r("tD"), A.mult)
+        tt(slot(1), slot(1), r("tC"), A.add)
+        tc(r("sb"), slot(1))
+        tt(r("sl"), slot(1), r("sb"), A.subtract)
+        rows("ST", 0, 0, P, r("sb"))
+        rows("ST", 1, 0, P, r("sl"))
+        ts(r("cc"), slot(2), float(XW), -1.0, A.mult, A.add)
+        g2("p5", "SW", P, "q16", "F1", "GR")
+        ts(r("LS16"), r("p5", 0, 128), -1.0, None, A.add)
+        tt(r("L3"), r("p5", 0, 128), r("cc"), A.add)
+        tc(r("L316"), r("L3"))
+        g2("p2", "ST", P, "LS16", "F1", "GR")
+        g2(None, X, 3 * XW, "L316", None, "XPHI")
+        tt(slot(0), r("p2", 0, 128), r("V1"), A.add)
+        ts(r("SBE"), slot(0), col(4), None, A.min)
+        send("e", t)
+        permute("v", "SBX", 0, "XPHI", (14, 15), 14)
+        send("x", t)
+        permute("s", XN, 0, "XPHI", range(6))
+        permute("v", XN, 0, "XPHI", range(6, 14))
+        ts(r(EX, 0, 128), slot(0), col(4), col(2), A.min, A.mult)
+        if t == 1:
+            dma("y", ext(T.y[:, 0:CUT], "y", 0, CUT), r(XN, 0, CUT))
+        arrive("ae%d" % t, NE, "LE%d" % t, 0, 128)
+        ts(slot(0), r("LE%d" % t), col(3), None, A.mult)
+        tt(r(EX, 0, 128), slot(0), r(EX, 0, 128), A.add)
+        arrive("ax%d" % t, NX, XN, CUT, P)
+
+    def send(what, t):
+        if what == "x":
+            to, src, out, k, skip, rs, ls = rl[0], r("SBX"), T["RLX%d" % t][:], NX, 0, "rx%d" % t, "lx%d" % t
+        else:
+            to, src, out, k, skip, rs, ls = rl[1], r("SBE"), T["RLE%d" % t][:], NE, NX, "rn%d" % t, "le%d" % t
+        need("g", [src], [])
+        rid, pid = topo.addr(to, core)
+        g.remote_dma(out, src[0], T.sem[rs], T.sem[ls], pid, rid, pick(topo, core, to, k, skip))
+        count[ls] = k
+        clock = dict(known["g"])
+        clock[ls] = k
+        note("dma", [src], [], ls, k, clock)
+
+    def arrive(sem, k, name, lo, hi):
+        count[sem] = k
+        note("dma", [], [r(name, lo, hi)], sem, k, {sem: k})
+
+    for t in range(2):
+        if t:
+            table_start(t)
+        walks(t)
+        hist()
+        grow(t)
+    dma("y", ext(T.ye[:], "ye"), r("E2", 0, 128))
+    dma("y", ext(T.y[:, CUT:P], "y", CUT, P), r("Y2", CUT, P))
+    for sem, val in count.items():
+        if known["g"].get(sem, 0) < val:
+            g.wait_ge(T.sem[sem], val)

@@ -1,50 +1,65 @@
+from concourse.bass import DstId, RemoteDMATransfer
 from concourse.mybir import dt, AluOpType, AxisListType, ActivationFunctionType
 
 A = AluOpType
 AF = ActivationFunctionType
 P = 2048
-SC = 12
+SC = 14
 VC = 64 - SC
-NVR = 40
+PIECES = ((0, 12), (12, 24), (24, VC))
+SG = 2
+EARLY = 12
+LAG = 16
+OW = 144
 XW = 2064
 CUT = 1792
-SWW = 8192
+SWA = 4096
+SWW = SWA + 12288
+MAINV = 56
+TAIL = 1808
 
-BLK = ["VF", "V1", "Q2", "ZERO", "two", "nhE", "hv", "KX", "HS", "HI", "mE", "ks", "kx", "K2", "FM", "Fs", "ex", "nex", "eq", "en",
-       "PF", "NB", "NN", "PN", "SP", "cc", "s", "L3", "tA", "tC", "tD", "EN", "HIw", "LOw", "NLO", "VAL", "nv", "hiF", "qq", "csb",
-       "ID", "TRI", "SHIFT", "SHR", "SHL", "RST", "MK0", "ONEF", "rowA", "rowB", "rowC", "rowD", "rowN", "rowT"]
+BLK = ["VF", "V1", "Q2", "V1h", "QNh", "ZERO", "nhE", "thr", "hv", "KXh", "KX", "VFh", "HS", "mE", "ik", "cont", "ks", "ws", "Fl",
+       "PF", "NB", "NN", "SP", "nex", "tA", "tC", "tD", "qq", "HP", "LO", "ID", "TRI", "SHIFT", "SHR", "NSHR", "SHL", "RST",
+       "GRP", "SEL", "D2", "D1", "DH", "CV", "CS", "ONEF", "rowA", "rowB", "rowD"]
 SCRATCH = {"BK": ("sbuf", [128, 128 * len(BLK)], "float32")}
-for n_ in ("E0", "E1", "E2", "hm", "RCH", "RC2", "CSs"):
-    SCRATCH[n_] = ("sbuf", [128, 132], "float32")
-for n_ in ("VI", "vint", "hii", "loi"):
+for n_ in ("E0", "E1", "E2", "RCH", "IC"):
+    SCRATCH[n_] = ("sbuf", [128, 136], "float32")
+for n_ in ("VI", "EI"):
     SCRATCH[n_] = ("sbuf", [128, 128], "int32")
-for n_ in ("B16", "EL16", "off16", "q16", "L316", "LS16", "Z16", "SBE", "RLE0", "RLE1", "LE0", "LE1"):
+for n_ in ("B16", "EL16", "off16", "q16", "L16", "Z16"):
     SCRATCH[n_] = ("sbuf", [128, 128], "uint16")
-for n_ in ("IH", "IDB", "NIDB", "hmb", "kb", "kl", "bb", "bl", "sb", "sl", "nb", "nl"):
+for n_ in ("IDB", "NIDB", "N2ID", "IDP", "IDN", "SHB", "kb", "kl", "bb", "bl", "sb", "sl", "nb", "nl", "Hb", "INV"):
     SCRATCH[n_] = ("sbuf", [128, 128], "bfloat16")
-for n_ in ("F1", "FP", "FN", "FA", "FB", "ONEB", "LOI"):
+for n_ in ("F1", "FP", "FN", "FA", "FB", "ONEB", "hm"):
     SCRATCH[n_] = ("sbuf", [128, 144], "bfloat16")
-for n_ in ("XPHI", "GR", "GK", "W", "KT", "ST", "HMR", "VD", "Y2", "R0", "R1"):
+for n_ in ("TI", "TV", "TS"):
+    SCRATCH[n_] = ("sbuf", [128, 160], "bfloat16")
+for n_ in ("XPHI", "GH", "GK", "W", "KT", "HMR", "VD", "R0", "R1", "ZT"):
     SCRATCH[n_] = ("sbuf", [128, 2048], "bfloat16")
+for n_ in ("IDL", "IDT", "V1H", "SBE", "RLE0", "RLE1", "LE0", "LE1"):
+    SCRATCH[n_] = ("sbuf", [128, 136], "float16")
 SCRATCH.update({
-    "X0": ("sbuf", [128, 3 * XW], "bfloat16"), "X1": ("sbuf", [128, 3 * XW], "bfloat16"),
+    "X0": ("sbuf", [128, 3 * XW], "bfloat16"), "X1": ("sbuf", [128, 3 * XW], "bfloat16"), "ST": ("sbuf", [128, 3 * XW], "bfloat16"),
     "XBS": ("sbuf", [128, XW], "bfloat16"), "MB": ("sbuf", [128, XW], "bfloat16"),
-    "SW": ("sbuf", [128, SWW], "bfloat16"),
-    "LH": ("sbuf", [128, 128 * 128], "bfloat16"), "RH": ("sbuf", [128, 128 * 130], "bfloat16"),
-    "ST0": ("sbuf", [128, 256], "int32"), "EI": ("sbuf", [128, 128], "int32"),
+    "SW": ("sbuf", [128, SWW], "bfloat16"), "SG_": ("sbuf", [128, 2080], "bfloat16"),
+    "GR": ("sbuf", [128, 8, 256], "bfloat16"), "OH": ("sbuf", [128, 128 * OW], "bfloat16"),
+    "ST0": ("sbuf", [128, 256], "int32"), "CB": ("sbuf", [128, 320], "bfloat16"), "CX": ("sbuf", [128, 256], "bfloat16"),
     "cols": ("sbuf", [128, 32], "float32"), "coli": ("sbuf", [128, 8], "int32"),
-    "SBX": ("sbuf", [128, 256], "bfloat16"), "RLX0": ("sbuf", [128, 256], "bfloat16"), "RLX1": ("sbuf", [128, 256], "bfloat16"),
+    "MSK": ("sbuf", [128, 16], "float32"), "YR": ("sbuf", [128, 32], "float32"),
+    "SBX": ("sbuf", [128, 272], "bfloat16"), "RLX0": ("sbuf", [128, 272], "bfloat16"), "RLX1": ("sbuf", [128, 272], "bfloat16"),
+    "Y2": ("sbuf", [128, XW], "bfloat16"),
 })
 for n_ in (0, 1):
     SCRATCH["MR%d" % n_] = ("sbuf", [128, 1024], "bfloat16")
-    SCRATCH["WD%d" % n_] = ("sbuf", [128, 32 * SC], "bfloat16")
     SCRATCH["GS%d" % n_] = ("sbuf", [128, 32 * SC], "bfloat16")
-    SCRATCH["ZF%d" % n_] = ("sbuf", [128, 128], "float32")
+    SCRATCH["U%d" % n_] = ("sbuf", [128, 128], "float32")
+    SCRATCH["UP%d" % n_] = ("sbuf", [128, 192], "float32")
 for n_ in range(8):
     SCRATCH["p%d" % n_] = ("psum", [128, 512], "float32")
-SEMAPHORES = ["q_v", "q_s", "q_t", "q_g"] + ["d%d" % k for k in range(40)] + \
+SEMAPHORES = ["q_v", "q_s", "q_t", "q_g"] + ["d%d" % k for k in range(70)] + \
     [a + b for a in ("rx", "rn", "lx", "le", "ax", "ae") for b in "01"]
 NX, NE = 8, 4
+EW = 136
 
 
 def pick(topo, src, dst, k, skip=0):
@@ -65,7 +80,7 @@ def relay_program(g, core, T, topo):
         if core == rl[0]:
             for t in range(2):
                 g.wait_ge(T.sem["rx%d" % t], NX)
-                out = T.X1[:, CUT:P] if t == 0 else T.Y2[:, CUT:P]
+                out = T.X1[:, CUT:XW] if t == 0 else T.Y2[:, CUT:XW]
                 g.remote_dma(out, T["RLX%d" % t][:], T.sem["ax%d" % t], T.sem["lx%d" % t], pid, rid, pick(topo, core, dst, NX))
             for t in range(2):
                 g.wait_ge(T.sem["lx%d" % t], NX)
@@ -99,9 +114,16 @@ def rank_program(g, core, T, topo):
         pp = slice(None) if p is None else p
         return (t[pp, lo:hi] if step is None else t[pp, lo:hi:step], name, lo, hi, tag)
 
+    def r3(name, a, b, lo, hi):
+        w = T[name].shape[2]
+        return (T[name][:, a, lo:hi] if b == a + 1 else T[name][:, a:b, lo:hi], name, a * w, b * w, None)
+
     def rev(name, p=None):
+        pp = slice(None) if p is None else p
+        if name not in where:
+            return (T[name][pp, 127::-1], name, 0, 128, None)
         o = where[name]
-        return (T.BK[slice(None) if p is None else p, o + 127:(o - 1 if o else None):-1], "BK", o, o + 128, None)
+        return (T.BK[pp, o + 127:(o - 1 if o else None):-1], "BK", o, o + 128, None)
 
     def ind(name, lo, hi, lname, a, b):
         return (T[name][:, lo:hi].indirect(T[lname][:, a:b]), name, lo, hi, None, (None, lname, a, b, None))
@@ -168,8 +190,8 @@ def rank_program(g, core, T, topo):
     def ext(ap, name, lo=0, hi=2048):
         return (ap, "#" + name, lo, hi, None)
 
-    def rows(name, k, lo, n, src):
-        dma("y", (T[name][k:128:16, lo:lo + n], name, lo, lo + n, "row%d" % k), src)
+    def rows(name, k, lo, src):
+        dma("y", (T[name][k:128:16, lo:lo + P], name, lo, lo + P, "row%d" % k), src)
 
     V, S, TE = g.vector, g.scalar, g.tensor
 
@@ -191,47 +213,45 @@ def rank_program(g, core, T, topo):
     def fill(out, val):
         op("v", [], [out], [lambda: V.memset(out[0], val)])
 
-    def scan(out, d0, d1, o0, o1):
-        op("v", [d0, d1], [out], [lambda: V.tensor_tensor_scan(out[0], d0[0], d1[0], 0.0, o0, o1)])
+    def scan(out, d0, d1, o0, o1, first=0.0):
+        op("v", [d0, d1], [out], [lambda: V.tensor_tensor_scan(out[0], d0[0], d1[0], first, o0, o1)])
 
-    def act(out, a, f, bias=0.0):
+    def reduce_(out, a, o):
+        op("v", [a], [out], [lambda: V.tensor_reduce(out[0], a[0], AxisListType.X, o)])
+
+    def act(out, a, f, bias=0.0, scale=1.0):
         rd = [a] + ([bias] if isinstance(bias, tuple) else [])
         bb = bias[0] if isinstance(bias, tuple) else bias
-        op("s", rd, [out], [lambda: S.activation(out[0], a[0], f, bias=bb, scale=1.0)])
+        op("s", rd, [out], [lambda: S.activation(out[0], a[0], f, bias=bb, scale=scale)])
+
+    def mms(out, pairs, first=True, last=True):
+        n = len(pairs)
+        for k, (lhs, rhs) in enumerate(pairs):
+            op("t", [lhs, rhs], [out], [lambda: TE.matmul(out[0], lhs[0], rhs[0], first and k == 0, last and k == n - 1)])
 
     def mm(bank, c0, c1, lhs, rhs, p=None):
-        out = r(bank, c0, c1, p=p)
-        op("t", [lhs, rhs], [out], [lambda: TE.matmul(out[0], lhs[0], rhs[0], True, True)])
+        mms(r(bank, c0, c1, p=p), [(lhs, rhs)])
 
-    def conv(bank, c0, parts):
-        n = parts[0][4]
-        out = r(bank, c0, c0 + n)
-        for k, (F, name, base, nat, nn) in enumerate(parts):
-            calls = []
-            for i in range(16):
-                lhs = T[F][:, 15 - i:143 - i]
-                rhs = T[name][:, base + 128 * i:base + 128 * i + nn] if nat else T[name][:, base + i:base + 16 * nn:16]
-                st, sp = (k == 0 and i == 0), (k == len(parts) - 1 and i == 15)
-                calls.append(lambda lhs=lhs, rhs=rhs, st=st, sp=sp: TE.matmul(out[0], lhs, rhs, st, sp))
-            rv = r(name, base, base + (2048 if nat else 16 * nn))
-            op("t", [r(F), rv], [out], calls)
+    def sums(F, pick_, targets=range(16)):
+        return [(r(F, 15 - i, 143 - i), pick_(i)) for i in targets]
+
+    def walkers(name, base, n):
+        return lambda i: r(name, base + i, base + 16 * n, 16)
 
     def col(k):
         return r("cols", k, k + 1)
 
-    def slot(k):
-        return r("p7", 128 * k, 128 * k + 128)
+    def slot(k, n=128):
+        return r("p7", 128 * k, 128 * k + n)
 
-    pVF, pV1, pQN, pVB = [r("p6", 128 * k, 128 * k + 128) for k in range(4)]
+    pVF, pV1, pVB = [r("p6", 128 * k, 128 * k + 128) for k in range(3)]
     p1 = slice(0, 1)
 
     dma("y", r("EI"), ext(T.ends[:], "ends"), True)
-    dma("s", r("X0", 0, P), ext(T.x[:], "x"), True)
+    dma("y", r("X0", 0, P), ext(T.x[:], "x"), True)
     dma("y", r("ST0"), ext(T.start[:], "start"), True)
-    dma("y", r("W"), ext(T.w[:], "w"), True)
     for h in range(2):
-        for k in range(2):
-            dma("y", r("WD%d" % h, 16 * SC * k, 16 * SC * (k + 1)), ext(T.w[:, 1024 * h + 16 * VC:1024 * h + 1024], "w"), True)
+        dma("y", r("W", 1024 * h, 1024 * h + 1024), ext(T.w[:, 1024 * h:1024 * h + 1024], "w"), True)
 
     def iota(out, pat, base, cm, small=True):
         op("g", [], [out], [lambda: g.iota(out[0], pat, base, cm, allow_small_or_imprecise_dtypes=True) if small else g.iota(out[0], pat, base, cm)])
@@ -239,187 +259,278 @@ def rank_program(g, core, T, topo):
     def asel(out, in_, pat, cmp, fl, base, cm):
         op("g", [in_], [out], [lambda: g.affine_select(out[0], in_[0], pat, cmp, fl, base, cm)])
 
+    def band(name, entries, lo=0, hi=128):
+        src = r("ZERO", lo, hi)
+        for a, b, val in entries:
+            asel(r(name, lo, hi), src, [[a, hi - lo]], A.not_equal, val, b, 1)
+            src = r(name, lo, hi)
+
     fill(r("ONEF"), 1.0)
     fill(r("ONEB"), 1.0)
+    fill(r("ZERO"), 0.0)
     fill(r("MB"), 0.0)
     fill(r("XBS", 0, 16), 0.0)
     fill(r("XBS", P, XW), 0.0)
     fill(r("X0", P, XW), 0.0)
-    fill(r("X1", P, XW), 0.0)
-    fill(r("ZERO"), 0.0)
     iota(r("VI"), [[1, 128]], 0, 128, False)
     asel(r("SHIFT"), r("ONEF"), [[-1, 128]], A.is_equal, 0.0, -1, 1)
     asel(r("SHIFT"), r("SHIFT"), [[0, 8], [1, 16]], A.not_equal, 0.0, -15, 0)
-    iota(r("coli", 0, 1), [[0, 1]], 0, 1, False)
+    asel(r("IDB"), r("ONEB", 0, 128), [[-1, 128]], A.is_equal, 0.0, 0, 1)
     asel(r("F1"), r("ONEB"), [[-16, 9], [0, 16]], A.is_ge, 0.0, 0, 1)
     asel(r("F1"), r("F1"), [[16, 9], [0, 16]], A.is_ge, 0.0, 15, -1)
     asel(r("F1"), r("F1"), [[0, 9], [1, 16]], A.is_equal, 0.0, -15, 0)
-    asel(r("IDB"), r("ONEB", 0, 128), [[-1, 128]], A.is_equal, 0.0, 0, 1)
-    iota(r("IH"), [[0, 8], [1, 16]], 1, 0)
-    asel(r("IH"), r("IH"), [[-16, 8], [0, 16]], A.is_ge, -1000.0, 0, 1)
-    asel(r("IH"), r("IH"), [[16, 8], [0, 16]], A.is_ge, -1000.0, 15, -1)
-    iota(r("LOI", 0, 130), [[1, 130]], -1, 0)
-    asel(r("TRI"), r("ONEF"), [[-16, 8], [0, 16]], A.is_ge, 0.0, 0, 1)
-    asel(r("TRI"), r("TRI"), [[16, 8], [0, 16]], A.is_ge, 0.0, 15, -1)
-    asel(r("TRI"), r("TRI"), [[1, 128]], A.is_ge, 0.0, -1, -1)
-    asel(r("RST"), r("ONEF"), [[0, 8], [1, 16]], A.not_equal, 0.0, 0, 0)
-    asel(r("MK0"), r("ONEF"), [[0, 8], [1, 16]], A.is_equal, 0.0, 0, 0)
-    asel(r("SHR"), r("RST"), [[-1, 128]], A.is_equal, 0.0, 1, 1)
-    asel(r("SHL"), r("RST"), [[1, 128]], A.is_equal, 0.0, -128, 1)
-    asel(r("ID"), r("ONEF"), [[-1, 128]], A.is_equal, 0.0, 0, 1)
-    iota(r("LH", 0, 2048), [[0, 128], [128, 16]], 0, 0)
-    iota(r("LH", 2048, 4096), [[1, 128], [0, 16]], 1, 0)
+    iota(r("CB"), [[-1, 5], [0, 64]], 5, 0)
     ts(r("VI"), r("VI"), 2047, None, A.bitwise_and)
     tc(r("VF"), r("VI"))
-    tc(pVF, r("VI"))
-    ts(r("V1"), r("VF"), 1.0, None, A.add)
-    ts(pV1, r("VF"), 1.0, None, A.add)
+    ts(pV1, r("VI"), 1.0, None, A.add)
+    act(r("NIDB"), r("IDB"), AF.Copy, scale=-1.0)
+    act(r("FP"), r("F1"), AF.Copy, scale=4096.0)
+    act(r("FN"), r("F1"), AF.Copy, scale=-4096.0)
+    act(r("IDN"), r("IDB"), AF.Copy, scale=-4096.0)
 
-    def later():
-        for n in ("HMR", "KT", "ST", "VD"):
-            iota(r(n), [[0, 2048]], 0, 0)
-        dma("y", (T.VD[0:128:16, :], "VD", 0, 2048, "a"), r("LH", 0, 2048, p=slice(0, 128, 16)))
-        dma("y", (T.VD[1:128:16, :], "VD", 0, 2048, "b"), r("LH", 2048, 4096, p=slice(1, 128, 16)))
-        ts(pVB, r("VF"), 6145.0, None, A.add)
-        ts(pQN, r("VF"), -1.0, 8192.0, A.mult, A.add)
-        ts(r("Q2"), r("VF"), 2.0, -8192.0, A.mult, A.add)
-        ts(r("coli", 1, 2), r("coli", 0, 1), 15, None, A.bitwise_and)
-        tc(col(0), r("coli", 1, 2))
+    def beside_first_walks():
+        iota(r("ZT"), [[0, 2048]], 0, 0)
+        for n in ("HMR", "KT", "VD"):
+            dma("y", r(n), r("ZT"))
+        for c in range(3):
+            dma("y", r("ST", XW * c, XW * c + P), r("ZT"))
+            dma("y", r("SW", P * c, P * c + P), r("ZT"))
+        iota(r("OH", 0, 2048), [[0, 128], [128, 16]], 0, 0)
+        iota(r("OH", 2048, 4096), [[1, 128], [0, 16]], 1, 0)
+        dma("y", (T.VD[0:128:16, :], "VD", 0, 2048, "a"), r("OH", 0, 2048, p=slice(0, 128, 16)))
+        dma("y", (T.VD[8:128:16, :], "VD", 0, 2048, "b"), r("OH", 2048, 4096, p=slice(0, 128, 16)))
+        iota(r("CX"), [[XW, 2], [0, 128]], XW, 0)
+        for c in (1, 2):
+            rows("SW", 4, SWA - P * c, r("CX", 128 * c - 128, 128 * c))
+        for n in ("UP0", "UP1"):
+            iota(r(n), [[0, 192]], 0, 0)
+        asel(r("SEL"), r("ZERO"), [[-8, 2], [-16, 8], [-1, 8]], A.not_equal, 1.0 / 128, 0, 1)
+        iota(r("TI"), [[1, 160]], -128, 0)
+        band("D2", [(-1, 1, 1.0), (-1, 0, -2.0), (-1, -1, 1.0), (1, 0, -1.0)])
+        band("D1", [(-1, 1, 1.0), (-1, 0, -1.0), (128, -127, -1.0)])
+        nv = 16 * (8 - SG)
+        band("DH", [(-1, 1, -1.0), (-1, 0, 2.0), (-1, -1, -1.0)], 0, nv)
+        band("DH", [(-1, -nv, 1.0), (-1, -nv - 1, -2.0), (-1, -nv - 2, 1.0)], nv, 128)
+        asel(r("DH", 15, nv, 16), r("DH", 15, nv, 16), [[-16, 8 - SG]], A.not_equal, 1.0, -15, 1)
+        asel(r("DH"), r("DH"), [[-16, 8], [0, 16]], A.is_ge, 0.0, 0, 1)
+        asel(r("DH"), r("DH"), [[16, 8], [0, 16]], A.is_ge, 0.0, 15, -1)
+        for n in ("CV", "CS"):
+            iota(r(n), [[0, 128]], 0, 0)
+        iota(r("IC"), [[1, EW]], 0, 0)
+        iota(r("RCH", 0, 4), [[0, 4]], 0, 0)
+        iota(r("SG_", CUT, TAIL), [[0, 16]], 0, 0)
+        iota(r("SG_", TAIL + 256, 2080), [[0, 16]], 0, 0)
+        iota(r("SBX", 256, 2 * EW), [[0, 16]], 0, 0)
+        asel(r("GRP"), r("ONEF"), [[-16, 8], [0, 16]], A.is_ge, 0.0, 0, 1)
+        asel(r("GRP"), r("GRP"), [[16, 8], [0, 16]], A.is_ge, 0.0, 15, -1)
+        asel(r("TRI"), r("GRP"), [[1, 128]], A.is_ge, 0.0, -1, -1)
+        asel(r("RST"), r("ONEF"), [[0, 8], [1, 16]], A.not_equal, 0.0, 0, 0)
+        asel(r("SHR"), r("RST"), [[-1, 128]], A.is_equal, 0.0, 1, 1)
+        asel(r("SHL"), r("RST"), [[1, 128]], A.is_equal, 0.0, -128, 1)
+        asel(r("ID"), r("ONEF"), [[-1, 128]], A.is_equal, 0.0, 0, 1)
+
+    def mark_tables():
+        ts(r("TV", 0, 128), r("TI", 0, 128), 1.0 / 128, None, A.mult)
+        tc(r("TV", 128, OW), r("TI", 129, OW + 1))
+        act(r("TS", 0, 128), r("TI", 0, 128), AF.Identity, 1.0 / 256, 1.0 / 128)
+
+    def growth_constants(part):
+        if part:
+            tc(r("SHB"), r("SHIFT"))
+            ts(pVB, r("VF"), 6145.0, None, A.add)
+            return
+        act(r("IDP"), r("IDB"), AF.Copy, scale=4096.0)
+        act(r("N2ID"), r("IDB"), AF.Copy, scale=-2.0)
+        act(r("NSHR"), r("SHR"), AF.Copy, scale=-1.0)
+        act(r("GRP"), r("GRP"), AF.Copy, scale=-1.0)
+        act(r("V1"), r("VF"), AF.Identity, 1.0)
+        act(r("Q2"), r("VF"), AF.Identity, -10239.5)
+        act(r("V1h"), r("VF"), AF.Identity, 0.5, 0.5)
+        act(r("QNh"), r("VF"), AF.Identity, 4096.0, -0.5)
+        tc(pVF, r("VF"))
+        ts(col(0), r("VF", 0, 1), 1.0 / 128, None, A.mult)
+
+    def late_constants():
         ts(col(1), col(0), 2.0, None, A.is_lt)
+        ts(col(4), col(0), 2.0, 2.0, A.is_ge, A.mult)
         ts(col(2), col(0), 14.0, None, A.is_lt)
         ts(col(3), col(0), 14.0, None, A.is_ge)
-        ts(col(4), col(3), 256.0, 1792.0, A.mult, A.add)
+
+    def last_constants():
+        ts(r("V1H"), r("IC"), r("VF", 0, 1), 1.0, A.add, A.add)
+        ts(r("MSK"), r("IC", 0, 16), col(0), None, A.is_equal)
         ts(r("FA"), r("F1"), col(1), None, A.mult)
-        tt(r("FB"), r("F1"), r("FA"), A.subtract)
+        ts(r("FB"), r("F1"), col(4), None, A.mult)
+        ts(r("IDL", 0, 128), r("ID"), col(2), None, A.mult)
+        ts(r("IDT", 0, 128), r("ID"), col(3), None, A.mult)
 
     def table_start(t):
         E = "E%d" % t
-        mm("p0", 0, 1, r("SHIFT"), r(E, 0, 1))
-        tt(slot(0), r(E, 0, 128), pV1, A.is_gt)
-        tt(slot(1), r("VF"), slot(0), A.add)
-        tc(r(E, 128, 129), r("p0", 0, 1))
         tt(slot(2), r(E, 1, 129), r(E, 0, 128), A.is_lt)
+        tt(slot(0), r(E, 0, 128), pV1, A.is_gt)
         tt(r("tC"), slot(2), r(E, 1, 129), A.mult)
+        tt(slot(1), r("VF"), slot(0), A.add)
         tt(slot(2), slot(1), r("tC"), A.max)
         tc(r("B16"), slot(2))
         tc(r("bb"), slot(2))
+
+    def table_rest(t):
+        E = "E%d" % t
         tt(r("bl"), slot(2), r("bb"), A.subtract)
-        rows("MB", 0, 1, P, r("bb"))
-        rows("MB", 1, 1, P, r("bl"))
+        rows("MB", 0, 1, r("bb"))
+        rows("MB", 1, 1, r("bl"))
+        g2("X%d" % t, XW, "B16", "XPHI")
+        permute("s", "XBS", 1, "XPHI", range(6))
+        permute("v", "XBS", 1, "XPHI", range(6, 16))
         tt(r("nhE"), slot(0), r(E, 0, 128), A.mult)
-        ts(slot(3), slot(0), 1.0e6, None, A.mult)
+        ts(r("thr"), slot(0), 1.0e6, None, A.mult)
         ts(r("EL16"), r(E, 0, 128), -1.0, None, A.add)
+
+    def walkers_start(t):
         for h in range(2):
             a = 128 * t + 64 * h
             ts(r("Z16", 64 * h, 64 * h + 64), r("ST0", a, a + 64), 1.0, None, A.add)
-            ts(r("ZF%d" % h, 0, 64), r("ST0", a, a + 64), 1.0, None, A.add)
+            ts(r("U%d" % h, 0, 64), r("ST0", a, a + 64), 6.0, None, A.add)
 
-    def permute(eng, dst_, off, src, blocks, base=0):
+    def permute(eng, dst_, off, src, blocks):
         for i in blocks:
-            o = r(dst_, off + 128 * (i - base), off + 128 * (i - base) + 128)
+            o = r(dst_, off + 128 * i, off + 128 * i + 128)
             a = r(src, i, 2048, 16)
             if eng == "v":
                 tc(o, a)
             else:
                 act(o, a, AF.Copy)
 
-    tc(r("E0", 0, 128), r("EI"))
-    table_start(0)
-    ts(r("FP"), r("F1"), 4096.0, None, A.mult)
-    ts(r("FN"), r("F1"), -4096.0, None, A.mult)
-    ts(r("NIDB"), r("IDB"), -1.0, None, A.mult)
-    later()
+    def gather(eng, out, src, lo, hi, lname, a, b):
+        i = ind(src, lo, hi, lname, a, b)
+        if eng == "v":
+            tc(out, i)
+        else:
+            act(out, i, AF.Copy)
 
-    def j_gather(h, which, t):
+    def g2(src, W, lname, out):
+        gather("v", r(out, 0, 1024), src, 0, W, lname, 0, 64)
+        gather("s", r(out, 1024, 2048), src, 0, W, lname, 64, 128)
+
+    def j_gather(h, which, t, a=0, b=VC):
         win, base = ("X%d" % t, 0) if which == 0 else ("XBS", 1024)
-        tt(r("R%d" % h, base, base + 16 * VC), ind(win, 0, XW, "Z16", 64 * h, 64 * h + VC), r("W", 1024 * h, 1024 * h + 16 * VC), A.min)
+        tt(r("R%d" % h, base + 16 * a, base + 16 * b), ind(win, 0, XW, "Z16", 64 * h + a, 64 * h + b),
+           r("W", 1024 * h + 16 * a, 1024 * h + 16 * b), A.min)
 
     def s_gather(h, t):
         n = 16 * SC
         for k, win in enumerate(("XBS", "X%d" % t)):
-            act(r("GS%d" % h, n * k, n * k + n), ind(win, 0, XW, "Z16", 64 * h + VC, 64 * h + 64), AF.Copy)
-        o = r("p%d" % (4 + h), 0, 2 * n)
-        op("t", [r("IDB"), r("NIDB"), r("WD%d" % h), r("GS%d" % h)], [o],
-           [lambda: TE.matmul(o[0], T.IDB[:], T["WD%d" % h][:], True, False),
-            lambda: TE.matmul(o[0], T.NIDB[:], T["GS%d" % h][:], False, True)])
+            gs = r("GS%d" % h, n * k, n * k + n)
+            gather("s", gs, win, 0, XW, "Z16", 64 * h + VC, 64 * h + 64)
+            mms(r("p%d" % (4 + h), n * k, n * k + n), [(r("IDB"), r("W", 1024 * h + 16 * VC, 1024 * h + 1024)), (r("NIDB"), gs)])
 
-    def s_meta(h):
-        act(r("MR%d" % h), ind("MB", 0, XW, "Z16", 64 * h, 64 * h + 64), AF.Copy)
-        conv("p%d" % (2 + h), 0, [("F1", "MR%d" % h, 0, False, 64)])
+    def s_meta(h, step):
+        gather("s", r("MR%d" % h), "MB", 0, XW, "Z16", 64 * h, 64 * h + 64)
+        shift = (r("IDB"), r("CB", 64 * step, 64 * step + 64)) if step < 5 else (r("IDN"), r("INV", 64 * h, 64 * h + 64))
+        mms(r("p%d" % (2 + h), 0, 64), [shift] + sums("F1", walkers("MR%d" % h, 0, 64)))
 
     def s_relu(h):
         n = 16 * SC
         for k in range(2):
             act(r("R%d" % h, 1024 * k + 16 * VC, 1024 * k + 1024), r("p%d" % (4 + h), n * k, n * k + n), AF.Relu)
-        conv("p%d" % h, 0, [("FP", "R%d" % h, 0, False, 64), ("FN", "R%d" % h, 1024, False, 64)])
+        mms(r("p%d" % h, 0, 64), sums("FP", walkers("R%d" % h, 0, 64)) + sums("FN", walkers("R%d" % h, 1024, 64)))
 
     def decide(h, step):
         z0 = 64 * (step % 2)
-        z1 = 64 - z0
-        zf = "ZF%d" % h
+        u = "U%d" % h
         a, b = 64 * h, 64 * h + 64
-        nv = r("nv", a, b)
-        tt(r("tA", a, b), r("p%d" % h, 0, 64), r(zf, z0, z0 + 64), A.max)
-        tt(nv, r("p%d" % (2 + h), 0, 64), r("tA", a, b), A.min)
-        if step < 5:
-            ts(r("Z16", a, b), nv, 1.0, None, A.add)
-            ts(r(zf, z1, z1 + 64), nv, 1.0, None, A.add)
-        if step == 1:
-            tt(r("VAL", a, b), r(zf, z1, z1 + 64), r(zf, z0, z0 + 64), A.not_equal)
-        if step == 5:
-            tc(r("vint", a, b), nv)
-            ts(r("hii", a, b), r("vint", a, b), 7, None, A.arith_shift_right)
-            ts(r("loi", a, b), r("vint", a, b), 127, None, A.bitwise_and)
-            ts(r("hiF", a, b), r("hii", a, b), 1.0, None, A.add)
-            ts(r("NLO", a, b), r("loi", a, b), -1.0, 0.5, A.mult, A.add)
-            tc(r("LOw", a, b), r("loi", a, b))
-            tt(r("HIw", a, b), r("hiF", a, b), r("VAL", a, b), A.mult)
+        old, new = r(u, z0, z0 + 64), (r(u, 64 - z0, 128 - z0) if step < 5 else r("UP%d" % h, 64, 128))
+
+        def last():
+            if step < 5:
+                ts(r("Z16", a, b), new, step - 4.0, None, A.add)
+            else:
+                turn(h)
+            if step == 1:
+                tt(r("INV", a, b), new, old, A.is_lt)
+        return [lambda: tt(r("tA", a, b), r("p%d" % h, 0, 64), old, A.max),
+                lambda: tt(new, r("p%d" % (2 + h), 0, 64), r("tA", a, b), A.min), last]
+
+    def turn(h):
+        a, b = 64 * h, 64 * h + 64
+        pp = r("p%d" % h, 0, 64)
+        mms(pp, [(r("UP%d" % h, 64, 192), r("SEL", 0, 64)), (r("UP%d" % h, 0, 128), r("SEL", 64, 128))])
+
+    def split(h):
+        a, b = 64 * h, 64 * h + 64
+        pp = r("p%d" % h, 0, 64)
+        ts(r("Hb", a, b), pp, 129.0 - 63.5 / 128, 128.0, A.add, A.max)
+        ts(r("HP", a, b), r("Hb", a, b), -128.0, None, A.add)
+        tt(r("LO", a, b), pp, r("HP", a, b), A.subtract)
+
+    def spell(gr, h, i):
+        j, c = 16 * gr + 8 * h + i, 64 * h + 8 * gr + i
+        o = OW * j
+        if gr < 8 - SG:
+            ts(r("OH", o, o + OW), r("TV", 0, OW), r("LO", c, c + 1), r("HP", c, c + 1), A.max, A.min)
+        else:
+            act(r("OH", o, o + 128), r("TS", 0, 128), AF.Sign, r("LO", c, c + 1), -1.0)
+            act(r("OH", o + 128, o + OW), r("TI", 128, OW), AF.Relu, r("HP", c, c + 1), -1.0)
+
+    def tally(gr, k):
+        o = OW * (16 * gr + k)
+        bank, c = ("p2", 16 * gr) if gr < 8 - SG else ("p4", 16 * (gr - 8 + SG))
+        mms(r(bank, c, c + 16), [(r("OH", o, o + 128), r("OH", o + 128, o + OW))], k == 0, k == 15)
 
     def walks(t):
-        g2(None, "X%d" % t, XW, "B16", None, "XPHI")
-        permute("s", "XBS", 1, "XPHI", range(6))
-        permute("v", "XBS", 1, "XPHI", range(6, 16))
         for s in range(12):
             h = s % 2
             s_gather(h, t)
-            s_meta(h)
+            s_meta(h, s // 2)
             j_gather(h, 0, t)
-            j_gather(h, 1, t)
-            s_relu(h)
             if s:
-                decide(1 - h, (s - 1) // 2)
-        decide(1, 5)
-
-    def hist():
-        order = []
-        kv = 0
-        for c in range(128):
-            want = (NVR * (c + 1)) // 128
-            order.append(("V" if want > kv else "S", c))
-            kv = max(kv, want)
-        vs = [c for e, c in order if e == "V"]
-        ss = [c for e, c in order if e == "S"]
-        for e, c in order:
-            lh = r("LH", 128 * c, 128 * c + 128)
-            ts(lh, r("IH"), r("HIw", c, c + 1), None, A.is_equal)
-            if e == "V":
-                rh = r("RH", 130 * c, 130 * c + 128)
-                ts(rh, r("LOI", 1, 129), r("LOw", c, c + 1), None, A.is_equal)
-                bank, n, st, sp = "p4", 128, c == vs[0], c == vs[-1]
+                for call, (a, b) in zip(decide(1 - h, (s - 1) // 2), PIECES):
+                    call()
+                    j_gather(h, 1, t, a, b)
             else:
-                rh = r("RH", 130 * c, 130 * c + 129)
-                act(rh, r("LOI", 0, 129), AF.Sign, r("NLO", c, c + 1))
-                bank, n, st, sp = "p5", 129, c == ss[0], c == ss[-1]
-            o = r(bank, 0, n)
-            op("t", [lh, rh], [o], [lambda: TE.matmul(o[0], lh[0], rh[0], st, sp)])
+                j_gather(h, 1, t)
+            s_relu(h)
+            if s == 8 and t == 0:
+                mark_tables()
 
-    def g2(bank, src, W, lname, F, out):
-        o, i = r(out, 0, 1024), ind(src, 0, W, lname, 0, 64)
-        op("v", [i], [o], [lambda: V.tensor_copy(o[0], i[0])])
-        act(r(out, 1024, 2048), ind(src, 0, W, lname, 64, 128), AF.Copy)
-        if F is not None:
-            for k in range(2):
-                conv(bank, 64 * k, [(F, out, 1024 * k, False, 64)])
+    def marks(t):
+        NV = 8 - SG
+        split(0)
+        early = [(gr, 0, i) for gr in range(NV) for i in range(8)][:EARLY]
+        for c in early:
+            spell(*c)
+        for gr in range(NV, 8):
+            for i in range(8):
+                spell(gr, 0, i)
+        for call in decide(1, 5):
+            call()
+        split(1)
+        mine = [(gr, k // 8, k % 8) for gr in range(NV) for k in range(16)]
+        theirs = [(gr, k // 8, k % 8) for gr in range(NV, 8) for k in range(16)]
+        todo = [c for c in theirs if c[1] == 1]
+        done = 0
+        for n, c in enumerate(mine):
+            if c not in early:
+                spell(*c)
+            tally(c[0], 8 * c[1] + c[2])
+            while done < len(theirs) and done * (len(mine) - LAG) < (n + 1) * len(theirs):
+                d = theirs[done]
+                if d in todo:
+                    spell(*d)
+                tally(d[0], 8 * d[1] + d[2])
+                done += 1
+            if n == len(mine) - LAG - 1:
+                act(r("CS", 16 * NV, 128), r("p4", 0, 16 * SG), AF.Copy)
+            if n == len(mine) - LAG // 2:
+                mms(r("p3", 0, 128), [(r("CS"), r("D1"))], True, False)
+        tc(r("CV", 0, 16 * NV), r("p2", 0, 16 * NV))
+        mms(r("p3", 0, 128), [(r("CV"), r("D2"))], False, True)
+        if t == 0:
+            growth_constants(0)
+        tc(r("tA"), r("p3", 0, 128))
+        mm("p0", 0, 128, r("DH"), r("tA"))
+        if t == 0:
+            growth_constants(1)
 
     def row(name):
         return r(name, p=p1)
@@ -428,154 +539,159 @@ def rank_program(g, core, T, topo):
         X = "X%d" % t
         XN, EX = ("X1" if t == 0 else "Y2"), "E%d" % (t + 1)
         HM = r("hm", 0, 128)
-        act(r("CSs", 0, 129), r("p5", 0, 129), AF.Copy)
-        act(r(X, XW, XW + P), r(X, 0, P), AF.Relu, -1.0)
-        tt(r("tA"), r("p5", 1, 129), r("CSs", 0, 128), A.subtract)
-        tt(slot(0), r("p4", 0, 128), r("tA"), A.add)
-        tc(r("tC"), slot(3))
-        tt(HM, slot(0), r("tC"), A.is_gt)
-        tc(r("hmb"), HM)
-        rows("HMR", 0, 0, P, r("hmb"))
-        mm("p0", 0, 1, r("SHIFT"), r("hm", 0, 1))
+        tt(HM, r("p0", 0, 128), r("thr"), A.is_gt)
+        rows("HMR", 0, 0, HM)
+        mm("p5", 0, 1, r("SHB"), r("hm", 0, 1))
         scan(r("HS"), HM, r("ZERO"), A.add, A.add)
-        mm("p1", 0, 1, r("TRI"), r("HS", 127, 128))
-        tc(r("hm", 128, 129), r("p0", 0, 1))
+        mm("p4", 0, 1, r("TRI"), r("HS", 127, 128))
         tt(r("hv"), HM, pVB, A.mult)
-        ts(r("HI"), r("HS"), r("p1", 0, 1), None, A.add)
-        tt(slot(1), r("HI"), pV1, A.subtract)
-        tt(r("KX"), HM, slot(1), A.subtract)
-        ts(r("kb"), slot(1), -1.0, None, A.mult)
-        tt(r("tA"), slot(1), r("kb"), A.add)
-        ts(r("kl"), r("tA"), -1.0, None, A.mult)
-        ts(col(12), r("KX", 127, 128), r("hm", 127, 128), None, A.subtract)
-        rows("KT", 0, 0, P, r("kb"))
-        rows("KT", 1, 0, P, r("kl"))
-        fill(r("SW", 0, 2048), 0.0)
-        g2("p2", "HMR", P, "B16", "F1", "GR")
-        tt(slot(0), r("p2", 0, 128), r("hm", 1, 129), A.max)
-        tt(r("mE"), slot(0), r("nhE"), A.mult)
+        tc(r("hm", 128, 129), r("p5", 0, 1))
+        ts(slot(1), r("HS"), r("p4", 0, 1), None, A.add)
+        tt(r("VFh"), r("hv"), pVF, A.max)
+        tt(slot(0), r("V1"), slot(1), A.subtract)
+        tc(r("kb"), slot(0))
+        tt(r("KX"), slot(0), r("hv"), A.max)
+        tt(r("kl"), slot(0), r("kb"), A.subtract)
+        rows("KT", 0, 0, r("kb"))
+        rows("KT", 1, 0, r("kl"))
+        ts(r("KXh"), r("KX"), 0.5, None, A.mult)
+        for k in range(2):
+            for eng, a in (("v", 64 * k), ("s", 64 * k + 32)):
+                gather(eng, r("GH", 16 * a, 16 * a + 512), "HMR", 0, P, "B16", a, a + 32)
+            mms(r("p2", 64 * k, 64 * k + 64), [(r("IDP"), r("hm", 64 * k + 1, 64 * k + 65))] + sums("FP", walkers("GH", 1024 * k, 64)))
+        act(r(X, XW, XW + P), r(X, 0, P), AF.Relu, -1.0)
+        if t == 0:
+            late_constants()
+        tt(r("mE"), r("p2", 0, 128), r("nhE"), A.min)
         scan(r("RCH", 1, 129), r("mE"), r("ZERO"), A.max, A.add)
-        mm("p3", 0, 128, r("RCH", 128, 129), r("SHR"), p=p1)
-        scan(row("rowA"), row("RST"), r("p3", 0, 128, p=p1), A.mult, A.max)
-        mm("p3", 200, 201, row("rowA"), r("ONEF", 0, 1, p=p1))
-        ts(r("RC2", 1, 129), r("RCH", 1, 129), r("p3", 200, 201), None, A.max)
-        tc(r("RC2", 0, 1), r("p3", 200, 201))
-        tt(slot(3), r("RC2", 1, 129), pVF, A.is_gt)
-        tt(slot(1), slot(3), HM, A.subtract)
-        scan(r("ks"), slot(1), r("ZERO"), A.add, A.add)
+        mm("p1", 0, 128, r("RCH", 128, 129), r("SHR"), p=p1)
+        if t == 0:
+            last_constants()
+        scan(row("rowA"), row("RST"), r("p1", 0, 128, p=p1), A.mult, A.max)
+        mm("p1", 200, 201, row("rowA"), r("ONEF", 0, 1, p=p1))
+        ts(slot(0, 129), r("RCH", 0, 129), r("p1", 200, 201), None, A.max)
+        tt(r("ik"), r("p7", 1, 129), r("VFh"), A.is_gt)
+        tt(r("cont"), slot(0), r("VF"), A.is_gt)
+        scan(r("ks"), r("ik"), r("ZERO"), A.add, A.add)
+        scan(r("ws"), r("cont"), r("ik"), A.mult, A.add, 8192.0)
         mm("p4", 0, 1, r("TRI"), r("ks", 127, 128))
-        tt(r("kx"), slot(1), r("ks"), A.subtract)
-        tt(slot(2), r("RC2", 0, 128), pVF, A.is_le)
-        ts(r("K2"), r("kx"), r("p4", 0, 1), -2.0, A.subtract, A.mult)
-        tt(r("FM"), slot(2), r("K2"), A.mult)
-        scan(r("Fs"), r("FM"), r("ZERO"), A.max, A.add)
-        mm("p5", 0, 128, r("Fs", 127, 128), r("SHR"), p=p1)
+        mms(r("p5", 0, 128, p=p1), [(r("ks", 127, 128), r("TRI")), (r("ws", 127, 128), r("NSHR"))])
+        tt(r("Fl"), r("ks"), r("ws"), A.subtract)
         ts(slot(0), r("ks"), r("p4", 0, 1), None, A.add)
         scan(row("rowB"), row("RST"), r("p5", 0, 128, p=p1), A.mult, A.max)
         mm("p5", 200, 201, row("rowB"), r("ONEF", 0, 1, p=p1))
         tc(r("nb"), slot(0))
         tt(r("nl"), slot(0), r("nb"), A.subtract)
-        rows("KT", 2, 0, P, r("nb"))
-        rows("KT", 3, 0, P, r("nl"))
-        ts(slot(1), r("Fs"), r("p5", 200, 201), None, A.max)
-        tt(slot(1), slot(1), r("KX"), A.add)
-        tt(slot(2), slot(1), r("hv"), A.max)
-        ts(r("off16"), slot(2), -1.0, None, A.add)
-        o = ind("SW", 0, SWW, "off16", 0, 128)
+        rows("KT", 2, 0, r("nb"))
+        rows("KT", 3, 0, r("nl"))
+        ts(slot(2), r("Fl"), r("p4", 0, 1), r("p5", 200, 201), A.add, A.max)
+        ts(r("tD"), r("ik"), -1.0, 1.0, A.mult, A.add)
+        tt(slot(3), slot(2), r("KXh"), A.add)
+        ts(r("YR", 17, 18), r("HS", 127, 128), -0.5, None, A.mult)
+        ts(r("off16"), slot(3), 2.0, -1.0, A.mult, A.add)
+        ts(r("YR", 16, 17), r("YR", 17, 18), r("ks", 127, 128), 64.0 - 256.0, A.add, A.add)
+        o = ind("SW", SWA, SWW, "off16", 0, 128)
         op("v", [r("VD")], [o], [lambda: V.tensor_copy(o[0], T.VD[:])])
         act(r(X, 2 * XW, 2 * XW + P), r(X, XW, XW + P), AF.Relu, -1.0)
-        act(r("GK"), ind("KT", 0, P, "EL16", 0, 128), AF.Copy)
-        conv("p2", 0, [("FA", "GK", 0, False, 128)])
-        conv("p1", 0, [("FB", "GK", 0, False, 128)])
-        conv("p0", 0, [("F1", "SW", 0, True, 128)])
-        ts(r("tA"), slot(2), 2049.0, 8192.0, A.is_lt, A.mult)
-        tt(r("tA"), slot(2), r("tA"), A.max)
-        op("v", [r("tA")], [col(8)], [lambda: V.tensor_reduce(col(8)[0], r("tA")[0], AxisListType.X, A.min)])
-        ts(col(9), col(8), -1.0, 8193.0, A.mult, A.add)
-        ts(col(10), r("p7", 127, 128), -2.0, 8192.0, A.mult, A.add)
-        tt(col(11), col(10), col(12), A.subtract)
-        mm("p5", 0, 128, col(9), r("ID"), p=p1)
-        mm("p5", 128, 256, col(11), r("ID"), p=p1)
-        ts(r("ex"), r("p0", 0, 128), 0.5, None, A.is_gt)
-        tt(r("eq"), r("ex"), pVF, A.mult)
-        tt(r("en"), r("ex"), pQN, A.mult)
-        scan(r("PF"), r("eq"), r("ZERO"), A.max, A.add)
-        scan(rev("NB"), rev("en"), r("ZERO"), A.max, A.add)
+        gather("s", r("GK"), "KT", 0, P, "EL16", 0, 128)
+        mms(r("p2", 0, 128), [(r("NIDB"), r("kb")), (r("NIDB"), r("kl"))] + sums("FA", walkers("GK", 0, 128)))
+        mms(r("p1", 0, 128), [(r("N2ID"), r("nb")), (r("N2ID"), r("nl"))] + sums("FB", walkers("GK", 0, 128)))
+        mms(r("p0", 0, 128), sums("FP", lambda i: r("SW", SWA + 128 * i, SWA + 128 * i + 128)))
+        for c in (1, 2):
+            dma("y", (T.SW[0:128:8, SWA - P * c:SWA - P * c + P], "SW", SWA - P * c, SWA - P * c + P, "row08"),
+                r("SW", SWA, SWA + P, p=slice(0, 128, 8)))
+        ts(r("tA"), slot(3), 1024.25, 8192.0, A.is_lt, A.mult)
+        tt(r("tA"), slot(3), r("tA"), A.max)
+        reduce_(col(8), r("tA"), A.min)
+        ts(r("YR", 0, 16), r("MSK"), col(8), -(4096.5 / 16), A.mult, A.add)
+        mm("p4", 0, 17, r("GRP"), r("YR", 0, 17))
+        scan(r("PF"), r("p0", 0, 128), r("V1h"), A.max, A.min)
+        scan(rev("NB"), rev("p0"), rev("QNh"), A.max, A.min)
         mm("p3", 0, 128, r("PF", 127, 128), r("SHR"), p=p1)
-        mm("p4", 0, 128, r("NB", 0, 1), r("SHL"), p=p1)
-        ts(r("nex"), r("ex"), -1.0, 1.0, A.mult, A.add)
-        scan(row("rowC"), row("RST"), r("p5", 0, 128, p=p1), A.mult, A.max)
-        tt(row("rowC"), row("rowC"), r("p5", 128, 256, p=p1), A.max)
+        mm("p5", 0, 128, r("NB", 0, 1), r("SHL"), p=p1)
+        ts(r("nex"), r("p0", 0, 128), 0.0, None, A.is_equal)
+        reduce_(col(9), r("p4", 0, 17), A.max)
         scan(row("rowA"), row("RST"), r("p3", 0, 128, p=p1), A.mult, A.max)
         mm("p3", 200, 201, row("rowA"), r("ONEF", 0, 1, p=p1))
-        tt(row("rowN"), rev("rowC", p1), row("MK0"), A.mult)
-        tt(row("rowT"), r("p4", 0, 128, p=p1), row("rowN"), A.max)
-        scan(rev("rowD", p1), row("RST"), row("rowT"), A.mult, A.max)
-        mm("p4", 200, 201, row("rowD"), r("ONEF", 0, 1, p=p1))
-        tt(r("tC"), r("p2", 0, 128), r("KX"), A.subtract)
-        ts(r("tD"), slot(3), -1.0, 1.0, A.mult, A.add)
-        ts(slot(0), r("PF"), r("p3", 200, 201), None, A.max)
-        ts(slot(1), r("p1", 0, 128), 2.0, None, A.mult)
-        ts(r("NN"), r("NB"), r("p4", 200, 201), None, A.max)
-        tt(slot(2), slot(0), r("NN"), A.subtract)
+        scan(rev("rowD", p1), row("RST"), r("p5", 0, 128, p=p1), A.mult, A.max)
+        mm("p5", 200, 201, row("rowD"), r("ONEF", 0, 1, p=p1))
+        tt(r("tC"), r("p1", 0, 128), r("tD"), A.mult)
+        ts(slot(0), r("PF"), r("p3", 200, 201), -6144.0, A.max, A.add)
+        ts(r("NN"), r("NB"), r("p5", 200, 201), col(9), A.max, A.max)
+        tt(slot(2), r("p2", 0, 128), r("tC"), A.add)
+        tt(slot(1), slot(0), r("NN"), A.subtract)
         tt(r("SP"), slot(0), r("NN"), A.add)
-        tt(slot(2), slot(2), r("Q2"), A.is_lt)
-        ts(r("s"), r("SP"), -0.5, 4095.5, A.mult, A.add)
-        tt(slot(2), slot(2), r("nex"), A.add)
-        tt(r("csb"), slot(2), r("s"), A.mult)
-        tt(r("qq"), r("csb"), pVF, A.subtract)
-        ts(r("q16"), r("qq"), -1.0, None, A.mult)
-        tt(slot(1), slot(1), r("K2"), A.subtract)
-        tt(slot(1), slot(1), r("tD"), A.mult)
-        tt(slot(1), slot(1), r("tC"), A.add)
-        tc(r("sb"), slot(1))
-        tt(r("sl"), slot(1), r("sb"), A.subtract)
-        rows("ST", 0, 0, P, r("sb"))
-        rows("ST", 1, 0, P, r("sl"))
-        ts(r("cc"), slot(2), float(XW), -1.0, A.mult, A.add)
-        g2("p5", "SW", P, "q16", "F1", "GR")
-        ts(r("LS16"), r("p5", 0, 128), -1.0, None, A.add)
-        tt(r("L3"), r("p5", 0, 128), r("cc"), A.add)
-        tc(r("L316"), r("L3"))
-        g2("p2", "ST", P, "LS16", "F1", "GR")
-        g2(None, X, 3 * XW, "L316", None, "XPHI")
-        tt(slot(0), r("p2", 0, 128), r("V1"), A.add)
-        ts(r("SBE"), slot(0), col(4), None, A.min)
-        send("e", t)
-        permute("v", "SBX", 0, "XPHI", (14, 15), 14)
-        send("x", t)
-        permute("s", XN, 0, "XPHI", range(6))
-        permute("v", XN, 0, "XPHI", range(6, 14))
-        ts(r(EX, 0, 128), slot(0), col(4), col(2), A.min, A.mult)
-        if t == 1:
-            dma("y", ext(T.y[:, 0:CUT], "y", 0, CUT), r(XN, 0, CUT))
-        arrive("ae%d" % t, NE, "LE%d" % t, 0, 128)
-        ts(slot(0), r("LE%d" % t), col(3), None, A.mult)
-        tt(r(EX, 0, 128), slot(0), r(EX, 0, 128), A.add)
-        arrive("ax%d" % t, NX, XN, CUT, P)
+        tt(slot(1), slot(1), r("Q2"), A.is_lt)
+        tc(r("sb"), slot(2))
+        tt(slot(1), slot(1), r("nex"), A.add)
+        tt(r("sl"), slot(2), r("sb"), A.subtract)
+        for c in range(3):
+            rows("ST", 0, XW * c, r("sb"))
+            rows("ST", 1, XW * c, r("sl"))
+        tt(r("tA"), slot(1), r("SP"), A.mult)
+        tt(r("qq"), r("tA"), pVF, A.add)
+        ts(r("q16"), r("qq"), float(SWA), None, A.add)
+        for k in range(2):
+            for m in range(4 * k, 4 * k + 4):
+                gather("vs"[m // 2 % 2], r3("GR", m, m + 1, 0, 256), "SW", 0, SWA + P, "q16", 16 * m, 16 * m + 16)
+            mms(r("p4", 64 * k, 64 * k + 64), sums("F1", lambda i: r3("GR", 4 * k, 4 * k + 4, 16 * i, 16 * i + 16)))
+        for i in (14, 15):
+            ts(r("L16", 8 * i, 8 * i + 8), r("p4", i, 128, 16), -1.0, None, A.add)
+        gather("s", r("SG_", TAIL, TAIL + 256), "ST", 0, 3 * XW, "L16", 112, 128)
+        gather("v", r("SBX", 0, 256), X, 0, 3 * XW, "L16", 112, 128)
+        mms(r("p2", 0, EW), [(r("IDT", 0, 128), r("V1H", 0, EW))] +
+            sums("F1", lambda i: r("SG_", TAIL + 128 * (i - 14), TAIL + 128 * (i - 14) + EW), (14, 15)))
+        for m in range(8):
+            if m == 3:
+                ts(r("SBE", 0, EW), r("p2", 0, EW), float(P), None, A.min)
+                send(t)
+            ts(r("L16", m, 112, 8, tag="m%d" % m), r("p4", 16 * m, 16 * m + 14), -1.0, None, A.add)
+        for src, out in ((X, XN), ("ST", "SG_")):
+            gather("s", r(out, 16 * MAINV, CUT), src, 0, 3 * XW, "L16", MAINV, 112)
+            gather("v", r(out, 0, 16 * MAINV), src, 0, 3 * XW, "L16", 0, MAINV)
+            if t == 1 and src == X:
+                dma("y", ext(T.y[:, 0:CUT], "y", 0, CUT), r(XN, 0, CUT))
+        mms(r("p1", 0, EW), [(r("IDL", 0, 128), r("V1H", 0, EW))] + sums("F1", lambda i: r("SG_", 128 * i, 128 * i + EW), range(14)))
+        if t == 0:
+            walkers_start(1)
+        ts(slot(0, EW), r("p1", 0, EW), float(CUT), None, A.min)
+        arrive("ae%d" % t, NE, "LE%d" % t, 0, 136)
+        tt(r(EX, 0, EW), slot(0, EW), r("LE%d" % t, 0, EW), A.add)
+        arrive("ax%d" % t, NX, XN, CUT, XW)
 
-    def send(what, t):
-        if what == "x":
-            to, src, out, k, skip, rs, ls = rl[0], r("SBX"), T["RLX%d" % t][:], NX, 0, "rx%d" % t, "lx%d" % t
-        else:
-            to, src, out, k, skip, rs, ls = rl[1], r("SBE"), T["RLE%d" % t][:], NE, NX, "rn%d" % t, "le%d" % t
-        need("g", [src], [])
-        rid, pid = topo.addr(to, core)
-        g.remote_dma(out, src[0], T.sem[rs], T.sem[ls], pid, rid, pick(topo, core, to, k, skip))
-        count[ls] = k
+    def send(t):
+        parts = [(rl[1], T.SBE[:], T["RLE%d" % t][:], "rn%d" % t)]
+        parts += [(rl[0], T.SBX[:, EW * k:EW * k + EW], T["RLX%d" % t][:, EW * k:EW * k + EW], "rx%d" % t) for k in range(2)]
+        srcs, ls = [r("SBE"), r("SBX")], "lx%d" % t
+        need("g", srcs, [])
+        transfers = []
+        for k, (to, src, out, rs) in enumerate(parts):
+            rid, pid = topo.addr(to, core)
+            transfers.append(RemoteDMATransfer(dst_ids=[DstId(rid=rid, pnc=pid)], dma_engine_mask=pick(topo, core, to, NE, NE * k),
+                                               remote_sem=T.sem[rs], src=src, dst=out))
+        g.remote_dma_fused(transfers, local_sem=T.sem[ls])
+        count[ls] = 3 * NE
         clock = dict(known["g"])
-        clock[ls] = k
-        note("dma", [src], [], ls, k, clock)
+        clock[ls] = 3 * NE
+        note("dma", srcs, [], ls, 3 * NE, clock)
 
     def arrive(sem, k, name, lo, hi):
         count[sem] = k
         note("dma", [], [r(name, lo, hi)], sem, k, {sem: k})
 
+    tc(r("E0", 0, 128), r("EI"))
+    mm("p0", 0, 1, r("SHIFT"), r("E0", 0, 1))
+    walkers_start(0)
+    tc(r("E0", 128, 129), r("p0", 0, 1))
     for t in range(2):
-        if t:
-            table_start(t)
+        table_start(t)
+        table_rest(t)
+        if t == 0:
+            beside_first_walks()
+        else:
+            dma("y", r("SW", SWA, SWA + P, p=slice(0, 128, 8)), r("ZT", p=slice(0, 128, 8)))
         walks(t)
-        hist()
+        marks(t)
         grow(t)
     dma("y", ext(T.ye[:], "ye"), r("E2", 0, 128))
     dma("y", ext(T.y[:, CUT:P], "y", CUT, P), r("Y2", CUT, P))

@@ -7,46 +7,51 @@ P = 2048
 SC = 14
 VC = 64 - SC
 PIECES = ((0, 12), (12, 24), (24, VC))
-SG = 2
-EARLY = 12
-LAG = 16
-OW = 144
-XW = 2064
+SX = 6
+EARLY = (6, 2, 0, 5, 2, 2, 2)
+LAG = 15
+OW = 96
+XB = 2064
+XW = 2192
+EW = 136
+MW = 256 + EW
 CUT = 1792
 SWA = 4096
 SWW = SWA + 12288
 MAINV = 56
 TAIL = 1808
 
-BLK = ["VF", "V1", "Q2", "V1h", "QNh", "ZERO", "nhE", "thr", "hv", "KXh", "KX", "VFh", "HS", "mE", "ik", "cont", "ks", "ws", "Fl",
-       "PF", "NB", "NN", "SP", "nex", "tA", "tC", "tD", "qq", "HP", "LO", "ID", "TRI", "SHIFT", "SHR", "NSHR", "SHL", "RST",
-       "GRP", "SEL", "D2", "D1", "DH", "CV", "CS", "ONEF", "rowA", "rowB", "rowD"]
+BLK = ["VF", "V1", "Q2", "V1h", "QNh", "ZERO", "nhE", "thr", "hv", "KXh", "KX", "VFh", "Fl",
+       "PF", "NB", "NN", "SP", "nex", "tA", "tC", "tD", "qq", "HP", "LO", "SHIFT", "SHR", "SHL", "RST",
+       "GRP", "SEL", "D2", "D1", "IS", "IR", "N2I", "N2E", "N2S", "ONEF", "rowA", "rowD"]
 SCRATCH = {"BK": ("sbuf", [128, 128 * len(BLK)], "float32")}
-for n_ in ("E0", "E1", "E2", "RCH", "IC"):
+for n_ in ("E0", "E1", "E2"):
     SCRATCH[n_] = ("sbuf", [128, 136], "float32")
 for n_ in ("VI", "EI"):
     SCRATCH[n_] = ("sbuf", [128, 128], "int32")
 for n_ in ("B16", "EL16", "off16", "q16", "L16", "Z16"):
     SCRATCH[n_] = ("sbuf", [128, 128], "uint16")
-for n_ in ("IDB", "NIDB", "N2ID", "IDP", "IDN", "SHB", "kb", "kl", "bb", "bl", "sb", "sl", "nb", "nl", "Hb", "INV"):
+for n_ in ("IDB", "NIDB", "N2ID", "IDP", "IDN", "SHB", "kb", "kl", "bb", "bl", "sb", "sl", "nb", "nl", "Hb", "INV", "HS", "ik",
+           "cont", "ks", "ws", "TRI", "NSHR", "SELE"):
     SCRATCH[n_] = ("sbuf", [128, 128], "bfloat16")
-for n_ in ("F1", "FP", "FN", "FA", "FB", "ONEB", "hm"):
+for n_ in ("F1", "FP", "FN", "FA", "FB", "FT0", "FT1", "ONEB", "hm"):
     SCRATCH[n_] = ("sbuf", [128, 144], "bfloat16")
 for n_ in ("TI", "TV", "TS"):
     SCRATCH[n_] = ("sbuf", [128, 160], "bfloat16")
 for n_ in ("XPHI", "GH", "GK", "W", "KT", "HMR", "VD", "R0", "R1", "ZT"):
     SCRATCH[n_] = ("sbuf", [128, 2048], "bfloat16")
-for n_ in ("IDL", "IDT", "V1H", "SBE", "RLE0", "RLE1", "LE0", "LE1"):
+for n_ in ("Bh", "mE", "RCH", "SHR16", "rowA16", "rowB16"):
     SCRATCH[n_] = ("sbuf", [128, 136], "float16")
 SCRATCH.update({
     "X0": ("sbuf", [128, 3 * XW], "bfloat16"), "X1": ("sbuf", [128, 3 * XW], "bfloat16"), "ST": ("sbuf", [128, 3 * XW], "bfloat16"),
-    "XBS": ("sbuf", [128, XW], "bfloat16"), "MB": ("sbuf", [128, XW], "bfloat16"),
+    "XBS": ("sbuf", [128, XB], "bfloat16"), "MB": ("sbuf", [128, XB], "bfloat16"), "KR": ("sbuf", [128, 128 + EW], "bfloat16"),
     "SW": ("sbuf", [128, SWW], "bfloat16"), "SG_": ("sbuf", [128, 2080], "bfloat16"),
     "GR": ("sbuf", [128, 8, 256], "bfloat16"), "OH": ("sbuf", [128, 128 * OW], "bfloat16"),
+    "CV": ("sbuf", [128, 256], "float32"), "CS": ("sbuf", [128, 256], "float32"),
     "ST0": ("sbuf", [128, 256], "int32"), "CB": ("sbuf", [128, 320], "bfloat16"), "CX": ("sbuf", [128, 256], "bfloat16"),
     "cols": ("sbuf", [128, 32], "float32"), "coli": ("sbuf", [128, 8], "int32"),
     "MSK": ("sbuf", [128, 16], "float32"), "YR": ("sbuf", [128, 32], "float32"),
-    "SBX": ("sbuf", [128, 272], "bfloat16"), "RLX0": ("sbuf", [128, 272], "bfloat16"), "RLX1": ("sbuf", [128, 272], "bfloat16"),
+    "SBX": ("sbuf", [128, MW], "bfloat16"), "RL0": ("sbuf", [128, MW // 2], "bfloat16"), "RL1": ("sbuf", [128, MW // 2], "bfloat16"),
     "Y2": ("sbuf", [128, XW], "bfloat16"),
 })
 for n_ in (0, 1):
@@ -57,9 +62,8 @@ for n_ in (0, 1):
 for n_ in range(8):
     SCRATCH["p%d" % n_] = ("psum", [128, 512], "float32")
 SEMAPHORES = ["q_v", "q_s", "q_t", "q_g"] + ["d%d" % k for k in range(70)] + \
-    [a + b for a in ("rx", "rn", "lx", "le", "ax", "ae") for b in "01"]
-NX, NE = 8, 4
-EW = 136
+    [a + b for a in ("rx", "lx", "ax") for b in "01"]
+NX = 8
 
 
 def pick(topo, src, dst, k, skip=0):
@@ -77,19 +81,13 @@ def relay_program(g, core, T, topo):
         if core not in rl[:2]:
             continue
         rid, pid = topo.addr(dst, core)
-        if core == rl[0]:
-            for t in range(2):
-                g.wait_ge(T.sem["rx%d" % t], NX)
-                out = T.X1[:, CUT:XW] if t == 0 else T.Y2[:, CUT:XW]
-                g.remote_dma(out, T["RLX%d" % t][:], T.sem["ax%d" % t], T.sem["lx%d" % t], pid, rid, pick(topo, core, dst, NX))
-            for t in range(2):
-                g.wait_ge(T.sem["lx%d" % t], NX)
-        else:
-            for t in range(2):
-                g.wait_ge(T.sem["rn%d" % t], NE)
-                g.remote_dma(T["LE%d" % t][:], T["RLE%d" % t][:], T.sem["ae%d" % t], T.sem["le%d" % t], pid, rid, pick(topo, core, dst, NE))
-            for t in range(2):
-                g.wait_ge(T.sem["le%d" % t], NE)
+        lo = CUT + MW // 2 * rl.index(core)
+        for t in range(2):
+            g.wait_ge(T.sem["rx%d" % t], NX)
+            out = (T.X1 if t == 0 else T.Y2)[:, lo:lo + MW // 2]
+            g.remote_dma(out, T["RL%d" % t][:], T.sem["ax%d" % t], T.sem["lx%d" % t], pid, rid, pick(topo, core, dst, NX))
+        for t in range(2):
+            g.wait_ge(T.sem["lx%d" % t], NX)
 
 
 def rank_program(g, core, T, topo):
@@ -250,8 +248,11 @@ def rank_program(g, core, T, topo):
     dma("y", r("EI"), ext(T.ends[:], "ends"), True)
     dma("y", r("X0", 0, P), ext(T.x[:], "x"), True)
     dma("y", r("ST0"), ext(T.start[:], "start"), True)
-    for h in range(2):
+
+    def load_weapons(h):
         dma("y", r("W", 1024 * h, 1024 * h + 1024), ext(T.w[:, 1024 * h:1024 * h + 1024], "w"), True)
+
+    load_weapons(0)
 
     def iota(out, pat, base, cm, small=True):
         op("g", [], [out], [lambda: g.iota(out[0], pat, base, cm, allow_small_or_imprecise_dtypes=True) if small else g.iota(out[0], pat, base, cm)])
@@ -270,8 +271,8 @@ def rank_program(g, core, T, topo):
     fill(r("ZERO"), 0.0)
     fill(r("MB"), 0.0)
     fill(r("XBS", 0, 16), 0.0)
-    fill(r("XBS", P, XW), 0.0)
-    fill(r("X0", P, XW), 0.0)
+    fill(r("XBS", P, XB), 0.0)
+    fill(r("X0", P, XB), 0.0)
     iota(r("VI"), [[1, 128]], 0, 128, False)
     asel(r("SHIFT"), r("ONEF"), [[-1, 128]], A.is_equal, 0.0, -1, 1)
     asel(r("SHIFT"), r("SHIFT"), [[0, 8], [1, 16]], A.not_equal, 0.0, -15, 0)
@@ -304,35 +305,44 @@ def rank_program(g, core, T, topo):
             rows("SW", 4, SWA - P * c, r("CX", 128 * c - 128, 128 * c))
         for n in ("UP0", "UP1"):
             iota(r(n), [[0, 192]], 0, 0)
-        asel(r("SEL"), r("ZERO"), [[-8, 2], [-16, 8], [-1, 8]], A.not_equal, 1.0 / 128, 0, 1)
-        iota(r("TI"), [[1, 160]], -128, 0)
-        band("D2", [(-1, 1, 1.0), (-1, 0, -2.0), (-1, -1, 1.0), (1, 0, -1.0)])
-        band("D1", [(-1, 1, 1.0), (-1, 0, -1.0), (128, -127, -1.0)])
-        nv = 16 * (8 - SG)
-        band("DH", [(-1, 1, -1.0), (-1, 0, 2.0), (-1, -1, -1.0)], 0, nv)
-        band("DH", [(-1, -nv, 1.0), (-1, -nv - 1, -2.0), (-1, -nv - 2, 1.0)], nv, 128)
-        asel(r("DH", 15, nv, 16), r("DH", 15, nv, 16), [[-16, 8 - SG]], A.not_equal, 1.0, -15, 1)
-        asel(r("DH"), r("DH"), [[-16, 8], [0, 16]], A.is_ge, 0.0, 0, 1)
-        asel(r("DH"), r("DH"), [[16, 8], [0, 16]], A.is_ge, 0.0, 15, -1)
+        asel(r("SEL"), r("ZERO"), [[-8, 2], [-16, 8], [-1, 8]], A.not_equal, 1.0 / 64, 0, 1)
+        iota(r("TI", 0, 112), [[1, 112]], -64, 0)
+        band("D2", [(-1, 1, -1.0), (-1, 0, 2.0), (-1, -1, -1.0), (1, 0, 1.0)], 0, 64)
+        band("D1", [(-1, 1, 1.0), (-1, 0, -1.0), (64, -63, -1.0)], 0, 64)
         for n in ("CV", "CS"):
-            iota(r(n), [[0, 128]], 0, 0)
-        iota(r("IC"), [[1, EW]], 0, 0)
-        iota(r("RCH", 0, 4), [[0, 4]], 0, 0)
+            iota(r(n), [[0, 256]], 0, 0)
+        asel(r("RST"), r("ONEF"), [[0, 8], [1, 16]], A.not_equal, 0.0, 0, 0)
+        asel(r("SHR"), r("RST"), [[-1, 128]], A.is_equal, 0.0, 1, 1)
+        asel(r("IS"), r("SHIFT"), [[-1, 128]], A.not_equal, 1.0, 0, 1)
+        asel(r("IR"), r("SHR"), [[-1, 128]], A.not_equal, 1.0, 0, 1)
+        band("N2I", [(-1, 0, -2.0)])
+        band("N2E", [(-1, 0, -2.0)])
+        asel(r("N2E", 15, 128, 16), r("N2E", 15, 128, 16), [[-16, 8]], A.not_equal, -1.0, -15, 1)
+        band("N2S", [(-1, -1, -2.0)])
+        asel(r("N2S"), r("N2S"), [[0, 8], [1, 16]], A.not_equal, 0.0, -15, 0)
         iota(r("SG_", CUT, TAIL), [[0, 16]], 0, 0)
         iota(r("SG_", TAIL + 256, 2080), [[0, 16]], 0, 0)
-        iota(r("SBX", 256, 2 * EW), [[0, 16]], 0, 0)
         asel(r("GRP"), r("ONEF"), [[-16, 8], [0, 16]], A.is_ge, 0.0, 0, 1)
         asel(r("GRP"), r("GRP"), [[16, 8], [0, 16]], A.is_ge, 0.0, 15, -1)
         asel(r("TRI"), r("GRP"), [[1, 128]], A.is_ge, 0.0, -1, -1)
-        asel(r("RST"), r("ONEF"), [[0, 8], [1, 16]], A.not_equal, 0.0, 0, 0)
-        asel(r("SHR"), r("RST"), [[-1, 128]], A.is_equal, 0.0, 1, 1)
         asel(r("SHL"), r("RST"), [[1, 128]], A.is_equal, 0.0, -128, 1)
-        asel(r("ID"), r("ONEF"), [[-1, 128]], A.is_equal, 0.0, 0, 1)
+        asel(r("FA"), r("F1"), [[16, 9], [0, 16]], A.is_ge, 0.0, 1, -1)
+        asel(r("FB"), r("F1"), [[-16, 9], [0, 16]], A.is_ge, 0.0, -2, 1)
+        for b in range(2):
+            asel(r("FT%d" % b), r("F1"), [[-16, 9], [0, 16]], A.is_equal, 0.0, -14 - b, 1)
+        for gr in range(8):
+            asel(r("MSK"), r("MSK") if gr else r("ZERO", 0, 16), [[-1, 16]], A.not_equal, 1.0, -16 * gr, 1)
+        iota(r("KR", 0, 128), [[0, 8], [128, 16]], 0, 0)
+        iota(r("KR", 128, 128 + EW), [[1, EW]], 1, 0)
+        iota(r("SELE"), [[0, 128]], 0, 0)
+        for i in (14, 15):
+            for d, val in ((0, 1.0), (2, 0.5)):
+                asel(r("SELE", i, 128, 16), r("SELE", i, 128, 16), [[-16, 8]], A.not_equal, val, d - i, 1)
 
     def mark_tables():
-        ts(r("TV", 0, 128), r("TI", 0, 128), 1.0 / 128, None, A.mult)
-        tc(r("TV", 128, OW), r("TI", 129, OW + 1))
-        act(r("TS", 0, 128), r("TI", 0, 128), AF.Identity, 1.0 / 256, 1.0 / 128)
+        ts(r("TV", 0, 64), r("TI", 0, 64), 1.0 / 64, None, A.mult)
+        tc(r("TV", 64, OW), r("TI", 65, OW + 1))
+        act(r("TS", 0, 64), r("TI", 0, 64), AF.Identity, 1.0 / 128, 1.0 / 64)
 
     def growth_constants(part):
         if part:
@@ -347,44 +357,48 @@ def rank_program(g, core, T, topo):
         act(r("Q2"), r("VF"), AF.Identity, -10239.5)
         act(r("V1h"), r("VF"), AF.Identity, 0.5, 0.5)
         act(r("QNh"), r("VF"), AF.Identity, 4096.0, -0.5)
+        act(r("FB"), r("FB"), AF.Copy, scale=2.0)
+        act(col(3), r("VF", 0, 1), AF.Sign, -(CUT - 64.0))
+        act(col(4), col(3), AF.Identity, (CUT + P) / 2, (P - CUT) / 2)
         tc(pVF, r("VF"))
-        ts(col(0), r("VF", 0, 1), 1.0 / 128, None, A.mult)
+        tc(r("RCH", 0, 1), r("ZERO", 0, 1))
 
-    def late_constants():
-        ts(col(1), col(0), 2.0, None, A.is_lt)
-        ts(col(4), col(0), 2.0, 2.0, A.is_ge, A.mult)
-        ts(col(2), col(0), 14.0, None, A.is_lt)
-        ts(col(3), col(0), 14.0, None, A.is_ge)
-
-    def last_constants():
-        ts(r("V1H"), r("IC"), r("VF", 0, 1), 1.0, A.add, A.add)
-        ts(r("MSK"), r("IC", 0, 16), col(0), None, A.is_equal)
-        ts(r("FA"), r("F1"), col(1), None, A.mult)
-        ts(r("FB"), r("F1"), col(4), None, A.mult)
-        ts(r("IDL", 0, 128), r("ID"), col(2), None, A.mult)
-        ts(r("IDT", 0, 128), r("ID"), col(3), None, A.mult)
-
-    def table_start(t):
-        E = "E%d" % t
+    def table_start(E):
         tt(slot(2), r(E, 1, 129), r(E, 0, 128), A.is_lt)
         tt(slot(0), r(E, 0, 128), pV1, A.is_gt)
         tt(r("tC"), slot(2), r(E, 1, 129), A.mult)
         tt(slot(1), r("VF"), slot(0), A.add)
-        tt(slot(2), slot(1), r("tC"), A.max)
-        tc(r("B16"), slot(2))
-        tc(r("bb"), slot(2))
+        tt(r("Bh", 0, 128), slot(1), r("tC"), A.max)
 
-    def table_rest(t):
-        E = "E%d" % t
-        tt(r("bl"), slot(2), r("bb"), A.subtract)
-        rows("MB", 0, 1, r("bb"))
-        rows("MB", 1, 1, r("bl"))
-        g2("X%d" % t, XW, "B16", "XPHI")
+    def second_kids(X, n):
+        ts(r("B16"), r("Bh", 0, 128), 128.0 * n - 1, None, A.min)
+        if n == 16:
+            kid_rows()
+        g2(X, 128 * n, "B16", "XPHI")
         permute("s", "XBS", 1, "XPHI", range(6))
-        permute("v", "XBS", 1, "XPHI", range(6, 16))
-        tt(r("nhE"), slot(0), r(E, 0, 128), A.mult)
-        ts(r("thr"), slot(0), 1.0e6, None, A.mult)
-        ts(r("EL16"), r(E, 0, 128), -1.0, None, A.add)
+        permute("v", "XBS", 1, "XPHI", range(6, n))
+
+    def kid_rows():
+        tc(r("bb"), r("Bh", 0, 128))
+        rows("MB", 0, 1, r("bb"))
+        tt(r("bl"), r("Bh", 0, 128), r("bb"), A.subtract)
+        rows("MB", 1, 1, r("bl"))
+
+    def second_kids_arrived(X):
+        for b in range(2):
+            mms(r("p2", 8 * b, 8 * b + 8), sums("FT%d" % b, lambda i: r("Bh", i, 128, 16)))
+        kid_rows()
+        j_gather(0, 0, 1, 0, 32)
+        tc(r("L16", 112, 128), r("p2", 0, 16))
+        j_gather(0, 0, 1, 32, VC)
+        gather("v", r("XBS", CUT + 1, P + 1), X, 0, P, "L16", 112, 128)
+        tc(r("B16"), r("Bh", 0, 128))
+
+    def place_tables(t):
+        E = "E%d" % t
+        return [lambda: tt(r("nhE"), slot(0), r(E, 0, 128), A.mult),
+                lambda: ts(r("thr"), slot(0), 1.0e6, None, A.mult),
+                lambda: ts(r("EL16"), r(E, 0, 128), -1.0, None, A.add)]
 
     def walkers_start(t):
         for h in range(2):
@@ -414,18 +428,18 @@ def rank_program(g, core, T, topo):
 
     def j_gather(h, which, t, a=0, b=VC):
         win, base = ("X%d" % t, 0) if which == 0 else ("XBS", 1024)
-        tt(r("R%d" % h, base + 16 * a, base + 16 * b), ind(win, 0, XW, "Z16", 64 * h + a, 64 * h + b),
+        tt(r("R%d" % h, base + 16 * a, base + 16 * b), ind(win, 0, XB, "Z16", 64 * h + a, 64 * h + b),
            r("W", 1024 * h + 16 * a, 1024 * h + 16 * b), A.min)
 
     def s_gather(h, t):
         n = 16 * SC
-        for k, win in enumerate(("XBS", "X%d" % t)):
+        for k, win in ((1, "X%d" % t), (0, "XBS")):
             gs = r("GS%d" % h, n * k, n * k + n)
-            gather("s", gs, win, 0, XW, "Z16", 64 * h + VC, 64 * h + 64)
+            gather("s", gs, win, 0, XB, "Z16", 64 * h + VC, 64 * h + 64)
             mms(r("p%d" % (4 + h), n * k, n * k + n), [(r("IDB"), r("W", 1024 * h + 16 * VC, 1024 * h + 1024)), (r("NIDB"), gs)])
 
     def s_meta(h, step):
-        gather("s", r("MR%d" % h), "MB", 0, XW, "Z16", 64 * h, 64 * h + 64)
+        gather("s", r("MR%d" % h), "MB", 0, XB, "Z16", 64 * h, 64 * h + 64)
         shift = (r("IDB"), r("CB", 64 * step, 64 * step + 64)) if step < 5 else (r("IDN"), r("INV", 64 * h, 64 * h + 64))
         mms(r("p%d" % (2 + h), 0, 64), [shift] + sums("F1", walkers("MR%d" % h, 0, 64)))
 
@@ -459,30 +473,45 @@ def rank_program(g, core, T, topo):
     def split(h):
         a, b = 64 * h, 64 * h + 64
         pp = r("p%d" % h, 0, 64)
-        ts(r("Hb", a, b), pp, 129.0 - 63.5 / 128, 128.0, A.add, A.max)
-        ts(r("HP", a, b), r("Hb", a, b), -128.0, None, A.add)
-        tt(r("LO", a, b), pp, r("HP", a, b), A.subtract)
+        return [lambda: ts(r("Hb", a, b), pp, 129.0 - 31.5 / 64, 128.0, A.add, A.max),
+                lambda: ts(r("HP", a, b), r("Hb", a, b), -128.0, None, A.add),
+                lambda: tt(r("LO", a, b), pp, r("HP", a, b), A.subtract)]
 
     def spell(gr, h, i):
         j, c = 16 * gr + 8 * h + i, 64 * h + 8 * gr + i
         o = OW * j
-        if gr < 8 - SG:
+        if (gr, h, i) in mine:
             ts(r("OH", o, o + OW), r("TV", 0, OW), r("LO", c, c + 1), r("HP", c, c + 1), A.max, A.min)
         else:
-            act(r("OH", o, o + 128), r("TS", 0, 128), AF.Sign, r("LO", c, c + 1), -1.0)
-            act(r("OH", o + 128, o + OW), r("TI", 128, OW), AF.Relu, r("HP", c, c + 1), -1.0)
+            act(r("OH", o, o + 64), r("TS", 0, 64), AF.Sign, r("LO", c, c + 1), -1.0)
+            act(r("OH", o + 64, o + OW), r("TI", 64, OW), AF.Relu, r("HP", c, c + 1), -1.0)
 
-    def tally(gr, k):
-        o = OW * (16 * gr + k)
-        bank, c = ("p2", 16 * gr) if gr < 8 - SG else ("p4", 16 * (gr - 8 + SG))
-        mms(r(bank, c, c + 16), [(r("OH", o, o + 128), r("OH", o + 128, o + OW))], k == 0, k == 15)
+    def tally(c):
+        own = [d for d in (mine if c in mine else theirs) if d[0] == c[0]]
+        o = OW * (16 * c[0] + 8 * c[1] + c[2])
+        out = r("p2" if c in mine else "p4", 32 * c[0], 32 * c[0] + 32, p=p64)
+        mms(out, [(r("OH", o, o + 64), r("OH", o + 64, o + OW))], c == own[0], c == own[-1])
+
+    tiles = [(gr, h, i) for gr in range(8) for h in range(2) for i in range(8)]
+    theirs = [c for c in tiles if c[0] > 5 or (c[0] == 5 and 8 * c[1] + c[2] < SX)]
+    mine = [c for c in tiles if c not in theirs]
+    p64 = slice(0, 64)
+
+    def lo_differences(bank, C, D):
+        for b in range(2):
+            mm(bank, 64 * b, 64 * b + 64, r(C, b, 256, 2, p=p64), r(D, 0, 64, p=p64))
+
+    def hi_differences(Y, mats, first):
+        for b in range(2):
+            mms(r("p%d" % b, 0, 64), [(r(mats[b][k]), r(Y, 64 * k, 64 * k + 64)) for k in range(2)], first, not first)
 
     def walks(t):
         for s in range(12):
             h = s % 2
             s_gather(h, t)
             s_meta(h, s // 2)
-            j_gather(h, 0, t)
+            if s or not t:
+                j_gather(h, 0, t)
             if s:
                 for call, (a, b) in zip(decide(1 - h, (s - 1) // 2), PIECES):
                     call()
@@ -494,41 +523,43 @@ def rank_program(g, core, T, topo):
                 mark_tables()
 
     def marks(t):
-        NV = 8 - SG
-        split(0)
-        early = [(gr, 0, i) for gr in range(NV) for i in range(8)][:EARLY]
-        for c in early:
-            spell(*c)
-        for gr in range(NV, 8):
-            for i in range(8):
-                spell(gr, 0, i)
-        for call in decide(1, 5):
+        for call, other in zip(split(0), place_tables(t)):
             call()
-        split(1)
-        mine = [(gr, k // 8, k % 8) for gr in range(NV) for k in range(16)]
-        theirs = [(gr, k // 8, k % 8) for gr in range(NV, 8) for k in range(16)]
-        todo = [c for c in theirs if c[1] == 1]
+            other()
+        for c in theirs:
+            if c[1] == 0:
+                spell(*c)
+        first = [c for c in mine if c[1] == 0]
+        early = []
+        for n, call in zip(EARLY, decide(1, 5) + split(1) + [None]):
+            for c in first[len(early):len(early) + n]:
+                spell(*c)
+            early = first[:len(early) + n]
+            if call:
+                call()
         done = 0
         for n, c in enumerate(mine):
             if c not in early:
                 spell(*c)
-            tally(c[0], 8 * c[1] + c[2])
+            tally(c)
             while done < len(theirs) and done * (len(mine) - LAG) < (n + 1) * len(theirs):
                 d = theirs[done]
-                if d in todo:
+                if d[1] == 1:
                     spell(*d)
-                tally(d[0], 8 * d[1] + d[2])
+                tally(d)
                 done += 1
             if n == len(mine) - LAG - 1:
-                act(r("CS", 16 * NV, 128), r("p4", 0, 16 * SG), AF.Copy)
-            if n == len(mine) - LAG // 2:
-                mms(r("p3", 0, 128), [(r("CS"), r("D1"))], True, False)
-        tc(r("CV", 0, 16 * NV), r("p2", 0, 16 * NV))
-        mms(r("p3", 0, 128), [(r("CV"), r("D2"))], False, True)
+                act(r("CS", 160, 256, p=p64), r("p4", 160, 256, p=p64), AF.Copy)
+            if n == len(mine) - 2 * LAG // 3:
+                lo_differences("p5", "CS", "D1")
+                act(r("tC"), r("p5", 0, 128), AF.Copy)
+        tc(r("CV", 0, 192, p=p64), r("p2", 0, 192, p=p64))
+        hi_differences("tC", (("IS", "N2I"), ("N2S", "IS")), True)
+        lo_differences("p3", "CV", "D2")
         if t == 0:
             growth_constants(0)
         tc(r("tA"), r("p3", 0, 128))
-        mm("p0", 0, 128, r("DH"), r("tA"))
+        hi_differences("tA", (("N2I", "IR"), ("IS", "N2E")), False)
         if t == 0:
             growth_constants(1)
 
@@ -539,10 +570,11 @@ def rank_program(g, core, T, topo):
         X = "X%d" % t
         XN, EX = ("X1" if t == 0 else "Y2"), "E%d" % (t + 1)
         HM = r("hm", 0, 128)
-        tt(HM, r("p0", 0, 128), r("thr"), A.is_gt)
+        for b in range(2):
+            tt(r("hm", 64 * b, 64 * b + 64), r("p%d" % b, 0, 64), r("thr", 64 * b, 64 * b + 64), A.is_gt)
         rows("HMR", 0, 0, HM)
         mm("p5", 0, 1, r("SHB"), r("hm", 0, 1))
-        scan(r("HS"), HM, r("ZERO"), A.add, A.add)
+        scan(r("HS"), HM, r("ZT", 0, 128), A.add, A.add)
         mm("p4", 0, 1, r("TRI"), r("HS", 127, 128))
         tt(r("hv"), HM, pVB, A.mult)
         tc(r("hm", 128, 129), r("p5", 0, 1))
@@ -561,25 +593,24 @@ def rank_program(g, core, T, topo):
             mms(r("p2", 64 * k, 64 * k + 64), [(r("IDP"), r("hm", 64 * k + 1, 64 * k + 65))] + sums("FP", walkers("GH", 1024 * k, 64)))
         act(r(X, XW, XW + P), r(X, 0, P), AF.Relu, -1.0)
         if t == 0:
-            late_constants()
-        tt(r("mE"), r("p2", 0, 128), r("nhE"), A.min)
-        scan(r("RCH", 1, 129), r("mE"), r("ZERO"), A.max, A.add)
-        mm("p1", 0, 128, r("RCH", 128, 129), r("SHR"), p=p1)
-        if t == 0:
-            last_constants()
-        scan(row("rowA"), row("RST"), r("p1", 0, 128, p=p1), A.mult, A.max)
-        mm("p1", 200, 201, row("rowA"), r("ONEF", 0, 1, p=p1))
+            tc(r("SHR16", 0, 128), r("SHR"))
+        one16 = r("SHR16", 1, 2, p=p1)
+        tt(r("mE", 0, 128), r("p2", 0, 128), r("nhE"), A.min)
+        scan(r("RCH", 1, 129), r("mE", 0, 128), r("ZT", 0, 128), A.max, A.add)
+        mm("p1", 0, 128, r("RCH", 128, 129), r("SHR16", 0, 128), p=p1)
+        scan(r("rowA16", 0, 128, p=p1), row("RST"), r("p1", 0, 128, p=p1), A.mult, A.max)
+        mm("p1", 200, 201, r("rowA16", 0, 128, p=p1), one16)
         ts(slot(0, 129), r("RCH", 0, 129), r("p1", 200, 201), None, A.max)
         tt(r("ik"), r("p7", 1, 129), r("VFh"), A.is_gt)
         tt(r("cont"), slot(0), r("VF"), A.is_gt)
-        scan(r("ks"), r("ik"), r("ZERO"), A.add, A.add)
+        scan(r("ks"), r("ik"), r("ZT", 0, 128), A.add, A.add)
         scan(r("ws"), r("cont"), r("ik"), A.mult, A.add, 8192.0)
         mm("p4", 0, 1, r("TRI"), r("ks", 127, 128))
         mms(r("p5", 0, 128, p=p1), [(r("ks", 127, 128), r("TRI")), (r("ws", 127, 128), r("NSHR"))])
         tt(r("Fl"), r("ks"), r("ws"), A.subtract)
         ts(slot(0), r("ks"), r("p4", 0, 1), None, A.add)
-        scan(row("rowB"), row("RST"), r("p5", 0, 128, p=p1), A.mult, A.max)
-        mm("p5", 200, 201, row("rowB"), r("ONEF", 0, 1, p=p1))
+        scan(r("rowB16", 0, 128, p=p1), row("RST"), r("p5", 0, 128, p=p1), A.mult, A.max)
+        mm("p5", 200, 201, r("rowB16", 0, 128, p=p1), one16)
         tc(r("nb"), slot(0))
         tt(r("nl"), slot(0), r("nb"), A.subtract)
         rows("KT", 2, 0, r("nb"))
@@ -627,7 +658,7 @@ def rank_program(g, core, T, topo):
         tt(r("sl"), slot(2), r("sb"), A.subtract)
         for c in range(3):
             rows("ST", 0, XW * c, r("sb"))
-            rows("ST", 1, XW * c, r("sl"))
+            rows("ST", 2, XW * c, r("sl"))
         tt(r("tA"), slot(1), r("SP"), A.mult)
         tt(r("qq"), r("tA"), pVF, A.add)
         ts(r("q16"), r("qq"), float(SWA), None, A.add)
@@ -639,11 +670,11 @@ def rank_program(g, core, T, topo):
             ts(r("L16", 8 * i, 8 * i + 8), r("p4", i, 128, 16), -1.0, None, A.add)
         gather("s", r("SG_", TAIL, TAIL + 256), "ST", 0, 3 * XW, "L16", 112, 128)
         gather("v", r("SBX", 0, 256), X, 0, 3 * XW, "L16", 112, 128)
-        mms(r("p2", 0, EW), [(r("IDT", 0, 128), r("V1H", 0, EW))] +
-            sums("F1", lambda i: r("SG_", TAIL + 128 * (i - 14), TAIL + 128 * (i - 14) + EW), (14, 15)))
+        mms(r("p2", 0, EW), sums("FA", lambda i: r("SG_", TAIL + 128 * (i - 14), TAIL + 128 * (i - 14) + EW), (14, 15)) +
+            sums("FB", lambda i: r("SG_", TAIL + 128 * (i - 12), TAIL + 128 * (i - 12) + EW), (12, 13)))
         for m in range(8):
             if m == 3:
-                ts(r("SBE", 0, EW), r("p2", 0, EW), float(P), None, A.min)
+                tc(r("SBX", 256, MW), r("p2", 0, EW))
                 send(t)
             ts(r("L16", m, 112, 8, tag="m%d" % m), r("p4", 16 * m, 16 * m + 14), -1.0, None, A.add)
         for src, out in ((X, XN), ("ST", "SG_")):
@@ -651,29 +682,33 @@ def rank_program(g, core, T, topo):
             gather("v", r(out, 0, 16 * MAINV), src, 0, 3 * XW, "L16", 0, MAINV)
             if t == 1 and src == X:
                 dma("y", ext(T.y[:, 0:CUT], "y", 0, CUT), r(XN, 0, CUT))
-        mms(r("p1", 0, EW), [(r("IDL", 0, 128), r("V1H", 0, EW))] + sums("F1", lambda i: r("SG_", 128 * i, 128 * i + EW), range(14)))
+        ends = [(r("KR", 0, 128, p=p1), r("ONEB", 0, EW, p=p1)), (r("ONEB", 0, 128, p=p1), r("KR", 128, 128 + EW, p=p1))] + \
+            sums("F1", lambda i: r("SG_", 128 * i, 128 * i + EW), range(14))
         if t == 0:
+            mms(r("p3", 0, EW), ends)
             walkers_start(1)
-        ts(slot(0, EW), r("p1", 0, EW), float(CUT), None, A.min)
-        arrive("ae%d" % t, NE, "LE%d" % t, 0, 136)
-        tt(r(EX, 0, EW), slot(0, EW), r("LE%d" % t, 0, EW), A.add)
-        arrive("ax%d" % t, NX, XN, CUT, XW)
+            ts(r("E2", 0, EW), r("p3", 0, EW), float(CUT), None, A.min)
+            table_start("E2")
+            second_kids(XN, 14)
+        mms(r("p1", 0, EW), ends, True, False)
+        arrive("ax%d" % t, 2 * NX, XN, CUT, CUT + MW)
+        mms(r("p1", 0, EW), [(r("SELE"), r(XN, P, P + EW))], False, True)
+        ts(r(EX, 0, EW), r("p1", 0, EW), col(4), None, A.min)
 
     def send(t):
-        parts = [(rl[1], T.SBE[:], T["RLE%d" % t][:], "rn%d" % t)]
-        parts += [(rl[0], T.SBX[:, EW * k:EW * k + EW], T["RLX%d" % t][:, EW * k:EW * k + EW], "rx%d" % t) for k in range(2)]
-        srcs, ls = [r("SBE"), r("SBX")], "lx%d" % t
+        parts = [(rl[k], T.SBX[:, MW // 2 * k:MW // 2 * (k + 1)], T["RL%d" % t][:], "rx%d" % t) for k in range(2)]
+        srcs, ls = [r("SBX")], "lx%d" % t
         need("g", srcs, [])
         transfers = []
         for k, (to, src, out, rs) in enumerate(parts):
             rid, pid = topo.addr(to, core)
-            transfers.append(RemoteDMATransfer(dst_ids=[DstId(rid=rid, pnc=pid)], dma_engine_mask=pick(topo, core, to, NE, NE * k),
+            transfers.append(RemoteDMATransfer(dst_ids=[DstId(rid=rid, pnc=pid)], dma_engine_mask=pick(topo, core, to, NX, NX * k),
                                                remote_sem=T.sem[rs], src=src, dst=out))
         g.remote_dma_fused(transfers, local_sem=T.sem[ls])
-        count[ls] = 3 * NE
+        count[ls] = 2 * NX
         clock = dict(known["g"])
-        clock[ls] = 3 * NE
-        note("dma", srcs, [], ls, 3 * NE, clock)
+        clock[ls] = 2 * NX
+        note("dma", srcs, [], ls, 2 * NX, clock)
 
     def arrive(sem, k, name, lo, hi):
         count[sem] = k
@@ -684,11 +719,13 @@ def rank_program(g, core, T, topo):
     walkers_start(0)
     tc(r("E0", 128, 129), r("p0", 0, 1))
     for t in range(2):
-        table_start(t)
-        table_rest(t)
+        table_start("E%d" % t)
         if t == 0:
+            second_kids("X0", 16)
+            load_weapons(1)
             beside_first_walks()
         else:
+            second_kids_arrived("X1")
             dma("y", r("SW", SWA, SWA + P, p=slice(0, 128, 8)), r("ZT", p=slice(0, 128, 8)))
         walks(t)
         marks(t)

@@ -7,9 +7,11 @@ P = 2048
 SC = 14
 VC = 64 - SC
 PIECES = ((0, 12), (12, 24), (24, VC))
-SX = 6
-EARLY = (6, 2, 0, 5, 2, 2, 2)
-LAG = 15
+LAST_PIECES = ((0, 4), (4, 8), (8, 16), (16, 20), (20, 24), (24, VC))
+NS = 32
+LAG = 1
+PACE = 4
+EARLY = (10, 2, 0, 4, 2, 2, 2)
 OW = 96
 XB = 2064
 XW = 2192
@@ -19,11 +21,12 @@ CUT = 1792
 SWA = 4096
 SWW = SWA + 12288
 MAINV = 56
+STAYV = 24
 TAIL = 1808
 
 BLK = ["VF", "V1", "Q2", "V1h", "QNh", "ZERO", "nhE", "thr", "hv", "KXh", "KX", "VFh", "Fl",
-       "PF", "NB", "NN", "SP", "nex", "tA", "tC", "tD", "qq", "HP", "LO", "SHIFT", "SHR", "SHL", "RST",
-       "GRP", "SEL", "D2", "D1", "IS", "IR", "N2I", "N2E", "N2S", "ONEF", "rowA", "rowD"]
+       "NB", "NN", "SP", "nex", "tA", "tC", "tD", "qq", "SHIFT", "SHR", "SHL", "RST",
+       "GRP", "D2", "D1", "H00", "H01", "H10", "H11", "ONEF", "rowD"]
 SCRATCH = {"BK": ("sbuf", [128, 128 * len(BLK)], "float32")}
 for n_ in ("E0", "E1", "E2"):
     SCRATCH[n_] = ("sbuf", [128, 136], "float32")
@@ -32,7 +35,7 @@ for n_ in ("VI", "EI"):
 for n_ in ("B16", "EL16", "off16", "q16", "L16", "Z16"):
     SCRATCH[n_] = ("sbuf", [128, 128], "uint16")
 for n_ in ("IDB", "NIDB", "N2ID", "IDP", "IDN", "SHB", "kb", "kl", "bb", "bl", "sb", "sl", "nb", "nl", "Hb", "INV", "HS", "ik",
-           "cont", "ks", "ws", "TRI", "NSHR", "SELE"):
+           "cont", "ks", "ws", "TRI", "NSHR", "SELE", "SEL", "HP", "LO"):
     SCRATCH[n_] = ("sbuf", [128, 128], "bfloat16")
 for n_ in ("F1", "FP", "FN", "FA", "FB", "FT0", "FT1", "ONEB", "hm"):
     SCRATCH[n_] = ("sbuf", [128, 144], "bfloat16")
@@ -40,14 +43,16 @@ for n_ in ("TI", "TV", "TS"):
     SCRATCH[n_] = ("sbuf", [128, 160], "bfloat16")
 for n_ in ("XPHI", "GH", "GK", "W", "KT", "HMR", "VD", "R0", "R1", "ZT"):
     SCRATCH[n_] = ("sbuf", [128, 2048], "bfloat16")
-for n_ in ("Bh", "mE", "RCH", "SHR16", "rowA16", "rowB16"):
+for n_ in ("Bh", "PF", "mE", "RCH", "SHR16", "rowA16", "rowB16"):
     SCRATCH[n_] = ("sbuf", [128, 136], "float16")
 SCRATCH.update({
     "X0": ("sbuf", [128, 3 * XW], "bfloat16"), "X1": ("sbuf", [128, 3 * XW], "bfloat16"), "ST": ("sbuf", [128, 3 * XW], "bfloat16"),
     "XBS": ("sbuf", [128, XB], "bfloat16"), "MB": ("sbuf", [128, XB], "bfloat16"), "KR": ("sbuf", [128, 128 + EW], "bfloat16"),
     "SW": ("sbuf", [128, SWW], "bfloat16"), "SG_": ("sbuf", [128, 2080], "bfloat16"),
     "GR": ("sbuf", [128, 8, 256], "bfloat16"), "OH": ("sbuf", [128, 128 * OW], "bfloat16"),
-    "CV": ("sbuf", [128, 256], "float32"), "CS": ("sbuf", [128, 256], "float32"),
+    "CC": ("sbuf", [128, 384], "float32"),
+    "UP": ("sbuf", [128, 320], "float16"), "TB": ("sbuf", [128, 3072], "bfloat16"), "LT": ("sbuf", [128, 512], "bfloat16"),
+    "OS": ("sbuf", [128, 6144], "bfloat16"),
     "ST0": ("sbuf", [128, 256], "int32"), "CB": ("sbuf", [128, 320], "bfloat16"), "CX": ("sbuf", [128, 256], "bfloat16"),
     "cols": ("sbuf", [128, 32], "float32"), "coli": ("sbuf", [128, 8], "int32"),
     "MSK": ("sbuf", [128, 16], "float32"), "YR": ("sbuf", [128, 32], "float32"),
@@ -58,7 +63,6 @@ for n_ in (0, 1):
     SCRATCH["MR%d" % n_] = ("sbuf", [128, 1024], "bfloat16")
     SCRATCH["GS%d" % n_] = ("sbuf", [128, 32 * SC], "bfloat16")
     SCRATCH["U%d" % n_] = ("sbuf", [128, 128], "float32")
-    SCRATCH["UP%d" % n_] = ("sbuf", [128, 192], "float32")
 for n_ in range(8):
     SCRATCH["p%d" % n_] = ("psum", [128, 512], "float32")
 SEMAPHORES = ["q_v", "q_s", "q_t", "q_g"] + ["d%d" % k for k in range(70)] + \
@@ -243,7 +247,8 @@ def rank_program(g, core, T, topo):
         return r("p7", 128 * k, 128 * k + n)
 
     pVF, pV1, pVB = [r("p6", 128 * k, 128 * k + 128) for k in range(3)]
-    p1 = slice(0, 1)
+    halves = (slice(0, 64), slice(64, 128))
+    p1, p32, p33, row32 = slice(0, 1), slice(0, 32), slice(0, 33), slice(32, 33)
 
     dma("y", r("EI"), ext(T.ends[:], "ends"), True)
     dma("y", r("X0", 0, P), ext(T.x[:], "x"), True)
@@ -260,34 +265,35 @@ def rank_program(g, core, T, topo):
     def asel(out, in_, pat, cmp, fl, base, cm):
         op("g", [in_], [out], [lambda: g.affine_select(out[0], in_[0], pat, cmp, fl, base, cm)])
 
-    def band(name, entries, lo=0, hi=128):
-        src = r("ZERO", lo, hi)
+    def band(name, entries, lo=0, hi=128, p=None):
+        src = r("ZERO", lo, hi, p=p)
         for a, b, val in entries:
-            asel(r(name, lo, hi), src, [[a, hi - lo]], A.not_equal, val, b, 1)
-            src = r(name, lo, hi)
+            asel(r(name, lo, hi, p=p), src, [[a, hi - lo]], A.not_equal, val, b, 1)
+            src = r(name, lo, hi, p=p)
 
     fill(r("ONEF"), 1.0)
     fill(r("ONEB"), 1.0)
     fill(r("ZERO"), 0.0)
-    fill(r("MB"), 0.0)
-    fill(r("XBS", 0, 16), 0.0)
-    fill(r("XBS", P, XB), 0.0)
-    fill(r("X0", P, XB), 0.0)
     iota(r("VI"), [[1, 128]], 0, 128, False)
     asel(r("SHIFT"), r("ONEF"), [[-1, 128]], A.is_equal, 0.0, -1, 1)
     asel(r("SHIFT"), r("SHIFT"), [[0, 8], [1, 16]], A.not_equal, 0.0, -15, 0)
+    iota(r("TI", 0, 112), [[1, 112]], -64, 0)
     asel(r("IDB"), r("ONEB", 0, 128), [[-1, 128]], A.is_equal, 0.0, 0, 1)
     asel(r("F1"), r("ONEB"), [[-16, 9], [0, 16]], A.is_ge, 0.0, 0, 1)
     asel(r("F1"), r("F1"), [[16, 9], [0, 16]], A.is_ge, 0.0, 15, -1)
     asel(r("F1"), r("F1"), [[0, 9], [1, 16]], A.is_equal, 0.0, -15, 0)
     iota(r("CB"), [[-1, 5], [0, 64]], 5, 0)
+    fill(r("XBS", 0, 16), 0.0)
     ts(r("VI"), r("VI"), 2047, None, A.bitwise_and)
+    fill(r("XBS", P, XB), 0.0)
     tc(r("VF"), r("VI"))
     ts(pV1, r("VI"), 1.0, None, A.add)
+    fill(r("MB"), 0.0)
     act(r("NIDB"), r("IDB"), AF.Copy, scale=-1.0)
     act(r("FP"), r("F1"), AF.Copy, scale=4096.0)
     act(r("FN"), r("F1"), AF.Copy, scale=-4096.0)
     act(r("IDN"), r("IDB"), AF.Copy, scale=-4096.0)
+    fill(r("X0", P, XB), 0.0)
 
     def beside_first_walks():
         iota(r("ZT"), [[0, 2048]], 0, 0)
@@ -296,30 +302,34 @@ def rank_program(g, core, T, topo):
         for c in range(3):
             dma("y", r("ST", XW * c, XW * c + P), r("ZT"))
             dma("y", r("SW", P * c, P * c + P), r("ZT"))
-        iota(r("OH", 0, 2048), [[0, 128], [128, 16]], 0, 0)
-        iota(r("OH", 2048, 4096), [[1, 128], [0, 16]], 1, 0)
-        dma("y", (T.VD[0:128:16, :], "VD", 0, 2048, "a"), r("OH", 0, 2048, p=slice(0, 128, 16)))
-        dma("y", (T.VD[8:128:16, :], "VD", 0, 2048, "b"), r("OH", 2048, 4096, p=slice(0, 128, 16)))
+        asel(r("SEL"), r("ZT", 0, 128), [[-8, 2], [-16, 8], [-1, 8]], A.not_equal, 1.0 / 64, 0, 1)
+        asel(r("TB", 0, 2048, p=p32), r("ZT", p=p32), [[-1, 32], [0, 64]], A.not_equal, 128.0, 0, 1)
+        asel(r("TB", 2048, 3072, p=p32), r("ZT", 0, 1024, p=p32), [[-1, 32], [0, 32]], A.not_equal, 1.0, 0, 1)
+        iota(r("TS", 0, 64, p=p32), [[-2, 64]], 127, 0)
+        iota(r("TS", 64, 96, p=p32), [[-1, 32]], 0, 0)
+        dma("y", r("TB", 0, 2048, p=row32, tag="r32"), r("TS", 0, 64, p=p32))
+        dma("y", r("TB", 2048, 3072, p=row32, tag="r32"), r("TS", 64, 96, p=p32))
+        iota(r("LT"), [[0, 512]], 1, 0)
+        iota(r("OH", 0, 2048), [[1, 128], [0, 16]], 1, 0)
+        dma("y", (T.VD[8:128:16, :], "VD", 0, 2048, "row8"), r("OH", 0, 2048, p=slice(0, 128, 16)))
+        iota(r("KR", 0, 128), [[0, 8], [128, 16]], 0, 0)
+        rows("VD", 0, 0, r("KR", 0, 128))
         iota(r("CX"), [[XW, 2], [0, 128]], XW, 0)
         for c in (1, 2):
             rows("SW", 4, SWA - P * c, r("CX", 128 * c - 128, 128 * c))
-        for n in ("UP0", "UP1"):
-            iota(r(n), [[0, 192]], 0, 0)
-        asel(r("SEL"), r("ZERO"), [[-8, 2], [-16, 8], [-1, 8]], A.not_equal, 1.0 / 64, 0, 1)
-        iota(r("TI", 0, 112), [[1, 112]], -64, 0)
         band("D2", [(-1, 1, -1.0), (-1, 0, 2.0), (-1, -1, -1.0), (1, 0, 1.0)], 0, 64)
         band("D1", [(-1, 1, 1.0), (-1, 0, -1.0), (64, -63, -1.0)], 0, 64)
-        for n in ("CV", "CS"):
-            iota(r(n), [[0, 256]], 0, 0)
+        for n in ("D2", "D1"):
+            dma("y", r(n, 0, 64, p=halves[1]), r(n, 0, 64, p=halves[0]))
+        iota(r("CC", 128, 256), [[0, 128]], 0, 0)
         asel(r("RST"), r("ONEF"), [[0, 8], [1, 16]], A.not_equal, 0.0, 0, 0)
         asel(r("SHR"), r("RST"), [[-1, 128]], A.is_equal, 0.0, 1, 1)
-        asel(r("IS"), r("SHIFT"), [[-1, 128]], A.not_equal, 1.0, 0, 1)
-        asel(r("IR"), r("SHR"), [[-1, 128]], A.not_equal, 1.0, 0, 1)
-        band("N2I", [(-1, 0, -2.0)])
-        band("N2E", [(-1, 0, -2.0)])
-        asel(r("N2E", 15, 128, 16), r("N2E", 15, 128, 16), [[-16, 8]], A.not_equal, -1.0, -15, 1)
-        band("N2S", [(-1, -1, -2.0)])
-        asel(r("N2S"), r("N2S"), [[0, 8], [1, 16]], A.not_equal, 0.0, -15, 0)
+        for n, lo, src, val in (("H00", 0, "SHIFT", 1.0), ("H00", 64, "ZERO", -2.0), ("H10", 0, "ZERO", -2.0), ("H10", 64, "SHR", 1.0),
+                                ("H01", 64, "SHIFT", 1.0), ("H11", 0, "SHIFT", 1.0), ("H11", 64, "ZERO", -2.0)):
+            asel(r(n, lo, lo + 64), r(src, lo, lo + 64), [[-1, 64]], A.not_equal, val, -lo, 1)
+        asel(r("H11", 79, 128, 16), r("H11", 79, 128, 16), [[-16, 4]], A.not_equal, -1.0, -79, 1)
+        band("H01", [(-1, -1, -2.0)], 0, 64)
+        asel(r("H01", 0, 64), r("H01", 0, 64), [[0, 4], [1, 16]], A.not_equal, 0.0, -15, 0)
         iota(r("SG_", CUT, TAIL), [[0, 16]], 0, 0)
         iota(r("SG_", TAIL + 256, 2080), [[0, 16]], 0, 0)
         asel(r("GRP"), r("ONEF"), [[-16, 8], [0, 16]], A.is_ge, 0.0, 0, 1)
@@ -332,7 +342,6 @@ def rank_program(g, core, T, topo):
             asel(r("FT%d" % b), r("F1"), [[-16, 9], [0, 16]], A.is_equal, 0.0, -14 - b, 1)
         for gr in range(8):
             asel(r("MSK"), r("MSK") if gr else r("ZERO", 0, 16), [[-1, 16]], A.not_equal, 1.0, -16 * gr, 1)
-        iota(r("KR", 0, 128), [[0, 8], [128, 16]], 0, 0)
         iota(r("KR", 128, 128 + EW), [[1, EW]], 1, 0)
         iota(r("SELE"), [[0, 128]], 0, 0)
         for i in (14, 15):
@@ -340,13 +349,13 @@ def rank_program(g, core, T, topo):
                 asel(r("SELE", i, 128, 16), r("SELE", i, 128, 16), [[-16, 8]], A.not_equal, val, d - i, 1)
 
     def mark_tables():
-        ts(r("TV", 0, 64), r("TI", 0, 64), 1.0 / 64, None, A.mult)
-        tc(r("TV", 64, OW), r("TI", 65, OW + 1))
-        act(r("TS", 0, 64), r("TI", 0, 64), AF.Identity, 1.0 / 128, 1.0 / 64)
+        act(r("TV", 0, 64), r("TI", 0, 64), AF.Copy, scale=1.0 / 64)
+        act(r("TV", 64, OW), r("TI", 65, OW + 1), AF.Copy)
 
     def growth_constants(part):
         if part:
             tc(r("SHB"), r("SHIFT"))
+            tc(r("RCH", 0, 1), r("ZERO", 0, 1))
             ts(pVB, r("VF"), 6145.0, None, A.add)
             return
         act(r("IDP"), r("IDB"), AF.Copy, scale=4096.0)
@@ -361,14 +370,18 @@ def rank_program(g, core, T, topo):
         act(col(3), r("VF", 0, 1), AF.Sign, -(CUT - 64.0))
         act(col(4), col(3), AF.Identity, (CUT + P) / 2, (P - CUT) / 2)
         tc(pVF, r("VF"))
-        tc(r("RCH", 0, 1), r("ZERO", 0, 1))
+        tc(r("SHR16", 0, 128), r("SHR"))
 
-    def table_start(E):
+    def table_start(E, between=()):
+        other = list(between) + [lambda: None] * 3
+        other[0]()
         tt(slot(2), r(E, 1, 129), r(E, 0, 128), A.is_lt)
         tt(slot(0), r(E, 0, 128), pV1, A.is_gt)
         tt(r("tC"), slot(2), r(E, 1, 129), A.mult)
         tt(slot(1), r("VF"), slot(0), A.add)
+        other[1]()
         tt(r("Bh", 0, 128), slot(1), r("tC"), A.max)
+        other[2]()
 
     def second_kids(X, n):
         ts(r("B16"), r("Bh", 0, 128), 128.0 * n - 1, None, A.min)
@@ -390,7 +403,7 @@ def rank_program(g, core, T, topo):
         kid_rows()
         j_gather(0, 0, 1, 0, 32)
         tc(r("L16", 112, 128), r("p2", 0, 16))
-        j_gather(0, 0, 1, 32, VC)
+        j_gather(0, 0, 1, 32, 64)
         gather("v", r("XBS", CUT + 1, P + 1), X, 0, P, "L16", 112, 128)
         tc(r("B16"), r("Bh", 0, 128))
 
@@ -401,10 +414,8 @@ def rank_program(g, core, T, topo):
                 lambda: ts(r("EL16"), r(E, 0, 128), -1.0, None, A.add)]
 
     def walkers_start(t):
-        for h in range(2):
-            a = 128 * t + 64 * h
-            ts(r("Z16", 64 * h, 64 * h + 64), r("ST0", a, a + 64), 1.0, None, A.add)
-            ts(r("U%d" % h, 0, 64), r("ST0", a, a + 64), 6.0, None, A.add)
+        return [lambda: ts(r("Z16"), r("ST0", 128 * t, 128 * t + 128), 1.0, None, A.add)] + \
+            [lambda h=h: ts(r("U%d" % h, 0, 64), r("ST0", 128 * t + 64 * h, 128 * t + 64 * h + 64), 6.0, None, A.add) for h in range(2)]
 
     def permute(eng, dst_, off, src, blocks):
         for i in blocks:
@@ -441,19 +452,20 @@ def rank_program(g, core, T, topo):
     def s_meta(h, step):
         gather("s", r("MR%d" % h), "MB", 0, XB, "Z16", 64 * h, 64 * h + 64)
         shift = (r("IDB"), r("CB", 64 * step, 64 * step + 64)) if step < 5 else (r("IDN"), r("INV", 64 * h, 64 * h + 64))
-        mms(r("p%d" % (2 + h), 0, 64), [shift] + sums("F1", walkers("MR%d" % h, 0, 64)))
+        return lambda: mms(r("p%d" % (2 + h), 0, 64), [shift] + sums("F1", walkers("MR%d" % h, 0, 64)))
 
-    def s_relu(h):
+    def s_relu(h, alone):
         n = 16 * SC
-        for k in range(2):
+        for k in range(0 if alone else 2):
             act(r("R%d" % h, 1024 * k + 16 * VC, 1024 * k + 1024), r("p%d" % (4 + h), n * k, n * k + n), AF.Relu)
-        mms(r("p%d" % h, 0, 64), sums("FP", walkers("R%d" % h, 0, 64)) + sums("FN", walkers("R%d" % h, 1024, 64)))
+        return [lambda: mms(r("p%d" % h, 0, 64), sums("FP", walkers("R%d" % h, 0, 64)), True, False),
+                lambda: mms(r("p%d" % h, 0, 64), sums("FN", walkers("R%d" % h, 1024, 64)), False, True)]
 
     def decide(h, step):
         z0 = 64 * (step % 2)
         u = "U%d" % h
         a, b = 64 * h, 64 * h + 64
-        old, new = r(u, z0, z0 + 64), (r(u, 64 - z0, 128 - z0) if step < 5 else r("UP%d" % h, 64, 128))
+        old, new = r(u, z0, z0 + 64), (r(u, 64 - z0, 128 - z0) if step < 5 else r("UP", 128 * h + 64, 128 * h + 128))
 
         def last():
             if step < 5:
@@ -468,7 +480,8 @@ def rank_program(g, core, T, topo):
     def turn(h):
         a, b = 64 * h, 64 * h + 64
         pp = r("p%d" % h, 0, 64)
-        mms(pp, [(r("UP%d" % h, 64, 192), r("SEL", 0, 64)), (r("UP%d" % h, 0, 128), r("SEL", 64, 128))])
+        tc_ = 128 * h + 64
+        mms(pp, [(r("UP", tc_, tc_ + 128), r("SEL", 0, 64)), (r("UP", tc_ - 64, tc_ + 64), r("SEL", 64, 128))])
 
     def split(h):
         a, b = 64 * h, 64 * h + 64
@@ -480,86 +493,109 @@ def rank_program(g, core, T, topo):
     def spell(gr, h, i):
         j, c = 16 * gr + 8 * h + i, 64 * h + 8 * gr + i
         o = OW * j
-        if (gr, h, i) in mine:
-            ts(r("OH", o, o + OW), r("TV", 0, OW), r("LO", c, c + 1), r("HP", c, c + 1), A.max, A.min)
-        else:
-            act(r("OH", o, o + 64), r("TS", 0, 64), AF.Sign, r("LO", c, c + 1), -1.0)
-            act(r("OH", o + 64, o + OW), r("TI", 64, OW), AF.Relu, r("HP", c, c + 1), -1.0)
+        ts(r("OH", o, o + OW), r("TV", 0, OW), r("LO", c, c + 1), r("HP", c, c + 1), A.max, A.min)
 
     def tally(c):
-        own = [d for d in (mine if c in mine else theirs) if d[0] == c[0]]
-        o = OW * (16 * c[0] + 8 * c[1] + c[2])
-        out = r("p2" if c in mine else "p4", 32 * c[0], 32 * c[0] + 32, p=p64)
-        mms(out, [(r("OH", o, o + 64), r("OH", o + 64, o + OW))], c == own[0], c == own[-1])
+        own = [d for d in (mine if c in mine else theirs) if d[:2] == c[:2]]
+        if c in mine:
+            o = OW * (16 * c[0] + 8 * c[1] + c[2])
+            pair, bank, to = (r("OH", o, o + 64), r("OH", o + 64, o + OW)), "p2", 32 * (c[0] - 4)
+        else:
+            k, o = 8 * c[0] + c[2], 3072 * c[1]
+            pair = (r("OS", o + 64 * k, o + 64 * k + 64), r("OS", o + 2048 + 32 * k, o + 2048 + 32 * k + 32))
+            bank, to = "p4", 32 * c[0]
+        mms(r(bank, to, to + 32, p=halves[c[1]]), [pair], c == own[0], c == own[-1])
 
     tiles = [(gr, h, i) for gr in range(8) for h in range(2) for i in range(8)]
-    theirs = [c for c in tiles if c[0] > 5 or (c[0] == 5 and 8 * c[1] + c[2] < SX)]
+    theirs = [c for c in tiles if 8 * c[0] + c[2] < NS]
     mine = [c for c in tiles if c not in theirs]
-    p64 = slice(0, 64)
 
-    def lo_differences(bank, C, D):
-        for b in range(2):
-            mm(bank, 64 * b, 64 * b + 64, r(C, b, 256, 2, p=p64), r(D, 0, 64, p=p64))
+    def turn_back(h):
+        for k, n in enumerate(("LO", "HP")):
+            mm("p%d" % h, 64 + 128 * k, 192 + 128 * k, r(n, 64 * h, 64 * h + 32), r("IDB"), p=p32)
+        act(r("LT", 256 * h, 256 * h + 256, p=p32), r("p%d" % h, 64, 320, p=p32), AF.Copy)
 
-    def hi_differences(Y, mats, first):
-        for b in range(2):
-            mms(r("p%d" % b, 0, 64), [(r(mats[b][k]), r(Y, 64 * k, 64 * k + 64)) for k in range(2)], first, not first)
+    blocks = [(0, a, min(a + 8, NS)) for a in range(0, NS, 8)]
+    for a in range(0, NS, 16):
+        blocks.insert(blocks.index((0, a, min(a + 8, NS))), (1, a, min(a + 16, NS)))
+    nblock = [0]
+
+    def block(h, kind, a, b):
+        w, o = (64, 0) if kind == 0 else (32, 2048)
+        bank = r(("p5", "p0", "p3")[nblock[0] % 3], 0, w * (b - a))
+        nblock[0] += 1
+        mms(bank, [(r("LT", 256 * h + 128 * kind, 256 * h + 128 * kind + 128, p=p33), r("TB", o + w * a, o + w * b, p=p33))])
+        act(r("OS", 3072 * h + o + w * a, 3072 * h + o + w * b), bank, AF.Relu if kind else AF.Sign)
 
     def walks(t):
         for s in range(12):
             h = s % 2
-            s_gather(h, t)
-            s_meta(h, s // 2)
+            alone = t and not s
+            if not alone:
+                s_gather(h, t)
+            sum_meta = s_meta(h, s // 2)
+            if s < 11:
+                sum_meta()
             if s or not t:
                 j_gather(h, 0, t)
             if s:
-                for call, (a, b) in zip(decide(1 - h, (s - 1) // 2), PIECES):
+                calls = decide(1 - h, (s - 1) // 2) + (split(0) if s == 11 else [])
+                for call, (a, b) in zip(calls, PIECES if s < 11 else LAST_PIECES):
                     call()
                     j_gather(h, 1, t, a, b)
             else:
-                j_gather(h, 1, t)
-            s_relu(h)
-            if s == 8 and t == 0:
-                mark_tables()
+                j_gather(h, 1, t, 0, 64 if alone else VC)
+            if s == 11:
+                sum_meta()
+            sum_first, sum_second = s_relu(h, alone)
+            if s == 11:
+                turn_back(0)
+            sum_first()
+            if s == 11:
+                nblock[0] = 0
+                block(0, *blocks[0])
+                block(0, *blocks[1])
+            sum_second()
 
     def marks(t):
-        for call, other in zip(split(0), place_tables(t)):
-            call()
-            other()
-        for c in theirs:
-            if c[1] == 0:
+        steps, due = [], [[], []]
+        for h in range(2):
+            for b in blocks:
+                steps.append(lambda h=h, b=b, now=due.pop(0): [block(h, *b)] + [tally(c) for c in now])
+                due.append([c for c in theirs if c[1] == h and b[1] <= 8 * c[0] < b[2]] if b[0] == 0 else [])
+        steps = steps[2:]
+        steps.insert(3, lambda: turn_back(1))
+        steps.append(lambda: [tally(c) for c in due[0]])
+        steps.append(lambda: [tally(c) for c in due[1]] + [act(r("CC", 0, 128), r("p4", 0, 128), AF.Copy)])
+        order = sorted(mine, key=lambda c: c[1])
+        done = 0
+        for k, (n, call) in enumerate(zip(EARLY, decide(1, 5) + split(1) + [None])):
+            for c in order[done:done + n]:
                 spell(*c)
-        first = [c for c in mine if c[1] == 0]
-        early = []
-        for n, call in zip(EARLY, decide(1, 5) + split(1) + [None]):
-            for c in first[len(early):len(early) + n]:
-                spell(*c)
-            early = first[:len(early) + n]
             if call:
                 call()
-        done = 0
-        for n, c in enumerate(mine):
-            if c not in early:
-                spell(*c)
+            for c in order[done:done + n]:
+                tally(c)
+            done += n
+            if k in (2, 3, 4, 5):
+                steps.pop(0)()
+        for n, c in enumerate(order[done:]):
+            spell(*c)
+            if n % PACE == 0 and len(steps) > LAG:
+                steps.pop(0)()
             tally(c)
-            while done < len(theirs) and done * (len(mine) - LAG) < (n + 1) * len(theirs):
-                d = theirs[done]
-                if d[1] == 1:
-                    spell(*d)
-                tally(d)
-                done += 1
-            if n == len(mine) - LAG - 1:
-                act(r("CS", 160, 256, p=p64), r("p4", 160, 256, p=p64), AF.Copy)
-            if n == len(mine) - 2 * LAG // 3:
-                lo_differences("p5", "CS", "D1")
-                act(r("tC"), r("p5", 0, 128), AF.Copy)
-        tc(r("CV", 0, 192, p=p64), r("p2", 0, 192, p=p64))
-        hi_differences("tC", (("IS", "N2I"), ("N2S", "IS")), True)
-        lo_differences("p3", "CV", "D2")
+        for call in place_tables(t):
+            call()
+        tc(r("CC", 256, 384), r("p2", 0, 128))
+        while steps:
+            steps.pop(0)()
+        for b in range(2):
+            mms(r("p3", 64 * b, 64 * b + 64), [(r("CC", 128 + b, 384, 2), r("D2", 0, 64)), (r("CC", b, 256, 2), r("D1", 0, 64))])
         if t == 0:
             growth_constants(0)
         tc(r("tA"), r("p3", 0, 128))
-        hi_differences("tA", (("N2I", "IR"), ("IS", "N2E")), False)
+        for b in range(2):
+            mms(r("p%d" % b, 0, 64), [(r("H%d%d" % (k, b)), r("tA", 64 * k, 64 * k + 64)) for k in range(2)])
         if t == 0:
             growth_constants(1)
 
@@ -582,18 +618,16 @@ def rank_program(g, core, T, topo):
         tt(r("VFh"), r("hv"), pVF, A.max)
         tt(slot(0), r("V1"), slot(1), A.subtract)
         tc(r("kb"), slot(0))
-        tt(r("KX"), slot(0), r("hv"), A.max)
-        tt(r("kl"), slot(0), r("kb"), A.subtract)
         rows("KT", 0, 0, r("kb"))
-        rows("KT", 1, 0, r("kl"))
-        ts(r("KXh"), r("KX"), 0.5, None, A.mult)
         for k in range(2):
             for eng, a in (("v", 64 * k), ("s", 64 * k + 32)):
                 gather(eng, r("GH", 16 * a, 16 * a + 512), "HMR", 0, P, "B16", a, a + 32)
             mms(r("p2", 64 * k, 64 * k + 64), [(r("IDP"), r("hm", 64 * k + 1, 64 * k + 65))] + sums("FP", walkers("GH", 1024 * k, 64)))
         act(r(X, XW, XW + P), r(X, 0, P), AF.Relu, -1.0)
-        if t == 0:
-            tc(r("SHR16", 0, 128), r("SHR"))
+        tt(r("KX"), slot(0), r("hv"), A.max)
+        tt(r("kl"), slot(0), r("kb"), A.subtract)
+        rows("KT", 1, 0, r("kl"))
+        ts(r("KXh"), r("KX"), 0.5, None, A.mult)
         one16 = r("SHR16", 1, 2, p=p1)
         tt(r("mE", 0, 128), r("p2", 0, 128), r("nhE"), A.min)
         scan(r("RCH", 1, 129), r("mE", 0, 128), r("ZT", 0, 128), A.max, A.add)
@@ -636,19 +670,19 @@ def rank_program(g, core, T, topo):
         reduce_(col(8), r("tA"), A.min)
         ts(r("YR", 0, 16), r("MSK"), col(8), -(4096.5 / 16), A.mult, A.add)
         mm("p4", 0, 17, r("GRP"), r("YR", 0, 17))
-        scan(r("PF"), r("p0", 0, 128), r("V1h"), A.max, A.min)
         scan(rev("NB"), rev("p0"), rev("QNh"), A.max, A.min)
-        mm("p3", 0, 128, r("PF", 127, 128), r("SHR"), p=p1)
         mm("p5", 0, 128, r("NB", 0, 1), r("SHL"), p=p1)
+        scan(r("PF", 0, 128), r("p0", 0, 128), r("V1h"), A.max, A.min)
+        mm("p3", 0, 128, r("PF", 127, 128), r("SHR16", 0, 128), p=p1)
         ts(r("nex"), r("p0", 0, 128), 0.0, None, A.is_equal)
-        reduce_(col(9), r("p4", 0, 17), A.max)
-        scan(row("rowA"), row("RST"), r("p3", 0, 128, p=p1), A.mult, A.max)
-        mm("p3", 200, 201, row("rowA"), r("ONEF", 0, 1, p=p1))
         scan(rev("rowD", p1), row("RST"), r("p5", 0, 128, p=p1), A.mult, A.max)
         mm("p5", 200, 201, row("rowD"), r("ONEF", 0, 1, p=p1))
+        scan(r("rowA16", 0, 128, p=p1), row("RST"), r("p3", 0, 128, p=p1), A.mult, A.max)
+        mm("p3", 200, 201, r("rowA16", 0, 128, p=p1), one16)
+        reduce_(col(9), r("p4", 0, 17), A.max)
         tt(r("tC"), r("p1", 0, 128), r("tD"), A.mult)
-        ts(slot(0), r("PF"), r("p3", 200, 201), -6144.0, A.max, A.add)
         ts(r("NN"), r("NB"), r("p5", 200, 201), col(9), A.max, A.max)
+        ts(slot(0), r("PF", 0, 128), r("p3", 200, 201), -6144.0, A.max, A.add)
         tt(slot(2), r("p2", 0, 128), r("tC"), A.add)
         tt(slot(1), slot(0), r("NN"), A.subtract)
         tt(r("SP"), slot(0), r("NN"), A.add)
@@ -677,18 +711,24 @@ def rank_program(g, core, T, topo):
                 tc(r("SBX", 256, MW), r("p2", 0, EW))
                 send(t)
             ts(r("L16", m, 112, 8, tag="m%d" % m), r("p4", 16 * m, 16 * m + 14), -1.0, None, A.add)
-        for src, out in ((X, XN), ("ST", "SG_")):
-            gather("s", r(out, 16 * MAINV, CUT), src, 0, 3 * XW, "L16", MAINV, 112)
-            gather("v", r(out, 0, 16 * MAINV), src, 0, 3 * XW, "L16", 0, MAINV)
-            if t == 1 and src == X:
-                dma("y", ext(T.y[:, 0:CUT], "y", 0, CUT), r(XN, 0, CUT))
+        def stay(eng, src, out, a, b):
+            gather(eng, r(out, 16 * a, 16 * b), src, 0, 3 * XW, "L16", a, b)
         ends = [(r("KR", 0, 128, p=p1), r("ONEB", 0, EW, p=p1)), (r("ONEB", 0, 128, p=p1), r("KR", 128, 128 + EW, p=p1))] + \
-            sums("F1", lambda i: r("SG_", 128 * i, 128 * i + EW), range(14))
-        if t == 0:
+            sums("F1", lambda i: r("SG_", 128 * i, 128 * i + EW), (0, 1, 2, 7, 8, 9, 3, 4, 5, 6, 10, 11, 12, 13))
+        if t == 1:
+            for src, out in ((X, XN), ("ST", "SG_")):
+                stay("s", src, out, MAINV, 112)
+                stay("v", src, out, 0, MAINV)
+                if src == X:
+                    dma("y", ext(T.y[:, 0:CUT], "y", 0, CUT), r(XN, 0, CUT))
+        else:
+            for eng, a, b in (("v", 0, 32), ("s", 56, 88), ("v", 32, 56), ("s", 88, 112)):
+                stay(eng, "ST", "SG_", a, b)
             mms(r("p3", 0, EW), ends)
-            walkers_start(1)
+            stay("s", X, XN, STAYV, 112)
+            stay("v", X, XN, 0, STAYV)
             ts(r("E2", 0, EW), r("p3", 0, EW), float(CUT), None, A.min)
-            table_start("E2")
+            table_start("E2", walkers_start(1))
             second_kids(XN, 14)
         mms(r("p1", 0, EW), ends, True, False)
         arrive("ax%d" % t, 2 * NX, XN, CUT, CUT + MW)
@@ -716,11 +756,12 @@ def rank_program(g, core, T, topo):
 
     tc(r("E0", 0, 128), r("EI"))
     mm("p0", 0, 1, r("SHIFT"), r("E0", 0, 1))
-    walkers_start(0)
+    tc(r("UP"), r("MB", 0, 320))
     tc(r("E0", 128, 129), r("p0", 0, 1))
     for t in range(2):
-        table_start("E%d" % t)
+        table_start("E%d" % t, () if t else walkers_start(0))
         if t == 0:
+            mark_tables()
             second_kids("X0", 16)
             load_weapons(1)
             beside_first_walks()
@@ -730,8 +771,8 @@ def rank_program(g, core, T, topo):
         walks(t)
         marks(t)
         grow(t)
-    dma("y", ext(T.ye[:], "ye"), r("E2", 0, 128))
     dma("y", ext(T.y[:, CUT:P], "y", CUT, P), r("Y2", CUT, P))
+    dma("y", ext(T.ye[:], "ye"), r("E2", 0, 128))
     for sem, val in count.items():
         if known["g"].get(sem, 0) < val:
             g.wait_ge(T.sem[sem], val)

from concourse.bass import DstId, RemoteDMATransfer
from concourse.mybir import dt, AluOpType, AxisListType, ActivationFunctionType

A = AluOpType
AF = ActivationFunctionType
P = 2048
SC = 14
VC = 64 - SC
PIECES = ((0, 12), (12, 24), (24, VC))
LAST_PIECES = ((0, 4), (4, 8), (8, 16), (16, 20), (20, 24), (24, VC))
NS = 32
LAG = 1
PACE = 4
EARLY = (10, 2, 0, 4, 2, 2, 2)
OW = 96
XB = 2064
XW = 2192
EW = 136
MW = 256 + EW
CUT = 1792
SWA = 4096
SWW = SWA + 12288
MAINV = 56
STAYV = 24
TAIL = 1808

BLK = ["VF", "V1", "Q2", "V1h", "QNh", "ZERO", "nhE", "thr", "hv", "KXh", "KX", "VFh", "Fl",
       "NB", "NN", "SP", "nex", "tA", "tC", "tD", "qq", "SHIFT", "SHR", "SHL", "RST",
       "GRP", "D2", "D1", "H00", "H01", "H10", "H11", "ONEF", "rowD"]
SCRATCH = {"BK": ("sbuf", [128, 128 * len(BLK)], "float32")}
for n_ in ("E0", "E1", "E2"):
    SCRATCH[n_] = ("sbuf", [128, 136], "float32")
for n_ in ("VI", "EI"):
    SCRATCH[n_] = ("sbuf", [128, 128], "int32")
for n_ in ("B16", "EL16", "off16", "q16", "L16", "Z16"):
    SCRATCH[n_] = ("sbuf", [128, 128], "uint16")
for n_ in ("IDB", "NIDB", "N2ID", "IDP", "IDN", "SHB", "kb", "kl", "bb", "bl", "sb", "sl", "nb", "nl", "Hb", "INV", "HS", "ik",
           "cont", "ks", "ws", "TRI", "NSHR", "SELE", "SEL", "HP", "LO"):
    SCRATCH[n_] = ("sbuf", [128, 128], "bfloat16")
for n_ in ("F1", "FP", "FN", "FA", "FB", "FT0", "FT1", "ONEB", "hm"):
    SCRATCH[n_] = ("sbuf", [128, 144], "bfloat16")
for n_ in ("TI", "TV", "TS"):
    SCRATCH[n_] = ("sbuf", [128, 160], "bfloat16")
for n_ in ("XPHI", "GH", "GK", "W", "KT", "HMR", "VD", "R0", "R1", "ZT"):
    SCRATCH[n_] = ("sbuf", [128, 2048], "bfloat16")
for n_ in ("Bh", "PF", "mE", "RCH", "SHR16", "rowA16", "rowB16"):
    SCRATCH[n_] = ("sbuf", [128, 136], "float16")
SCRATCH.update({
    "X0": ("sbuf", [128, 3 * XW], "bfloat16"), "X1": ("sbuf", [128, 3 * XW], "bfloat16"), "ST": ("sbuf", [128, 3 * XW], "bfloat16"),
    "XBS": ("sbuf", [128, XB], "bfloat16"), "MB": ("sbuf", [128, XB], "bfloat16"), "KR": ("sbuf", [128, 128 + EW], "bfloat16"),
    "SW": ("sbuf", [128, SWW], "bfloat16"), "SG_": ("sbuf", [128, 2080], "bfloat16"),
    "GR": ("sbuf", [128, 8, 256], "bfloat16"), "OH": ("sbuf", [128, 128 * OW], "bfloat16"),
    "CC": ("sbuf", [128, 384], "float32"),
    "UP": ("sbuf", [128, 320], "float16"), "TB": ("sbuf", [128, 3072], "bfloat16"), "LT": ("sbuf", [128, 512], "bfloat16"),
    "OS": ("sbuf", [128, 6144], "bfloat16"),
    "ST0": ("sbuf", [128, 256], "int32"), "CB": ("sbuf", [128, 320], "bfloat16"), "CX": ("sbuf", [128, 256], "bfloat16"),
    "cols": ("sbuf", [128, 32], "float32"), "coli": ("sbuf", [128, 8], "int32"),
    "MSK": ("sbuf", [128, 16], "float32"), "YR": ("sbuf", [128, 32], "float32"),
    "SBX": ("sbuf", [128, MW], "bfloat16"), "RL0": ("sbuf", [128, MW // 2], "bfloat16"), "RL1": ("sbuf", [128, MW // 2], "bfloat16"),
    "Y2": ("sbuf", [128, XW], "bfloat16"),
})
for n_ in (0, 1):
    SCRATCH["MR%d" % n_] = ("sbuf", [128, 1024], "bfloat16")
    SCRATCH["GS%d" % n_] = ("sbuf", [128, 32 * SC], "bfloat16")
    SCRATCH["U%d" % n_] = ("sbuf", [128, 128], "float32")
for n_ in range(8):
    SCRATCH["p%d" % n_] = ("psum", [128, 512], "float32")
SEMAPHORES = ["q_v", "q_s", "q_t", "q_g"] + ["d%d" % k for k in range(70)] + \
    [a + b for a in ("rx", "lx", "ax") for b in "01"]
NX = 8


def pick(topo, src, dst, k, skip=0):
    return sum(1 << e for e in topo.engines(src, dst)[skip:skip + k])


def relays(topo, core, dst):
    return [c for c in topo.cores_of(core) if c != core and topo.die(c) == topo.die(core) and topo.may_write(c, dst)]


def relay_program(g, core, T, topo):
    for r, me in enumerate(T.cores):
        dst = T.cores[(r + 1) % len(T.cores)]
        rl = relays(topo, me, dst)
        if core not in rl[:2]:
            continue
        rid, pid = topo.addr(dst, core)
        lo = CUT + MW // 2 * rl.index(core)
        for t in range(2):
            g.wait_ge(T.sem["rx%d" % t], NX)
            out = (T.X1 if t == 0 else T.Y2)[:, lo:lo + MW // 2]
            g.remote_dma(out, T["RL%d" % t][:], T.sem["ax%d" % t], T.sem["lx%d" % t], pid, rid, pick(topo, core, dst, NX))
        for t in range(2):
            g.wait_ge(T.sem["lx%d" % t], NX)


def rank_program(g, core, T, topo):
    if T.rank_of(core) is None:
        return relay_program(g, core, T, topo)
    rank = T.rank_of(core)
    dst = T.cores[(rank + 1) % len(T.cores)]
    rl = relays(topo, core, dst)
    queues = {"v": g.vector, "s": g.scalar, "t": g.tensor, "g": g, "y": g.sync}
    count = {}
    known = {q: {} for q in queues}
    log = {}
    nd = [0]
    where = {n: 128 * k for k, n in enumerate(BLK)}

    def r(name, lo=0, hi=None, step=None, p=None, tag=None):
        if name in where:
            hi = 128 if hi is None else hi
            lo, hi, name = lo + where[name], hi + where[name], "BK"
        t = T[name]
        hi = t.shape[1] if hi is None else hi
        pp = slice(None) if p is None else p
        return (t[pp, lo:hi] if step is None else t[pp, lo:hi:step], name, lo, hi, tag)

    def r3(name, a, b, lo, hi):
        w = T[name].shape[2]
        return (T[name][:, a, lo:hi] if b == a + 1 else T[name][:, a:b, lo:hi], name, a * w, b * w, None)

    def rev(name, p=None):
        pp = slice(None) if p is None else p
        if name not in where:
            return (T[name][pp, 127::-1], name, 0, 128, None)
        o = where[name]
        return (T.BK[pp, o + 127:(o - 1 if o else None):-1], "BK", o, o + 128, None)

    def ind(name, lo, hi, lname, a, b):
        return (T[name][:, lo:hi].indirect(T[lname][:, a:b]), name, lo, hi, None, (None, lname, a, b, None))

    def need(q, reads, writes):
        want = {}
        for is_w, views in ((False, reads), (True, writes)):
            for v in views:
                bank = v[1][0] == "p" and v[1][1:].isdigit()
                for e in log.get(v[1], ()):
                    same = e[4] == q
                    if same and q == "t":
                        continue
                    if (same or not bank) and (e[0] >= v[3] or v[2] >= e[1] or (e[2] is not None and v[4] is not None and e[2] != v[4])):
                        continue
                    if not is_w and not e[3] and (same or not bank):
                        continue
                    old = want.get(e[5])
                    if old is None or old[0] < e[6]:
                        want[e[5]] = (e[6], e[7])
        kn = known[q]
        for sem in sorted(want, key=lambda k: -len(want[k][1])):
            val, clock = want[sem]
            if kn.get(sem, 0) >= val:
                continue
            queues[q].wait_ge(T.sem[sem], val)
            for k2, v2 in clock.items():
                if kn.get(k2, 0) < v2:
                    kn[k2] = v2
            kn[sem] = val

    def note(q, reads, writes, sem, val, clock):
        for is_w, views in ((False, reads), (True, writes)):
            for v in views:
                L = log.setdefault(v[1], [])
                if is_w:
                    L[:] = [e for e in L if not (v[2] <= e[0] and e[1] <= v[3] and (v[4] is None or v[4] == e[2]))]
                else:
                    L[:] = [e for e in L if not (not e[3] and e[4] == q and q != "dma" and e[0] >= v[2] and e[1] <= v[3])]
                L.append([v[2], v[3], v[4], is_w, q, sem, val, clock])

    def op(q, reads, writes, calls):
        reads = list(reads) + [v[5] for v in list(reads) + list(writes) if len(v) > 5]
        need(q, reads, writes)
        sem = "q_" + q
        for call in calls:
            call().then_inc(T.sem[sem], 1)
            count[sem] = count.get(sem, 0) + 1
        clock = dict(known[q])
        clock[sem] = count[sem]
        note(q, reads, writes, sem, count[sem], clock)

    def dma(q, out, in_, ext_in=False):
        sem = "d%d" % nd[0]
        nd[0] += 1
        reads, writes = ([] if ext_in else [in_]), ([out])
        need(q, reads, writes)
        queues[q].dma_start(out[0], in_[0]).then_inc(T.sem[sem], 16)
        count[sem] = 16
        clock = dict(known[q])
        clock[sem] = 16
        note("dma", reads, writes, sem, 16, clock)

    def ext(ap, name, lo=0, hi=2048):
        return (ap, "#" + name, lo, hi, None)

    def rows(name, k, lo, src):
        dma("y", (T[name][k:128:16, lo:lo + P], name, lo, lo + P, "row%d" % k), src)

    V, S, TE = g.vector, g.scalar, g.tensor

    def tt(out, a, b, o):
        op("v", [a, b], [out], [lambda: V.tensor_tensor(out[0], a[0], b[0], o)])

    def ts(out, a, s1, s2, o0, o1=None):
        rd = [a] + [s for s in (s1, s2) if isinstance(s, tuple)]
        x1 = s1[0] if isinstance(s1, tuple) else s1
        x2 = s2[0] if isinstance(s2, tuple) else s2
        if o1 is None:
            op("v", rd, [out], [lambda: V.tensor_scalar(out[0], a[0], x1, None, o0)])
        else:
            op("v", rd, [out], [lambda: V.tensor_scalar(out[0], a[0], x1, x2, o0, o1)])

    def tc(out, a):
        op("v", [a], [out], [lambda: V.tensor_copy(out[0], a[0])])

    def fill(out, val):
        op("v", [], [out], [lambda: V.memset(out[0], val)])

    def scan(out, d0, d1, o0, o1, first=0.0):
        op("v", [d0, d1], [out], [lambda: V.tensor_tensor_scan(out[0], d0[0], d1[0], first, o0, o1)])

    def reduce_(out, a, o):
        op("v", [a], [out], [lambda: V.tensor_reduce(out[0], a[0], AxisListType.X, o)])

    def act(out, a, f, bias=0.0, scale=1.0):
        rd = [a] + ([bias] if isinstance(bias, tuple) else [])
        bb = bias[0] if isinstance(bias, tuple) else bias
        op("s", rd, [out], [lambda: S.activation(out[0], a[0], f, bias=bb, scale=scale)])

    def mms(out, pairs, first=True, last=True):
        n = len(pairs)
        for k, (lhs, rhs) in enumerate(pairs):
            op("t", [lhs, rhs], [out], [lambda: TE.matmul(out[0], lhs[0], rhs[0], first and k == 0, last and k == n - 1)])

    def mm(bank, c0, c1, lhs, rhs, p=None):
        mms(r(bank, c0, c1, p=p), [(lhs, rhs)])

    def sums(F, pick_, targets=range(16)):
        return [(r(F, 15 - i, 143 - i), pick_(i)) for i in targets]

    def walkers(name, base, n):
        return lambda i: r(name, base + i, base + 16 * n, 16)

    def col(k):
        return r("cols", k, k + 1)

    def slot(k, n=128):
        return r("p7", 128 * k, 128 * k + n)

    pVF, pV1, pVB = [r("p6", 128 * k, 128 * k + 128) for k in range(3)]
    halves = (slice(0, 64), slice(64, 128))
    p1, p32, p33, row32 = slice(0, 1), slice(0, 32), slice(0, 33), slice(32, 33)

    dma("y", r("EI"), ext(T.ends[:], "ends"), True)
    dma("y", r("X0", 0, P), ext(T.x[:], "x"), True)
    dma("y", r("ST0"), ext(T.start[:], "start"), True)

    def load_weapons(h):
        dma("y", r("W", 1024 * h, 1024 * h + 1024), ext(T.w[:, 1024 * h:1024 * h + 1024], "w"), True)

    load_weapons(0)

    def iota(out, pat, base, cm, small=True):
        op("g", [], [out], [lambda: g.iota(out[0], pat, base, cm, allow_small_or_imprecise_dtypes=True) if small else g.iota(out[0], pat, base, cm)])

    def asel(out, in_, pat, cmp, fl, base, cm):
        op("g", [in_], [out], [lambda: g.affine_select(out[0], in_[0], pat, cmp, fl, base, cm)])

    def band(name, entries, lo=0, hi=128, p=None):
        src = r("ZERO", lo, hi, p=p)
        for a, b, val in entries:
            asel(r(name, lo, hi, p=p), src, [[a, hi - lo]], A.not_equal, val, b, 1)
            src = r(name, lo, hi, p=p)

    fill(r("ONEF"), 1.0)
    fill(r("ONEB"), 1.0)
    fill(r("ZERO"), 0.0)
    iota(r("VI"), [[1, 128]], 0, 128, False)
    asel(r("SHIFT"), r("ONEF"), [[-1, 128]], A.is_equal, 0.0, -1, 1)
    asel(r("SHIFT"), r("SHIFT"), [[0, 8], [1, 16]], A.not_equal, 0.0, -15, 0)
    iota(r("TI", 0, 112), [[1, 112]], -64, 0)
    asel(r("IDB"), r("ONEB", 0, 128), [[-1, 128]], A.is_equal, 0.0, 0, 1)
    asel(r("F1"), r("ONEB"), [[-16, 9], [0, 16]], A.is_ge, 0.0, 0, 1)
    asel(r("F1"), r("F1"), [[16, 9], [0, 16]], A.is_ge, 0.0, 15, -1)
    asel(r("F1"), r("F1"), [[0, 9], [1, 16]], A.is_equal, 0.0, -15, 0)
    iota(r("CB"), [[-1, 5], [0, 64]], 5, 0)
    fill(r("XBS", 0, 16), 0.0)
    ts(r("VI"), r("VI"), 2047, None, A.bitwise_and)
    fill(r("XBS", P, XB), 0.0)
    tc(r("VF"), r("VI"))
    ts(pV1, r("VI"), 1.0, None, A.add)
    fill(r("MB"), 0.0)
    act(r("NIDB"), r("IDB"), AF.Copy, scale=-1.0)
    act(r("FP"), r("F1"), AF.Copy, scale=4096.0)
    act(r("FN"), r("F1"), AF.Copy, scale=-4096.0)
    act(r("IDN"), r("IDB"), AF.Copy, scale=-4096.0)
    fill(r("X0", P, XB), 0.0)

    def beside_first_walks():
        iota(r("ZT"), [[0, 2048]], 0, 0)
        for n in ("HMR", "KT", "VD"):
            dma("y", r(n), r("ZT"))
        for c in range(3):
            dma("y", r("ST", XW * c, XW * c + P), r("ZT"))
            dma("y", r("SW", P * c, P * c + P), r("ZT"))
        asel(r("SEL"), r("ZT", 0, 128), [[-8, 2], [-16, 8], [-1, 8]], A.not_equal, 1.0 / 64, 0, 1)
        asel(r("TB", 0, 2048, p=p32), r("ZT", p=p32), [[-1, 32], [0, 64]], A.not_equal, 128.0, 0, 1)
        asel(r("TB", 2048, 3072, p=p32), r("ZT", 0, 1024, p=p32), [[-1, 32], [0, 32]], A.not_equal, 1.0, 0, 1)
        iota(r("TS", 0, 64, p=p32), [[-2, 64]], 127, 0)
        iota(r("TS", 64, 96, p=p32), [[-1, 32]], 0, 0)
        dma("y", r("TB", 0, 2048, p=row32, tag="r32"), r("TS", 0, 64, p=p32))
        dma("y", r("TB", 2048, 3072, p=row32, tag="r32"), r("TS", 64, 96, p=p32))
        iota(r("LT"), [[0, 512]], 1, 0)
        iota(r("OH", 0, 2048), [[1, 128], [0, 16]], 1, 0)
        dma("y", (T.VD[8:128:16, :], "VD", 0, 2048, "row8"), r("OH", 0, 2048, p=slice(0, 128, 16)))
        iota(r("KR", 0, 128), [[0, 8], [128, 16]], 0, 0)
        rows("VD", 0, 0, r("KR", 0, 128))
        iota(r("CX"), [[XW, 2], [0, 128]], XW, 0)
        for c in (1, 2):
            rows("SW", 4, SWA - P * c, r("CX", 128 * c - 128, 128 * c))
        band("D2", [(-1, 1, -1.0), (-1, 0, 2.0), (-1, -1, -1.0), (1, 0, 1.0)], 0, 64)
        band("D1", [(-1, 1, 1.0), (-1, 0, -1.0), (64, -63, -1.0)], 0, 64)
        for n in ("D2", "D1"):
            dma("y", r(n, 0, 64, p=halves[1]), r(n, 0, 64, p=halves[0]))
        iota(r("CC", 128, 256), [[0, 128]], 0, 0)
        asel(r("RST"), r("ONEF"), [[0, 8], [1, 16]], A.not_equal, 0.0, 0, 0)
        asel(r("SHR"), r("RST"), [[-1, 128]], A.is_equal, 0.0, 1, 1)
        for n, lo, src, val in (("H00", 0, "SHIFT", 1.0), ("H00", 64, "ZERO", -2.0), ("H10", 0, "ZERO", -2.0), ("H10", 64, "SHR", 1.0),
                                ("H01", 64, "SHIFT", 1.0), ("H11", 0, "SHIFT", 1.0), ("H11", 64, "ZERO", -2.0)):
            asel(r(n, lo, lo + 64), r(src, lo, lo + 64), [[-1, 64]], A.not_equal, val, -lo, 1)
        asel(r("H11", 79, 128, 16), r("H11", 79, 128, 16), [[-16, 4]], A.not_equal, -1.0, -79, 1)
        band("H01", [(-1, -1, -2.0)], 0, 64)
        asel(r("H01", 0, 64), r("H01", 0, 64), [[0, 4], [1, 16]], A.not_equal, 0.0, -15, 0)
        iota(r("SG_", CUT, TAIL), [[0, 16]], 0, 0)
        iota(r("SG_", TAIL + 256, 2080), [[0, 16]], 0, 0)
        asel(r("GRP"), r("ONEF"), [[-16, 8], [0, 16]], A.is_ge, 0.0, 0, 1)
        asel(r("GRP"), r("GRP"), [[16, 8], [0, 16]], A.is_ge, 0.0, 15, -1)
        asel(r("TRI"), r("GRP"), [[1, 128]], A.is_ge, 0.0, -1, -1)
        asel(r("SHL"), r("RST"), [[1, 128]], A.is_equal, 0.0, -128, 1)
        asel(r("FA"), r("F1"), [[16, 9], [0, 16]], A.is_ge, 0.0, 1, -1)
        asel(r("FB"), r("F1"), [[-16, 9], [0, 16]], A.is_ge, 0.0, -2, 1)
        for b in range(2):
            asel(r("FT%d" % b), r("F1"), [[-16, 9], [0, 16]], A.is_equal, 0.0, -14 - b, 1)
        for gr in range(8):
            asel(r("MSK"), r("MSK") if gr else r("ZERO", 0, 16), [[-1, 16]], A.not_equal, 1.0, -16 * gr, 1)
        iota(r("KR", 128, 128 + EW), [[1, EW]], 1, 0)
        iota(r("SELE"), [[0, 128]], 0, 0)
        for i in (14, 15):
            for d, val in ((0, 1.0), (2, 0.5)):
                asel(r("SELE", i, 128, 16), r("SELE", i, 128, 16), [[-16, 8]], A.not_equal, val, d - i, 1)

    def mark_tables():
        act(r("TV", 0, 64), r("TI", 0, 64), AF.Copy, scale=1.0 / 64)
        act(r("TV", 64, OW), r("TI", 65, OW + 1), AF.Copy)

    def growth_constants(part):
        if part:
            tc(r("SHB"), r("SHIFT"))
            tc(r("RCH", 0, 1), r("ZERO", 0, 1))
            ts(pVB, r("VF"), 6145.0, None, A.add)
            return
        act(r("IDP"), r("IDB"), AF.Copy, scale=4096.0)
        act(r("N2ID"), r("IDB"), AF.Copy, scale=-2.0)
        act(r("NSHR"), r("SHR"), AF.Copy, scale=-1.0)
        act(r("GRP"), r("GRP"), AF.Copy, scale=-1.0)
        act(r("V1"), r("VF"), AF.Identity, 1.0)
        act(r("Q2"), r("VF"), AF.Identity, -10239.5)
        act(r("V1h"), r("VF"), AF.Identity, 0.5, 0.5)
        act(r("QNh"), r("VF"), AF.Identity, 4096.0, -0.5)
        act(r("FB"), r("FB"), AF.Copy, scale=2.0)
        act(col(3), r("VF", 0, 1), AF.Sign, -(CUT - 64.0))
        act(col(4), col(3), AF.Identity, (CUT + P) / 2, (P - CUT) / 2)
        tc(pVF, r("VF"))
        tc(r("SHR16", 0, 128), r("SHR"))

    def table_start(E, between=()):
        other = list(between) + [lambda: None] * 3
        other[0]()
        tt(slot(2), r(E, 1, 129), r(E, 0, 128), A.is_lt)
        tt(slot(0), r(E, 0, 128), pV1, A.is_gt)
        tt(r("tC"), slot(2), r(E, 1, 129), A.mult)
        tt(slot(1), r("VF"), slot(0), A.add)
        other[1]()
        tt(r("Bh", 0, 128), slot(1), r("tC"), A.max)
        other[2]()

    def second_kids(X, n):
        ts(r("B16"), r("Bh", 0, 128), 128.0 * n - 1, None, A.min)
        if n == 16:
            kid_rows()
        g2(X, 128 * n, "B16", "XPHI")
        permute("s", "XBS", 1, "XPHI", range(6))
        permute("v", "XBS", 1, "XPHI", range(6, n))

    def kid_rows():
        tc(r("bb"), r("Bh", 0, 128))
        rows("MB", 0, 1, r("bb"))
        tt(r("bl"), r("Bh", 0, 128), r("bb"), A.subtract)
        rows("MB", 1, 1, r("bl"))

    def second_kids_arrived(X):
        for b in range(2):
            mms(r("p2", 8 * b, 8 * b + 8), sums("FT%d" % b, lambda i: r("Bh", i, 128, 16)))
        kid_rows()
        j_gather(0, 0, 1, 0, 32)
        tc(r("L16", 112, 128), r("p2", 0, 16))
        j_gather(0, 0, 1, 32, 64)
        gather("v", r("XBS", CUT + 1, P + 1), X, 0, P, "L16", 112, 128)
        tc(r("B16"), r("Bh", 0, 128))

    def place_tables(t):
        E = "E%d" % t
        return [lambda: tt(r("nhE"), slot(0), r(E, 0, 128), A.mult),
                lambda: ts(r("thr"), slot(0), 1.0e6, None, A.mult),
                lambda: ts(r("EL16"), r(E, 0, 128), -1.0, None, A.add)]

    def walkers_start(t):
        return [lambda: ts(r("Z16"), r("ST0", 128 * t, 128 * t + 128), 1.0, None, A.add)] + \
            [lambda h=h: ts(r("U%d" % h, 0, 64), r("ST0", 128 * t + 64 * h, 128 * t + 64 * h + 64), 6.0, None, A.add) for h in range(2)]

    def permute(eng, dst_, off, src, blocks):
        for i in blocks:
            o = r(dst_, off + 128 * i, off + 128 * i + 128)
            a = r(src, i, 2048, 16)
            if eng == "v":
                tc(o, a)
            else:
                act(o, a, AF.Copy)

    def gather(eng, out, src, lo, hi, lname, a, b):
        i = ind(src, lo, hi, lname, a, b)
        if eng == "v":
            tc(out, i)
        else:
            act(out, i, AF.Copy)

    def g2(src, W, lname, out):
        gather("v", r(out, 0, 1024), src, 0, W, lname, 0, 64)
        gather("s", r(out, 1024, 2048), src, 0, W, lname, 64, 128)

    def j_gather(h, which, t, a=0, b=VC):
        win, base = ("X%d" % t, 0) if which == 0 else ("XBS", 1024)
        tt(r("R%d" % h, base + 16 * a, base + 16 * b), ind(win, 0, XB, "Z16", 64 * h + a, 64 * h + b),
           r("W", 1024 * h + 16 * a, 1024 * h + 16 * b), A.min)

    def s_gather(h, t):
        n = 16 * SC
        for k, win in ((1, "X%d" % t), (0, "XBS")):
            gs = r("GS%d" % h, n * k, n * k + n)
            gather("s", gs, win, 0, XB, "Z16", 64 * h + VC, 64 * h + 64)
            mms(r("p%d" % (4 + h), n * k, n * k + n), [(r("IDB"), r("W", 1024 * h + 16 * VC, 1024 * h + 1024)), (r("NIDB"), gs)])

    def s_meta(h, step):
        gather("s", r("MR%d" % h), "MB", 0, XB, "Z16", 64 * h, 64 * h + 64)
        shift = (r("IDB"), r("CB", 64 * step, 64 * step + 64)) if step < 5 else (r("IDN"), r("INV", 64 * h, 64 * h + 64))
        return lambda: mms(r("p%d" % (2 + h), 0, 64), [shift] + sums("F1", walkers("MR%d" % h, 0, 64)))

    def s_relu(h, alone):
        n = 16 * SC
        for k in range(0 if alone else 2):
            act(r("R%d" % h, 1024 * k + 16 * VC, 1024 * k + 1024), r("p%d" % (4 + h), n * k, n * k + n), AF.Relu)
        return [lambda: mms(r("p%d" % h, 0, 64), sums("FP", walkers("R%d" % h, 0, 64)), True, False),
                lambda: mms(r("p%d" % h, 0, 64), sums("FN", walkers("R%d" % h, 1024, 64)), False, True)]

    def decide(h, step):
        z0 = 64 * (step % 2)
        u = "U%d" % h
        a, b = 64 * h, 64 * h + 64
        old, new = r(u, z0, z0 + 64), (r(u, 64 - z0, 128 - z0) if step < 5 else r("UP", 128 * h + 64, 128 * h + 128))

        def last():
            if step < 5:
                ts(r("Z16", a, b), new, step - 4.0, None, A.add)
            else:
                turn(h)
            if step == 1:
                tt(r("INV", a, b), new, old, A.is_lt)
        return [lambda: tt(r("tA", a, b), r("p%d" % h, 0, 64), old, A.max),
                lambda: tt(new, r("p%d" % (2 + h), 0, 64), r("tA", a, b), A.min), last]

    def turn(h):
        a, b = 64 * h, 64 * h + 64
        pp = r("p%d" % h, 0, 64)
        tc_ = 128 * h + 64
        mms(pp, [(r("UP", tc_, tc_ + 128), r("SEL", 0, 64)), (r("UP", tc_ - 64, tc_ + 64), r("SEL", 64, 128))])

    def split(h):
        a, b = 64 * h, 64 * h + 64
        pp = r("p%d" % h, 0, 64)
        return [lambda: ts(r("Hb", a, b), pp, 129.0 - 31.5 / 64, 128.0, A.add, A.max),
                lambda: ts(r("HP", a, b), r("Hb", a, b), -128.0, None, A.add),
                lambda: tt(r("LO", a, b), pp, r("HP", a, b), A.subtract)]

    def spell(gr, h, i):
        j, c = 16 * gr + 8 * h + i, 64 * h + 8 * gr + i
        o = OW * j
        ts(r("OH", o, o + OW), r("TV", 0, OW), r("LO", c, c + 1), r("HP", c, c + 1), A.max, A.min)

    def tally(c):
        own = [d for d in (mine if c in mine else theirs) if d[:2] == c[:2]]
        if c in mine:
            o = OW * (16 * c[0] + 8 * c[1] + c[2])
            pair, bank, to = (r("OH", o, o + 64), r("OH", o + 64, o + OW)), "p2", 32 * (c[0] - 4)
        else:
            k, o = 8 * c[0] + c[2], 3072 * c[1]
            pair = (r("OS", o + 64 * k, o + 64 * k + 64), r("OS", o + 2048 + 32 * k, o + 2048 + 32 * k + 32))
            bank, to = "p4", 32 * c[0]
        mms(r(bank, to, to + 32, p=halves[c[1]]), [pair], c == own[0], c == own[-1])

    tiles = [(gr, h, i) for gr in range(8) for h in range(2) for i in range(8)]
    theirs = [c for c in tiles if 8 * c[0] + c[2] < NS]
    mine = [c for c in tiles if c not in theirs]

    def turn_back(h):
        for k, n in enumerate(("LO", "HP")):
            mm("p%d" % h, 64 + 128 * k, 192 + 128 * k, r(n, 64 * h, 64 * h + 32), r("IDB"), p=p32)
        act(r("LT", 256 * h, 256 * h + 256, p=p32), r("p%d" % h, 64, 320, p=p32), AF.Copy)

    blocks = [(0, a, min(a + 8, NS)) for a in range(0, NS, 8)]
    for a in range(0, NS, 16):
        blocks.insert(blocks.index((0, a, min(a + 8, NS))), (1, a, min(a + 16, NS)))
    nblock = [0]

    def block(h, kind, a, b):
        w, o = (64, 0) if kind == 0 else (32, 2048)
        bank = r(("p5", "p0", "p3")[nblock[0] % 3], 0, w * (b - a))
        nblock[0] += 1
        mms(bank, [(r("LT", 256 * h + 128 * kind, 256 * h + 128 * kind + 128, p=p33), r("TB", o + w * a, o + w * b, p=p33))])
        act(r("OS", 3072 * h + o + w * a, 3072 * h + o + w * b), bank, AF.Relu if kind else AF.Sign)

    def walks(t):
        for s in range(12):
            h = s % 2
            alone = t and not s
            if not alone:
                s_gather(h, t)
            sum_meta = s_meta(h, s // 2)
            if s < 11:
                sum_meta()
            if s or not t:
                j_gather(h, 0, t)
            if s:
                calls = decide(1 - h, (s - 1) // 2) + (split(0) if s == 11 else [])
                for call, (a, b) in zip(calls, PIECES if s < 11 else LAST_PIECES):
                    call()
                    j_gather(h, 1, t, a, b)
            else:
                j_gather(h, 1, t, 0, 64 if alone else VC)
            if s == 11:
                sum_meta()
            sum_first, sum_second = s_relu(h, alone)
            if s == 11:
                turn_back(0)
            sum_first()
            if s == 11:
                nblock[0] = 0
                block(0, *blocks[0])
                block(0, *blocks[1])
            sum_second()

    def marks(t):
        steps, due = [], [[], []]
        for h in range(2):
            for b in blocks:
                steps.append(lambda h=h, b=b, now=due.pop(0): [block(h, *b)] + [tally(c) for c in now])
                due.append([c for c in theirs if c[1] == h and b[1] <= 8 * c[0] < b[2]] if b[0] == 0 else [])
        steps = steps[2:]
        steps.insert(3, lambda: turn_back(1))
        steps.append(lambda: [tally(c) for c in due[0]])
        steps.append(lambda: [tally(c) for c in due[1]] + [act(r("CC", 0, 128), r("p4", 0, 128), AF.Copy)])
        order = sorted(mine, key=lambda c: c[1])
        done = 0
        for k, (n, call) in enumerate(zip(EARLY, decide(1, 5) + split(1) + [None])):
            for c in order[done:done + n]:
                spell(*c)
            if call:
                call()
            for c in order[done:done + n]:
                tally(c)
            done += n
            if k in (2, 3, 4, 5):
                steps.pop(0)()
        for n, c in enumerate(order[done:]):
            spell(*c)
            if n % PACE == 0 and len(steps) > LAG:
                steps.pop(0)()
            tally(c)
        for call in place_tables(t):
            call()
        tc(r("CC", 256, 384), r("p2", 0, 128))
        while steps:
            steps.pop(0)()
        for b in range(2):
            mms(r("p3", 64 * b, 64 * b + 64), [(r("CC", 128 + b, 384, 2), r("D2", 0, 64)), (r("CC", b, 256, 2), r("D1", 0, 64))])
        if t == 0:
            growth_constants(0)
        tc(r("tA"), r("p3", 0, 128))
        for b in range(2):
            mms(r("p%d" % b, 0, 64), [(r("H%d%d" % (k, b)), r("tA", 64 * k, 64 * k + 64)) for k in range(2)])
        if t == 0:
            growth_constants(1)

    def row(name):
        return r(name, p=p1)

    def grow(t):
        X = "X%d" % t
        XN, EX = ("X1" if t == 0 else "Y2"), "E%d" % (t + 1)
        HM = r("hm", 0, 128)
        for b in range(2):
            tt(r("hm", 64 * b, 64 * b + 64), r("p%d" % b, 0, 64), r("thr", 64 * b, 64 * b + 64), A.is_gt)
        rows("HMR", 0, 0, HM)
        mm("p5", 0, 1, r("SHB"), r("hm", 0, 1))
        scan(r("HS"), HM, r("ZT", 0, 128), A.add, A.add)
        mm("p4", 0, 1, r("TRI"), r("HS", 127, 128))
        tt(r("hv"), HM, pVB, A.mult)
        tc(r("hm", 128, 129), r("p5", 0, 1))
        ts(slot(1), r("HS"), r("p4", 0, 1), None, A.add)
        tt(r("VFh"), r("hv"), pVF, A.max)
        tt(slot(0), r("V1"), slot(1), A.subtract)
        tc(r("kb"), slot(0))
        rows("KT", 0, 0, r("kb"))
        for k in range(2):
            for eng, a in (("v", 64 * k), ("s", 64 * k + 32)):
                gather(eng, r("GH", 16 * a, 16 * a + 512), "HMR", 0, P, "B16", a, a + 32)
            mms(r("p2", 64 * k, 64 * k + 64), [(r("IDP"), r("hm", 64 * k + 1, 64 * k + 65))] + sums("FP", walkers("GH", 1024 * k, 64)))
        act(r(X, XW, XW + P), r(X, 0, P), AF.Relu, -1.0)
        tt(r("KX"), slot(0), r("hv"), A.max)
        tt(r("kl"), slot(0), r("kb"), A.subtract)
        rows("KT", 1, 0, r("kl"))
        ts(r("KXh"), r("KX"), 0.5, None, A.mult)
        one16 = r("SHR16", 1, 2, p=p1)
        tt(r("mE", 0, 128), r("p2", 0, 128), r("nhE"), A.min)
        scan(r("RCH", 1, 129), r("mE", 0, 128), r("ZT", 0, 128), A.max, A.add)
        mm("p1", 0, 128, r("RCH", 128, 129), r("SHR16", 0, 128), p=p1)
        scan(r("rowA16", 0, 128, p=p1), row("RST"), r("p1", 0, 128, p=p1), A.mult, A.max)
        mm("p1", 200, 201, r("rowA16", 0, 128, p=p1), one16)
        ts(slot(0, 129), r("RCH", 0, 129), r("p1", 200, 201), None, A.max)
        tt(r("ik"), r("p7", 1, 129), r("VFh"), A.is_gt)
        tt(r("cont"), slot(0), r("VF"), A.is_gt)
        scan(r("ks"), r("ik"), r("ZT", 0, 128), A.add, A.add)
        scan(r("ws"), r("cont"), r("ik"), A.mult, A.add, 8192.0)
        mm("p4", 0, 1, r("TRI"), r("ks", 127, 128))
        mms(r("p5", 0, 128, p=p1), [(r("ks", 127, 128), r("TRI")), (r("ws", 127, 128), r("NSHR"))])
        tt(r("Fl"), r("ks"), r("ws"), A.subtract)
        ts(slot(0), r("ks"), r("p4", 0, 1), None, A.add)
        scan(r("rowB16", 0, 128, p=p1), row("RST"), r("p5", 0, 128, p=p1), A.mult, A.max)
        mm("p5", 200, 201, r("rowB16", 0, 128, p=p1), one16)
        tc(r("nb"), slot(0))
        tt(r("nl"), slot(0), r("nb"), A.subtract)
        rows("KT", 2, 0, r("nb"))
        rows("KT", 3, 0, r("nl"))
        ts(slot(2), r("Fl"), r("p4", 0, 1), r("p5", 200, 201), A.add, A.max)
        ts(r("tD"), r("ik"), -1.0, 1.0, A.mult, A.add)
        tt(slot(3), slot(2), r("KXh"), A.add)
        ts(r("YR", 17, 18), r("HS", 127, 128), -0.5, None, A.mult)
        ts(r("off16"), slot(3), 2.0, -1.0, A.mult, A.add)
        ts(r("YR", 16, 17), r("YR", 17, 18), r("ks", 127, 128), 64.0 - 256.0, A.add, A.add)
        o = ind("SW", SWA, SWW, "off16", 0, 128)
        op("v", [r("VD")], [o], [lambda: V.tensor_copy(o[0], T.VD[:])])
        act(r(X, 2 * XW, 2 * XW + P), r(X, XW, XW + P), AF.Relu, -1.0)
        gather("s", r("GK"), "KT", 0, P, "EL16", 0, 128)
        mms(r("p2", 0, 128), [(r("NIDB"), r("kb")), (r("NIDB"), r("kl"))] + sums("FA", walkers("GK", 0, 128)))
        mms(r("p1", 0, 128), [(r("N2ID"), r("nb")), (r("N2ID"), r("nl"))] + sums("FB", walkers("GK", 0, 128)))
        mms(r("p0", 0, 128), sums("FP", lambda i: r("SW", SWA + 128 * i, SWA + 128 * i + 128)))
        for c in (1, 2):
            dma("y", (T.SW[0:128:8, SWA - P * c:SWA - P * c + P], "SW", SWA - P * c, SWA - P * c + P, "row08"),
                r("SW", SWA, SWA + P, p=slice(0, 128, 8)))
        ts(r("tA"), slot(3), 1024.25, 8192.0, A.is_lt, A.mult)
        tt(r("tA"), slot(3), r("tA"), A.max)
        reduce_(col(8), r("tA"), A.min)
        ts(r("YR", 0, 16), r("MSK"), col(8), -(4096.5 / 16), A.mult, A.add)
        mm("p4", 0, 17, r("GRP"), r("YR", 0, 17))
        scan(rev("NB"), rev("p0"), rev("QNh"), A.max, A.min)
        mm("p5", 0, 128, r("NB", 0, 1), r("SHL"), p=p1)
        scan(r("PF", 0, 128), r("p0", 0, 128), r("V1h"), A.max, A.min)
        mm("p3", 0, 128, r("PF", 127, 128), r("SHR16", 0, 128), p=p1)
        ts(r("nex"), r("p0", 0, 128), 0.0, None, A.is_equal)
        scan(rev("rowD", p1), row("RST"), r("p5", 0, 128, p=p1), A.mult, A.max)
        mm("p5", 200, 201, row("rowD"), r("ONEF", 0, 1, p=p1))
        scan(r("rowA16", 0, 128, p=p1), row("RST"), r("p3", 0, 128, p=p1), A.mult, A.max)
        mm("p3", 200, 201, r("rowA16", 0, 128, p=p1), one16)
        reduce_(col(9), r("p4", 0, 17), A.max)
        tt(r("tC"), r("p1", 0, 128), r("tD"), A.mult)
        ts(r("NN"), r("NB"), r("p5", 200, 201), col(9), A.max, A.max)
        ts(slot(0), r("PF", 0, 128), r("p3", 200, 201), -6144.0, A.max, A.add)
        tt(slot(2), r("p2", 0, 128), r("tC"), A.add)
        tt(slot(1), slot(0), r("NN"), A.subtract)
        tt(r("SP"), slot(0), r("NN"), A.add)
        tt(slot(1), slot(1), r("Q2"), A.is_lt)
        tc(r("sb"), slot(2))
        tt(slot(1), slot(1), r("nex"), A.add)
        tt(r("sl"), slot(2), r("sb"), A.subtract)
        for c in range(3):
            rows("ST", 0, XW * c, r("sb"))
            rows("ST", 2, XW * c, r("sl"))
        tt(r("tA"), slot(1), r("SP"), A.mult)
        tt(r("qq"), r("tA"), pVF, A.add)
        ts(r("q16"), r("qq"), float(SWA), None, A.add)
        for k in range(2):
            for m in range(4 * k, 4 * k + 4):
                gather("vs"[m // 2 % 2], r3("GR", m, m + 1, 0, 256), "SW", 0, SWA + P, "q16", 16 * m, 16 * m + 16)
            mms(r("p4", 64 * k, 64 * k + 64), sums("F1", lambda i: r3("GR", 4 * k, 4 * k + 4, 16 * i, 16 * i + 16)))
        for i in (14, 15):
            ts(r("L16", 8 * i, 8 * i + 8), r("p4", i, 128, 16), -1.0, None, A.add)
        gather("s", r("SG_", TAIL, TAIL + 256), "ST", 0, 3 * XW, "L16", 112, 128)
        gather("v", r("SBX", 0, 256), X, 0, 3 * XW, "L16", 112, 128)
        mms(r("p2", 0, EW), sums("FA", lambda i: r("SG_", TAIL + 128 * (i - 14), TAIL + 128 * (i - 14) + EW), (14, 15)) +
            sums("FB", lambda i: r("SG_", TAIL + 128 * (i - 12), TAIL + 128 * (i - 12) + EW), (12, 13)))
        for m in range(8):
            if m == 3:
                tc(r("SBX", 256, MW), r("p2", 0, EW))
                send(t)
            ts(r("L16", m, 112, 8, tag="m%d" % m), r("p4", 16 * m, 16 * m + 14), -1.0, None, A.add)
        def stay(eng, src, out, a, b):
            gather(eng, r(out, 16 * a, 16 * b), src, 0, 3 * XW, "L16", a, b)
        ends = [(r("KR", 0, 128, p=p1), r("ONEB", 0, EW, p=p1)), (r("ONEB", 0, 128, p=p1), r("KR", 128, 128 + EW, p=p1))] + \
            sums("F1", lambda i: r("SG_", 128 * i, 128 * i + EW), (0, 1, 2, 7, 8, 9, 3, 4, 5, 6, 10, 11, 12, 13))
        if t == 1:
            for src, out in ((X, XN), ("ST", "SG_")):
                stay("s", src, out, MAINV, 112)
                stay("v", src, out, 0, MAINV)
                if src == X:
                    dma("y", ext(T.y[:, 0:CUT], "y", 0, CUT), r(XN, 0, CUT))
        else:
            for eng, a, b in (("v", 0, 32), ("s", 56, 88), ("v", 32, 56), ("s", 88, 112)):
                stay(eng, "ST", "SG_", a, b)
            mms(r("p3", 0, EW), ends)
            stay("s", X, XN, STAYV, 112)
            stay("v", X, XN, 0, STAYV)
            ts(r("E2", 0, EW), r("p3", 0, EW), float(CUT), None, A.min)
            table_start("E2", walkers_start(1))
            second_kids(XN, 14)
        mms(r("p1", 0, EW), ends, True, False)
        arrive("ax%d" % t, 2 * NX, XN, CUT, CUT + MW)
        mms(r("p1", 0, EW), [(r("SELE"), r(XN, P, P + EW))], False, True)
        ts(r(EX, 0, EW), r("p1", 0, EW), col(4), None, A.min)

    def send(t):
        parts = [(rl[k], T.SBX[:, MW // 2 * k:MW // 2 * (k + 1)], T["RL%d" % t][:], "rx%d" % t) for k in range(2)]
        srcs, ls = [r("SBX")], "lx%d" % t
        need("g", srcs, [])
        transfers = []
        for k, (to, src, out, rs) in enumerate(parts):
            rid, pid = topo.addr(to, core)
            transfers.append(RemoteDMATransfer(dst_ids=[DstId(rid=rid, pnc=pid)], dma_engine_mask=pick(topo, core, to, NX, NX * k),
                                               remote_sem=T.sem[rs], src=src, dst=out))
        g.remote_dma_fused(transfers, local_sem=T.sem[ls])
        count[ls] = 2 * NX
        clock = dict(known["g"])
        clock[ls] = 2 * NX
        note("dma", srcs, [], ls, 2 * NX, clock)

    def arrive(sem, k, name, lo, hi):
        count[sem] = k
        note("dma", [], [r(name, lo, hi)], sem, k, {sem: k})

    tc(r("E0", 0, 128), r("EI"))
    mm("p0", 0, 1, r("SHIFT"), r("E0", 0, 1))
    tc(r("UP"), r("MB", 0, 320))
    tc(r("E0", 128, 129), r("p0", 0, 1))
    for t in range(2):
        table_start("E%d" % t, () if t else walkers_start(0))
        if t == 0:
            mark_tables()
            second_kids("X0", 16)
            load_weapons(1)
            beside_first_walks()
        else:
            second_kids_arrived("X1")
            dma("y", r("SW", SWA, SWA + P, p=slice(0, 128, 8)), r("ZT", p=slice(0, 128, 8)))
        walks(t)
        marks(t)
        grow(t)
    dma("y", ext(T.y[:, CUT:P], "y", CUT, P), r("Y2", CUT, P))
    dma("y", ext(T.ye[:], "ye"), r("E2", 0, 128))
    for sem, val in count.items():
        if known["g"].get(sem, 0) < val:
            g.wait_ge(T.sem[sem], val)
